import numpy as np, ml_dtypes
CORES = [23,119,17,113]
N = 4
BF = ml_dtypes.bfloat16
P, TW, M, RO = 4096, 4096, 3, 4
def parts(rng):
    v = rng.integers(0, 128, (N, 8, 16, P)); v[:, :, 15] = rng.integers(0, 2, (N, 8, P))
    t = rng.integers(0, 128, (N, 8, 16, TW)); t[:, :, 15] = rng.integers(0, 2, (N, 8, TW))
    return v, t, rng.integers(1, 256, (N, 8, 16)), rng.integers(0, 2048, (N, 8, RO, M))
def pack(v, t, w, k):
    return {"x": v.reshape(N, 128, P).astype(np.float32).astype(BF), "tm": t.reshape(N, 128, TW).astype(np.float32).astype(BF),
            "wt": np.ascontiguousarray(w.reshape(N, 128, 1)).astype(np.int32),
            "km": np.repeat(k.reshape(N, 8, 1, RO * M), 16, axis=2).reshape(N, 128, RO * M).astype(np.int32)}
def aim(rng, q, noth):
    u = np.arange(1, 4096, 2); i = u.copy()
    for _ in range(4): i = (i * (2 - u * i)) & 4095
    kk = ((q - (u * u >> 5)) * i) & (P - 1)
    ok = np.flatnonzero((kk < 2048) & (((u * u >> 4) & (TW - 1)) != noth))
    s = int(rng.choice(ok)); return int(u[s]), int(kk[s])
def column(rng, w, u, s):
    c = rng.integers(0, 128, 16); c[15] = s; c[:2] = 0
    z = (u - int(np.sum(w * c))) & 4095; c[0] = z & 63; c[1] = z >> 6
    return c
def setup_inputs(rng):
    return pack(*parts(rng))
def setup_inputs_ends(rng):
    v, t, w, k = parts(rng); w[:, :, 0] = 1; w[:, :, 1] = 64; w[:, :, 15] = 0
    for r in range(N):
        o = (r + 1) % N
        for g in range(8):
            case = (g - r) % 9
            a = int(rng.integers(1, P // 4)); b = int(rng.integers(P // 2, 3 * P // 4))
            if case < 2: a, b = 0, P - 1
            if case in (2, 3): b = a + 1
            if case == 8: a, b = int(rng.integers(1, P // 8)), int(rng.integers(7 * P // 8, P - 8))
            p, q = a, b
            if case == 7 or (case < 6 and rng.random() < 0.5): p, q = b, a
            s = int(rng.integers(0, 2)); u, k[r, g, 0, 0] = aim(rng, q, -1); c = column(rng, w[r, g], u, s); h = (u * u >> 4) & (TW - 1)
            if case == 4: v[r, g, 15] = s
            v[r, g, :, p] = c; v[r, g, :, q] = c
            if case in (0, 3): v[r, g, 15, q] = 1 - s
            t[o, g, :15, h] = c[:15]
            if case == 6: v[r, g, :, int(rng.integers(a + 1, b))] = c
            if case == 7: v[r, g, :, b + 3] = c
            if case in (1, 4, 5, 7, 8):
                p2, q2 = {1: (P // 3, P // 2), 4: (a + 1, P - 1), 5: (b - 1, b + 1), 7: (a + 2, b - 2), 8: (P // 2, P - 3)}[case]
                if (case == 4 and r % 2 == 0) or rng.random() < 0.5: p2, q2 = q2, p2
                u2, k[r, g, 0, 1] = aim(rng, q2, h); c2 = column(rng, w[r, g], u2, s if case == 4 else int(rng.integers(0, 2))); h2 = (u2 * u2 >> 4) & (TW - 1)
                v[r, g, :, p2] = c2; v[r, g, :, q2] = c2; t[o, g, :15, h2] = c2[:15]; t[o, g, 0, h2] = c2[0] ^ (2 if case == 8 else 1)
            if case == 8:
                ks = np.arange(2048); zs = ((u * u >> 5) + ks * u) & (P - 1)
                ks = ks[(zs > a) & (zs < b) & (zs != P // 2)]
                k[r, g, 0, 2] = int(rng.choice(ks)); z = ((u * u >> 5) + int(k[r, g, 0, 2]) * u) & (P - 1)
                cz = c.copy(); cz[0] = c[0] ^ 1; uz = (u + int(cz[0]) - int(c[0])) & 4095
                v[r, g, :, z] = cz; t[o, g, :15, (u * uz >> 4) & (TW - 1)] = c[:15]
    return pack(v, t, w, k)
def setup_inputs_kinds(rng):
    v, t, w, k = parts(rng); w[:] = w[:1].copy(); w[:, :, 15] = 0
    for g in (0, 2, 4):
        w[:, g, 0] = 1; w[:, g, 1] = 64; w[:, g, (2 if g == 2 else 8):] = 0
        u = 3 if g == 4 else 2 * int(rng.integers(0, 2048)) + 1; c = column(rng, w[0, g], u, 0)
        if g != 2: v[:, g, :8] = c[:8, None]
        else:
            v[:, g, :2] = c[:2, None]; v[:, g, 2:15] = rng.integers(0, 41, (N, 13, P)); k[:, g, 0] = k[:, g, 0, :1].copy()
            for r in range(N): v[r, g, 2:15, ((u * u >> 5) + int(k[r, g, 0, 0]) * u) & (P - 1)] = rng.integers(120, 128, 13)
    for g in (1, 3, 5, 6, 7):
        n = 5 if g % 2 else int(rng.integers(2, 6)); kd = rng.integers(0, 128, (16, n))
        if g % 2:
            kd[:, 4] = rng.integers(40, 88, 16)
            kd[:, :4] = kd[:, 4:] + rng.integers(8, 41, (16, 4)) * (2 * rng.integers(0, 2, (16, 4)) - 1)
        for r in range(N):
            kind = rng.integers(0, n, P)
            if g % 2:
                c = r % 4; uc, u4 = [int(np.sum(w[r, g] * kd[:, i])) & 4095 for i in (c, 4)]
                kind[((u4 * u4 >> 5) + k[r, g, 0] * u4) & (P - 1)] = c
                t[(r + 1) % N, g, :15, (uc * u4 >> 4) & (TW - 1)] = (kd[:15, c] + kd[:15, 4]) >> 1
            v[r, g] = kd[:, kind]
    v[:, :, 15] = rng.integers(0, 2, (N, 8, P))
    return pack(v, t, w, k)
def setup_inputs_void(rng):
    v, t, w, k = parts(rng); w[:, :, 0] = 1; w[:, :, 1] = 64; k[:, ::2] = k[:, ::2, :1, :1].copy()
    for g in (0, 6):
        v[:, g, 2:15] &= 3; t[:, g, :15] = 124 + (t[:, g, :15] & 3)
    us = np.arange(4096); j = np.arange(P)
    for r in range(N):
        for g in range(8):
            pre = np.full(P, -1); pre[((us * us >> 5) + int(k[r, g, 0, 0]) * us) & (P - 1)] = us
            z = (pre - np.sum(w[r, g, 2:, None] * v[r, g, 2:], axis=0)) & 4095
            v[r, g, 0] = np.where(pre >= 0, z & 63, v[r, g, 0]); v[r, g, 1] = np.where(pre >= 0, z >> 6, v[r, g, 1])
            if g in (0, 6):
                u = np.sum(w[r, g, :, None] * v[r, g], axis=0) & 4095; q = ((u * u >> 5) + int(k[r, g, 0, 0]) * u) & (P - 1)
                h = (u * u[q] >> 4) & (TW - 1); free = np.flatnonzero((q == j) & ~np.isin(h, h[q != j]))
                if len(free):
                    p = int(rng.choice(free)); t[(r + 1) % N, g, :15, int(h[p])] = v[r, g, :15, p]
    return pack(v, t, w, k)
def setup_inputs_small(rng):
    v, t, w, k = parts(rng)
    return pack(v & 1, t & 1, w, k)
def setup_inputs_spread(rng):
    v, t, w, k = parts(rng); both = []
    for a in (v, t):
        n = a.shape[-1]; b = np.minimum((np.exp2(8 * rng.random((N, 8, 1, n))) * rng.random(a.shape)).astype(np.int64), 127)
        z = rng.integers(0, 32, (N, 8, 1, n)); b = np.where(z == 0, 0, np.where(z == 1, 127, b)); b[:, :, 15] = a[:, :, 15]; both.append(b)
    w = np.minimum(np.exp2(8.1 * rng.random((N, 8, 16))).astype(np.int64), 255); w[:, :, 3] = 0; w[:, :, 4] = 255
    w[:, 5] = rng.integers(200, 256, (N, 16)); w[:, 6] = 255
    both[0][:, 5, :15] = rng.integers(100, 128, (N, 15, P)); both[0][:, 6, :15] = rng.integers(64, 128, (N, 15, P))
    both[0][:, 6, :15, P - 1] = 127; both[0][:, 6, 15, P - 1] = 1
    k = np.minimum(np.exp2(11.1 * rng.random((N, 8, RO, M))).astype(np.int64) - 1, 2047); k[:, 1, 0, 0] = 0; k[:, 2, 0, 1] = 2047
    return pack(both[0], both[1], w, k)
def check_inputs(d):
    bad = []
    for name in ("x", "tm"):
        a = np.asarray(d[name]).astype(np.float32)
        if not np.all((a >= 0) & (a <= 127) & (np.floor(a) == a)): bad.append("whole numbers of " + name)
        if not np.all(a[:, 15::16] <= 1): bad.append("signs of " + name)
    for name, hi in (("wt", 255), ("km", 2047)):
        if np.min(d[name]) < 0 or np.max(d[name]) > hi: bad.append("range of " + name)
    a = np.asarray(d["km"]); a = a.reshape(a.shape[0], 8, 16, -1)
    if not np.all(a == a[:, :, :1]): bad.append("rows of km alike")
    return bad
def reference(x, tm, wt, km):
    v = x.astype(np.float32).astype(np.int32).reshape(N, 8, 16, P); tp = tm.astype(np.float32).astype(np.int32).reshape(N, 8, 16, TW)
    w = wt.astype(np.int32).reshape(N, 8, 16, 1); k = km.astype(np.int32).reshape(N, 8, 16, RO, M)[:, :, 0]; j = np.arange(P)
    for t in range(RO):
        u = np.add.reduce(w * v, axis=2, dtype=np.int32) & 4095
        bq = bd = None
        for m in range(M):
            q = ((u * u >> 5) + k[:, :, t, m][:, :, None] * u) & (P - 1)
            xq = np.take_along_axis(v, q[:, :, None, :], 3)
            dm = np.where(q == j, 8192, np.add.reduce(np.abs(v - xq)[:, :, :15], axis=2))
            if m == 0: bq, bd = q, dm
            else: bq, bd = np.where(dm < bd, q, bq), np.minimum(bd, dm)
        xq = np.take_along_axis(v, bq[:, :, None, :], 3)
        h = (u * np.take_along_axis(u, bq, 2) >> 4) & (TW - 1)
        got = np.stack([np.take_along_axis(tp[(r + 1 + t % (N - 1)) % N], h[r][:, None, :], 2) for r in range(N)])
        e = bd + np.add.reduce(np.abs(v + xq - 2 * got)[:, :, :15], axis=2)
        alike = v[:, :, 15] == xq[:, :, 15]; lo = np.minimum(j, bq); hi = np.maximum(j, bq)
        nv = np.empty_like(v)
        for r in range(N):
            for g in range(8):
                p = int(np.argmin(e[r, g])); a, b = int(lo[r, g, p]), int(hi[r, g, p])
                z = v[r, g].copy(); z[:15, a] = (v[r, g, :15, a] + v[r, g, :15, b]) >> 1
                tp[r, g, :, int(h[r, g, p])] = z[:, a]
                if not alike[r, g, p]:
                    z[:, a + 1:b + 1] = z[:, a + 1:b + 1][:, ::-1].copy(); z[15, a + 1:b + 1] = 1 - z[15, a + 1:b + 1]
                else:
                    c, d = b, P - 1
                    inside = alike[r, g] & (lo[r, g] > a) & (lo[r, g] < b)
                    if np.any(inside):
                        p2 = int(np.argmin(np.where(inside, e[r, g], 2 ** 20)))
                        if hi[r, g, p2] > b: c, d = int(lo[r, g, p2]), int(hi[r, g, p2])
                    z = z[:, np.concatenate([j[:a + 1], j[b + 1:d + 1], j[c + 1:b + 1], j[a + 1:c + 1], j[d + 1:]])]
                nv[r, g] = z
        v = nv
    return {"y": v.reshape(N, 128, P).astype(np.float32).astype(BF)}

@@ -1,0 +1,644 @@
+from concourse.mybir import AluOpType, AxisListType, ActivationFunctionType
+
+P = 4096
+FO = P + 16
+XW = FO + P
+HALF = 2048
+HC = 128
+BANK = 512
+SDT = (1856, 672, 480, 352, 512, 512)
+SY = (608, 448)
+SET = (768, 448)
+YC = 1248
+CUT = (1024, 1536)
+MOVE = ((0, 1024, "s"), (1024, 2048, "v"), (2048, 3072, "s"), (3072, 4096, "v"))
+VOID = 1920.0
+
+BF, F4, I4, U2 = "bfloat16", "float32", "int32", "uint16"
+SCRATCH = {"PS": ("psum", [128, 4096], F4)}
+for _names, _w, _d in ((("XB0", "XB1"), XW, BF), (("T1", "T2", "T3"), P + 16, BF), (("TMB", "YB", "ZB", "NX"), P, BF),
+                       (("AD0", "AD1", "AD2"), HALF, BF), (("XQ", "NA"), 1024, BF), (("SG1", "SG2", "VD"), 256, BF), (("EQ",), 768, BF),
+                       (("KM",), 12, I4), (("WT", "PIX", "II", "GI"), 1, I4), (("KMF",), 12, F4),
+                       (("WTF", "IF", "GF", "PF", "G15", "FM", "FM2", "SM", "I0", "PADC"), 1, F4),
+                       (("ROW", "Z0"), 144, F4), (("ROWI", "ROWG"), 128, I4), (("NB", "NF", "PN"), 256, F4),
+                       (("GM", "IDF", "I2K"), 128, F4), (("D16",), 16, F4), (("ZW", "ZD", "ZE", "ZS"), 144, BF),
+                       (("IB", "IN", "IEQ", "IVD"), 128, BF), (("UR", "U", "US", "V1", "KI", "IQ", "IH", "KD", "UQ", "UA", "UH"), 256, I4),
+                       (("QR", "QI"), 768, I4), (("QO",), 768, U2), (("QB",), 768, F4), (("QSO", "HO", "RO"), 256, U2),
+                       (("KA", "KB", "KF", "DIRT", "CC", "NN", "K2", "Y0", "Y1", "VA", "TA", "TB", "TC"), 256, F4),
+                       (("CF",), 64, F4), (("CI",), 16, I4), (("OFF",), 16, U2), (("R32",), 32, F4), (("GQ",), 64, F4),
+                       (("XA", "XC"), 16, F4), (("NI", "NJ"), 16, I4),
+                       (("UP0", "UP1", "UP2", "RU10", "RU11", "RU12", "RU20", "RU30", "RU31"), 32, F4)):
+    for _n in _names:
+        SCRATCH[_n] = ("sbuf", [128, _w], _d)
+UPD = [(1, 0), (2, 0), (3, 0), (1, 1), (3, 1), (1, 2)]
+SEMAPHORES = (["cv", "cs", "cp", "cg", "km", "wt", "xf", "sa", "sb", "ls"] + ["x%d" % i for i in range(4)] + ["tm%d" % i for i in range(2)]
+              + ["nx0", "nx1"] + ["y%d" % i for i in range(4)] + ["rt1", "rt2", "rt3"] + ["ru%d%d" % u for u in UPD])
+
+OP = AluOpType
+ACT = ActivationFunctionType
+COPY = ACT.Identity
+
+
+def r(name, c0, c1, step=1):
+    return ("r", name, c0, c1, step)
+
+
+def ind(win, off):
+    return ("i", win, off)
+
+
+def rank_program(g, core, T, topo):
+    rank = T.rank_of(core)
+    if rank is None:
+        return
+    N = len(T.cores)
+    queue = {"v": g.vector, "s": g.scalar, "p": g.tensor, "g": g, "y": g.sync}
+    own = {"v": "cv", "s": "cs", "p": "cp", "g": "cg"}
+    total = {}
+    clock = {q: {} for q in queue}
+    rec = {}
+    bank = {}
+    serial = [0]
+
+    def merge(a, b):
+        for k, v in b.items():
+            if a.get(k, 0) < v:
+                a[k] = v
+
+    def need(q, outs, ins):
+        deps = []
+        for (_, name, c0, c1, st) in ins:
+            for x in rec.get(name, []):
+                if x[2] and x[0] < c1 and c0 < x[1]:
+                    deps.append(x)
+        for (_, name, c0, c1, st) in outs:
+            for x in rec.get(name, []):
+                if x[0] < c1 and c0 < x[1] and not (x[3] == q and q == "p"):
+                    deps.append(x)
+        for (_, name, c0, c1, st) in list(outs) + list(ins):
+            if name == "PS":
+                for b in range(c0 // BANK, (c1 - 1) // BANK + 1):
+                    for q2, x in bank.get(b, {}).items():
+                        if q2 != q:
+                            deps.append(x)
+        ck = clock[q]
+        deps.sort(key=lambda x: -x[6])
+        todo = {}
+        for x in deps:
+            sem, val = x[4]
+            if ck.get(sem, 0) < val:
+                todo[sem] = max(todo.get(sem, 0), val)
+                merge(ck, x[5])
+        for sem, val in todo.items():
+            queue[q].wait_ge(T.sem[sem], val)
+
+    def note(q, ck, outs, ins, tok):
+        serial[0] += 1
+        snap = dict(ck)
+        merge(snap, {tok[0]: tok[1]})
+        for lst, w in ((ins, False), (outs, True)):
+            for (_, name, c0, c1, st) in lst:
+                new = (c0, c1, w, q, tok, snap, serial[0])
+                old = rec.get(name, [])
+                if w and st == 1:
+                    old = [x for x in old if not (c0 <= x[0] and x[1] <= c1)]
+                elif not w:
+                    old = [x for x in old if x[2] or x[3] != q or not (c0 <= x[0] and x[1] <= c1)]
+                old.append(new)
+                rec[name] = old
+                if name == "PS":
+                    for b in range(c0 // BANK, (c1 - 1) // BANK + 1):
+                        bank.setdefault(b, {})[q] = new
+
+    def ap(a):
+        if isinstance(a, tuple) and a and a[0] == "r":
+            return T[a[1]][:, a[2]:a[3]] if a[4] == 1 else T[a[1]][:, a[2]:a[3]:a[4]]
+        if isinstance(a, tuple) and a and a[0] == "i":
+            return ap(a[1]).indirect(ap(a[2]))
+        return a
+
+    def regs(a):
+        if isinstance(a, tuple) and a and a[0] == "r":
+            return [a]
+        if isinstance(a, tuple) and a and a[0] == "i":
+            return [a[1], a[2]]
+        return []
+
+    def bump(sem, n):
+        total[sem] = total.get(sem, 0) + n
+        return (sem, total[sem])
+
+    def E(q, call, out, *args, **kw):
+        outs = regs(out)
+        ins = outs[1:]
+        outs = outs[:1]
+        for a in list(args) + list(kw.values()):
+            ins = ins + regs(a)
+        need(q, outs, ins)
+        tok = bump(own[q], 1)
+        call(ap(out), *[ap(a) for a in args], **{k: ap(v) for k, v in kw.items()}).then_inc(T.sem[tok[0]], 1)
+        note(q, clock[q], outs, ins, tok)
+
+    def dma(q, sem, out_ap, in_ap, outs, ins):
+        need(q, outs, ins)
+        tok = bump(sem, 16)
+        queue[q].dma_start(out_ap, in_ap).then_inc(T.sem[sem], 16)
+        note(q + "dma", clock[q], outs, ins, tok)
+
+    def arrival(outs, tok):
+        note("remote", {}, outs, [], tok)
+
+    def ts(out, a, s1, s2, o0, o1=None):
+        if o1 is None:
+            E("v", g.vector.tensor_scalar, out, a, s1, None, o0)
+        else:
+            E("v", g.vector.tensor_scalar, out, a, s1, s2, o0, o1)
+
+    def tt(out, a, b, o):
+        E("v", g.vector.tensor_tensor, out, a, b, o)
+
+    def cp(out, a):
+        E("v", g.vector.tensor_copy, out, a)
+
+    def red(out, a):
+        E("v", g.vector.tensor_reduce, out, a, AxisListType.X, OP.min)
+
+    def act(out, a, f, **kw):
+        E("s", g.scalar.activation, out, a, f, **kw)
+
+    def mm(out, lhsT, rhs, start, stop):
+        E("p", g.tensor.matmul, out, lhsT, rhs, start, stop)
+
+    def ps(b, c0, c1):
+        return r("PS", b * BANK + c0, b * BANK + c1)
+
+    def cf(k):
+        return r("CF", k, k + 1)
+
+    def wsum(col, z, buf, c0, n, start, stop):
+        for i in range(16):
+            mm(r("PS", col, col + n // 16), r(z, 15 - i, 143 - i), r(buf, c0 + i, c0 + n, 16), start and i == 0, stop and i == 15)
+
+    U0, UQ0, SG0, PIX0 = (0, BANK + 128), (128, BANK + 256), 384, 2 * BANK + 384
+    K0 = (2 * BANK, 3 * BANK + 128)
+    KU0, KEY = 4 * BANK, 4 * BANK + 384
+    SMALL1, SMALL2 = 256, BANK + 384
+    CLAMP, YSUM = ps(7, 0, 256), ps(6, 256, 512)
+    PIXW = r("PS", PIX0, PIX0 + 256)
+
+    dma("s", "wt", T.WT[:], T.wt[:], [r("WT", 0, 1)], [])
+    dma("s", "km", T.KM[:], T.km[:], [r("KM", 0, 12)], [])
+    for i in range(4):
+        c = r("XB0", 1024 * i, 1024 * i + 1024)
+        dma("y", "x%d" % i, ap(c), T.x[:, 1024 * i:1024 * i + 1024], [c], [])
+    for i in range(2):
+        c = r("TMB", 2048 * i, 2048 * i + 2048)
+        dma("s", "tm%d" % i, ap(c), T.tm[:, 2048 * i:2048 * i + 2048], [c], [])
+    NXC = [HALF * h + min(SDT[3 * h:3 * h + 3] + SY[h:h + 1]) for h in (0, 1)]
+    for h in (0, 1):
+        c = r("NX", NXC[h], HALF * h + HALF)
+        dma("y", "nx%d" % h, ap(c), T.x[:, NXC[h]:HALF * h + HALF], [c], [])
+    E("g", g.iota, r("PIX", 0, 1), [[0, 1]], 0, 1)
+    E("g", g.iota, r("ROW", 0, 144), [[1, 144]], 0, 0, allow_small_or_imprecise_dtypes=True)
+    E("g", g.iota, r("NB", 0, 256), [[16, 256]], 0, 0, allow_small_or_imprecise_dtypes=True)
+    E("g", g.iota, r("ROWI", 0, 128), [[1, 128]], 0, 0)
+    for j in (1, 2, 3):
+        E("v", g.vector.memset, r("T%d" % j, P, P + 16), 0.0)
+    for j in (0, 1):
+        E("v", g.vector.memset, r("XB%d" % j, P, P + 16), 0.0)
+    for j in (0, 1, 2):
+        E("v", g.vector.memset, r("UP%d" % j, 0, 32), 0.0)
+    IF, PF, FM, INV15 = r("IF", 0, 1), r("PF", 0, 1), r("FM", 0, 1), r("SM", 0, 1)
+    Z0, ROWM = r("Z0", 0, 144), r("ROW", 0, 128)
+    ts(r("II", 0, 1), r("PIX", 0, 1), 15, None, OP.bitwise_and)
+    ts(r("GI", 0, 1), r("PIX", 0, 1), 4, None, OP.arith_shift_right)
+    cp(PF, r("PIX", 0, 1))
+    cp(IF, r("II", 0, 1))
+    cp(r("GF", 0, 1), r("GI", 0, 1))
+    cp(r("WTF", 0, 1), r("WT", 0, 1))
+    ts(r("G15", 0, 1), r("GF", 0, 1), 16.0, 15.0, OP.mult, OP.add)
+    ts(FM, IF, 14.5, None, OP.is_lt)
+    ts(INV15, IF, 14.5, None, OP.is_gt)
+    ts(Z0, r("ROW", 0, 144), r("G15", 0, 1), None, OP.is_equal)
+    ts(r("ZW", 0, 144), Z0, r("WTF", 0, 1), None, OP.mult)
+    cp(r("KMF", 0, 12), r("KM", 0, 12))
+    ts(r("NF", 0, 256), r("NB", 0, 256), IF, None, OP.add)
+    cp(PIXW, r("NF", 0, 256))
+    ts(r("IB", 0, 128), ROWM, PF, None, OP.is_equal)
+    ts(r("IN", 0, 128), ROWM, PF, -1.0, OP.is_equal, OP.mult)
+    ts(r("IEQ", 0, 128), ROWM, PF, VOID * 16384.0, OP.is_equal, OP.mult)
+    ts(r("IDF", 0, 128), ROWM, PF, None, OP.is_equal)
+    ts(r("ZD", 0, 144), Z0, FM, 16384.0, OP.mult, OP.mult)
+
+    sent = [0]
+
+    def send(dst, out_ap, in_reg, sem, use):
+        need("g", [], [in_reg])
+        rid, pid, _ = topo.addr(dst)
+        m = 0
+        for e in use:
+            m |= 1 << e
+        g.remote_dma(out_ap, ap(in_reg), T.sem[sem], T.sem["ls"], pid, rid, m)
+        sent[0] += len(use)
+
+    def lanes(src, dst):
+        e = topo.engines(src, dst)
+        if topo.chip(src) != topo.chip(dst):
+            return e
+        far = [topo.engines(src, c) for c in T.cores if topo.chip(c) != topo.chip(src)]
+        rest = [k for k in e if not any(k in f for f in far)]
+        return rest if rest else e
+
+    asker = {j: T.cores[(rank - j) % N] for j in (1, 2, 3)}
+    for j in (1, 2, 3):
+        n = len(lanes(T.cores[(rank + j) % N], core))
+        bump("rt%d" % j, n * (2 if j == 1 else 1))
+        arrival([r("T%d" % j, 0, P)], ("rt%d" % j, total["rt%d" % j]))
+        for (jj, t) in UPD:
+            if jj == j:
+                arrival([r("RU%d%d" % (j, t), 0, 32)], bump("ru%d%d" % (j, t), n))
+    for i in range(2):
+        c = r("TMB", 2048 * i, 2048 * i + 2048)
+        act(c, c, COPY, scale=2.0)
+        send(asker[1], T.T1[:, 2048 * i:2048 * i + 2048], c, "rt1", lanes(core, asker[1]))
+    send(asker[2], T.T2[:, 0:P], r("TMB", 0, P), "rt2", lanes(core, asker[2]))
+    send(asker[3], T.T3[:, 0:P], r("TMB", 0, P), "rt3", lanes(core, asker[3]))
+
+    def late_constants():
+        ts(r("D16", 0, 16), r("ROW", 0, 16), IF, None, OP.is_equal)
+        ts(r("ROWG", 0, 128), r("ROWI", 0, 128), 4, None, OP.arith_shift_right)
+        ts(r("ZE", 0, 144), Z0, FM, 2048.0, OP.mult, OP.mult)
+        ts(r("ZS", 0, 144), Z0, INV15, None, OP.mult)
+        ts(r("GM", 0, 128), r("ROWG", 0, 128), r("GF", 0, 1), None, OP.is_equal)
+        ts(r("IVD", 0, 128), ROWM, PF, VOID * 2048.0, OP.is_equal, OP.mult)
+        ts(r("I2K", 0, 128), ROWM, PF, 2048.0, OP.is_equal, OP.mult)
+        ts(r("PN", 0, 256), r("NF", 0, 256), -14680064.0, None, OP.add)
+        ts(r("I0", 0, 1), IF, 0.5, None, OP.is_lt)
+        ts(r("PADC", 0, 1), IF, 0.5, 4096.0, OP.is_gt, OP.mult)
+        tt(r("PADC", 0, 1), r("PADC", 0, 1), IF, OP.add)
+        ts(r("FM2", 0, 1), FM, -1.0, 2.0, OP.mult, OP.add)
+
+    def u_block(xb, b):
+        wsum(U0[b // 2] + (b % 2) * 64, "ZW", xb, 1024 * b, 1024, True, True)
+
+    def flip_copy(xb, first):
+        x0, full = r(xb, 0, P), r(xb, FO, FO + P)
+        dma("y", "sa", T.SG1[:], T[xb][15:128:16, 0:P], [r("SG1", 0, 256)], [x0])
+        dma("y", "xf", ap(full), T.x[:] if first else ap(x0), [full], [] if first else [x0])
+        ts(r("SG2", 0, 256), r("SG1", 0, 256), -1.0, 1.0, OP.mult, OP.add)
+        dma("y", "sb", T[xb][15:128:16, FO:FO + P], T.SG2[:], [full], [r("SG2", 0, 256)])
+
+    for b in range(4):
+        u_block("XB0", b)
+
+    ring = [0]
+
+    def pieces(n):
+        k = -(-n // BANK)
+        cut = [min(n, -(-n * i // (32 * k)) * 32) for i in range(k + 1)]
+        return list(zip(cut[:-1], cut[1:]))
+
+    def run(*chains):
+        chains = list(chains)
+        while chains:
+            chains = [c for c in chains if next(c, 0) is None]
+
+    for t in range(4):
+        X, X2 = "XB%d" % (t % 2), "XB%d" % (1 - t % 2)
+        xwin = r(X, 0, P)
+        tj = 1 + t % 3
+        TB = "T%d" % tj
+
+        def W(name, h, k=0):
+            return r(name, 256 * k, 256 * k + 256) if h == 2 else r(name, 256 * k + HC * h, 256 * k + HC * h + HC)
+
+        def kur(h, m):
+            return r("PS", KU0 + 256 * m + HC * h, KU0 + 256 * m + HC * h + HC)
+
+        def list_ops(h):
+            cp(W("UR", h), r("PS", U0[h], U0[h] + HC))
+            yield
+            ts(W("U", h), W("UR", h), 4095, None, OP.bitwise_and)
+            yield
+            tt(W("US", h), W("U", h), W("U", h), OP.mult)
+            ts(kur(h, 0), W("U", h), r("KMF", 3 * t, 3 * t + 1), None, OP.mult)
+            ts(W("V1", h), W("US", h), 5, None, OP.arith_shift_right)
+            yield
+            for _ in q_ops(h, 0):
+                yield
+
+        def q_ops(h, m):
+            if m:
+                ts(kur(h, m), W("U", h), r("KMF", 3 * t + m, 3 * t + m + 1), None, OP.mult)
+                yield
+            tt(W("QR", h, m), kur(h, m), W("V1", h), OP.add)
+            yield
+            ts(W("QI", h, m), W("QR", h, m), 4095, None, OP.bitwise_and)
+            yield
+            cp(W("QO", h, m), W("QI", h, m))
+
+        def q_more(m):
+            tt(W("EQ", 2, m), W("QI", 2, m), PIXW, OP.is_equal)
+            ts(W("QB", 2, m), W("QI", 2, m), 4096.0 * m - 16777216.0, None, OP.add)
+
+        def d_v(h, m):
+            oc, s = 256 * m + HC * h, SDT[3 * h + m]
+            tt(r("AD%d" % m, s, HALF), ind(xwin, r("QO", oc + s // 16, oc + HC)), r("NX", HALF * h + s, HALF * h + HALF), OP.subtract)
+
+        def d_s(h, m):
+            todo = []
+            for c, e in pieces(SDT[3 * h + m]):
+                k, n = ring[0] % 2, e - c
+                ring[0] += 1
+                oc = 256 * m + HC * h
+                act(r("XQ", 512 * k, 512 * k + n), ind(xwin, r("QO", oc + c // 16, oc + e // 16)), COPY)
+                mm(ps(6 + k, 0, n), r("IB", 0, 128), r("XQ", 512 * k, 512 * k + n), True, False)
+                mm(ps(6 + k, 0, n), r("IN", 0, 128), r(X, HALF * h + c, HALF * h + e), False, True)
+                todo.append((c, n, k))
+                if len(todo) > 1:
+                    d_abs(m, todo.pop(0))
+            return todo
+
+        def d_abs(m, job):
+            c, n, k = job
+            act(r("AD%d" % m, c, c + n), ps(6 + k, 0, n), ACT.Abs)
+
+        def d_vabs(h, m):
+            c = r("AD%d" % m, SDT[3 * h + m], HALF)
+            act(c, c, ACT.Abs)
+
+        def d_sum(h, m):
+            c = K0[h] + 128 * m
+            mm(r("PS", c, c + HC), r("IDF", 0, 128), W("QB", h, m), True, False)
+            mm(r("PS", c, c + HC), r("IEQ", 0, 128), W("EQ", h, m), False, False)
+            wsum(c, "ZD", "AD%d" % m, 0, HALF, False, True)
+
+        def choose(h):
+            c = K0[h]
+            cp(W("KA", h), r("PS", c, c + 128))
+            tt(W("KB", h), r("PS", c + 128, c + 256), W("KA", h), OP.min)
+            tt(W("KI", h), r("PS", c + 256, c + 384), W("KB", h), OP.min)
+            ts(W("IQ", h), W("KI", h), 4095, None, OP.bitwise_and)
+            cp(W("QSO", h), W("IQ", h))
+
+        def y_v(h, c0, c1):
+            c0, c1 = c0 + HALF * h, c1 + HALF * h
+            tt(r("YB", c0, c1), ind(xwin, r("QSO", c0 // 16, c1 // 16)), r("NX", c0, c1), OP.add)
+
+        def y_s(h):
+            c0 = HALF * h + SY[h]
+            act(r("YB", HALF * h, c0), ind(xwin, r("QSO", HC * h, c0 // 16)), COPY)
+
+        def u_sum(h):
+            wsum(UQ0[h], "ZW", "YB", HALF * h, HALF, True, True)
+
+        def s_sum(h):
+            wsum(SG0 + HC * h, "ZS", "YB", HALF * h, HALF, True, False)
+            wsum(SG0 + HC * h, "ZS", X, HALF * h, SY[h], False, True)
+
+        def h_ops(h):
+            s, c = SY[h] // 16, HC * h
+            cp(r("UQ", c, c + s), r("PS", UQ0[h], UQ0[h] + s))
+            tt(r("UQ", c + s, c + HC), r("PS", UQ0[h] + s, UQ0[h] + HC), r("U", c + s, c + HC), OP.subtract)
+            ts(W("UA", h), W("UQ", h), 4095, None, OP.bitwise_and)
+            tt(W("UH", h), W("UA", h), W("U", h), OP.mult)
+            ts(W("IH", h), W("UH", h), 4, 4095, OP.arith_shift_right, OP.bitwise_and)
+            cp(W("HO", h), W("IH", h))
+
+        def t_v(h, c0, c1):
+            c0, c1 = c0 + HALF * h, c1 + HALF * h
+            tt(r("ZB", c0, c1), ind(r(TB, 0, P), r("HO", c0 // 16, c1 // 16)), r("YB", c0, c1), OP.subtract)
+
+        def t_s(h):
+            todo = []
+            for c, e in pieces(SET[h]):
+                k, n = ring[0] % 2, e - c
+                ring[0] += 1
+                p0 = HALF * h + c
+                act(r("NA", 512 * k, 512 * k + n), ind(r(TB, 0, P), r("HO", p0 // 16, (p0 + n) // 16)), COPY, scale=-1.0)
+                mm(ps(6 + k, 0, n), r("IB", 0, 128), r("YB", p0, p0 + n), True, False)
+                if c < SY[h]:
+                    n1 = min(n, SY[h] - c)
+                    mm(ps(6 + k, 0, n1), r("IB", 0, 128), r(X, p0, p0 + n1), False, False)
+                mm(ps(6 + k, 0, n), r("IB", 0, 128), r("NA", 512 * k, 512 * k + n), False, True)
+                todo.append((p0, n, k))
+                if len(todo) > 1:
+                    t_abs(todo.pop(0))
+            return todo
+
+        def t_abs(job):
+            p0, n, k = job
+            act(r("ZB", p0, p0 + n), ps(6 + k, 0, n), ACT.Abs)
+
+        def t_vabs(h, c0, c1):
+            act(r("ZB", HALF * h + c0, HALF * h + c1), r("ZB", HALF * h + c0, HALF * h + c1), ACT.Abs)
+
+        def e_head(h):
+            w0, w1 = HC * h, HC * h + HC
+            o = r("PS", KEY + w0, KEY + w1)
+            mm(o, r("IDF", 0, 128), r("PN", w0, w1), True, False)
+            mm(o, r("I2K", 0, 128), r("KF", w0, w1), False, False)
+            mm(o, r("IVD", 0, 128), r("VD", w0, w1), False, False)
+
+        def e_sum(h, c0, c1):
+            wsum(KEY + HC * h + c0 // 16, "ZE", "ZB", HALF * h + c0, c1 - c0, False, c1 == HALF)
+
+        if t:
+            act(r("NX", NXC[0], HALF), r(X, NXC[0], HALF), COPY)
+            c = r("NX", NXC[1], P)
+            dma("y", "nx1", ap(c), T[X][:, NXC[1]:P], [c], [r(X, NXC[1], P)])
+        run(list_ops(0))
+        pend = None
+        for n, (h, m) in enumerate([(h, m) for h in (0, 1) for m in (0, 1, 2)]):
+            left = d_s(h, m)
+            if pend is not None:
+                d_vabs(*pend)
+            for job in left:
+                d_abs(m, job)
+            if n == 1:
+                q_more(0)
+                q_more(1)
+            elif n == 2:
+                q_more(2)
+            if pend is not None:
+                d_sum(*pend)
+            pend = (h, m)
+            if n == 0:
+                d_v(0, 0)
+                run(list_ops(1), q_ops(0, 1))
+                d_v(0, 1)
+                run(q_ops(0, 2), q_ops(1, 1), q_ops(1, 2))
+            elif n == 1:
+                d_v(0, 2)
+            elif n == 2:
+                if t == 0:
+                    late_constants()
+            else:
+                d_v(h, m)
+                if n == 3:
+                    flip_copy(X, t == 0)
+                if n == 4:
+                    choose(0)
+        d_vabs(1, 2)
+        d_sum(1, 2)
+        y_s(0)
+        y_v(0, SY[0], HALF)
+        u_sum(0)
+        s_sum(0)
+        choose(1)
+        y_s(1)
+        y_v(1, SY[1], YC)
+        for (j, tu) in UPD:
+            if j == tj and tu < t:
+                RU = "RU%d%d" % (j, tu)
+                cp(r("OFF", 8 + 2 * tu, 9 + 2 * tu), r(RU, 16, 17))
+                cp(ind(r(TB, 0, P + 16), r("OFF", 8 + 2 * tu, 9 + 2 * tu)), r(RU, 0, 16))
+        h_ops(0)
+        y_v(1, YC, HALF)
+        mid = (SET[0] + HALF) // 2 // 32 * 32
+        left = t_s(0)
+        u_sum(1)
+        ts(W("KD", 2), W("KI", 2), 14, None, OP.arith_shift_right)
+        t_v(0, SET[0], mid)
+        cp(W("KF", 2), W("KD", 2))
+        ts(W("VD", 2), W("KD", 2), VOID - 1024.0, None, OP.is_ge)
+        e_head(0)
+        e_head(1)
+        h_ops(1)
+        t_v(0, mid, HALF)
+        s_sum(1)
+        for job in left:
+            t_abs(job)
+        t_vabs(0, SET[0], mid)
+        left = t_s(1)
+        t_vabs(0, mid, HALF)
+        e_sum(0, 0, HALF)
+        for job in left:
+            t_abs(job)
+        cuts = [SET[1], CUT[0], CUT[1], HALF]
+        for c0, c1 in zip(cuts[:-1], cuts[1:]):
+            t_v(1, c0, c1)
+            t_vabs(1, c0, c1)
+        e_sum(1, 0, CUT[0])
+        e_sum(1, CUT[0], HALF)
+        red(cf(0), r("PS", KEY, KEY + HC))
+        ts(r("R32", 0, 16), r("D16", 0, 16), cf(0), None, OP.mult)
+        tt(ps(2, 0, 256), W("IQ", 2), PIXW, OP.min)
+        ts(W("DIRT", 2), r("PS", SG0, SG0 + 256), 1.0, None, OP.not_equal)
+        tt(W("CC", 2), ps(2, 0, 256), W("DIRT", 2), OP.mult)
+        red(cf(1), r("PS", KEY + HC, KEY + 2 * HC))
+        ts(r("R32", 16, 32), r("D16", 0, 16), cf(1), None, OP.mult)
+
+        s1, s2 = SMALL1, SMALL2
+        mm(r("PS", s1, s1 + 32), r("GM", 0, 128), r("R32", 0, 32), True, True)
+        kk = r("CI", 0, 1)
+        red(kk, r("PS", s1, s1 + 32))
+        ts(r("CI", 1, 2), kk, 4, 255, OP.arith_shift_right, OP.bitwise_and)
+        ts(r("CI", 2, 3), kk, 15, None, OP.bitwise_and)
+        cp(r("OFF", 0, 1), r("CI", 1, 2))
+        tt(cf(2), r("II", 0, 1), r("CI", 2, 3), OP.is_equal)
+        ts(r("CI", 3, 4), kk, 4095, None, OP.bitwise_and)
+        for n, w in enumerate(["IQ", "DIRT", "IH"]):
+            ts(r("GQ", 16 * n, 16 * n + 16), ind(r(w, 0, 256), r("OFF", 0, 1)), cf(2), None, OP.mult)
+        mm(r("PS", s2, s2 + 48), r("GM", 0, 128), r("GQ", 0, 48), True, True)
+        cp(cf(3), r("CI", 3, 4))
+        q1, dirc, hc = r("PS", s2, s2 + 1), r("PS", s2 + 16, s2 + 17), r("PS", s2 + 32, s2 + 33)
+        a, b = cf(6), cf(7)
+        ts(cf(4), q1, cf(3), 0.5, OP.min, OP.add)
+        ts(cf(5), q1, cf(3), -0.5, OP.max, OP.add)
+        ts(CLAMP, r("CC", 0, 256), cf(4), cf(5), OP.max, OP.min)
+        ts(a, q1, cf(3), None, OP.min)
+        ts(b, q1, cf(3), None, OP.max)
+        tt(r("NN", 0, 256), CLAMP, r("CC", 0, 256), OP.is_equal)
+        ts(r("OFF", 2, 3), q1, cf(3), None, OP.min)
+        ts(r("OFF", 4, 5), q1, cf(3), None, OP.max)
+        tt(r("K2", 0, 256), r("PS", KEY, KEY + 256), r("NN", 0, 256), OP.mult)
+        if t < 3:
+            ts(r("UP%d" % t, 16, 17), hc, r("I0", 0, 1), r("PADC", 0, 1), OP.mult, OP.add)
+        cp(cf(8), dirc)
+        mm(YSUM, r("IDF", 0, 128), r("NF", 0, 256), True, False)
+        red(cf(0), r("K2", 0, 256))
+        act(cf(9), cf(8), COPY, scale=-1.0, bias=1.0)
+        act(cf(10), a, COPY, bias=b)
+        act(cf(18), cf(9), COPY, scale=FO + 1.0)
+        act(cf(12), a, COPY, scale=-1.0, bias=b)
+        act(cf(11), cf(10), COPY, scale=cf(9), bias=cf(18))
+        act(cf(32), cf(12), COPY, scale=cf(8))
+        act(cf(19), cf(11), COPY, scale=-1.0)
+        act(cf(13), cf(12), COPY, scale=cf(8), bias=cf(19))
+        act(cf(20), cf(9), COPY, scale=4095.0)
+        act(cf(21), b, COPY, scale=cf(8), bias=cf(20))
+        act(cf(25), cf(32), COPY, scale=-1.0)
+        act(r("XA", 0, 16), ind(xwin, r("OFF", 2, 3)), COPY, scale=r("FM2", 0, 1))
+        act(r("XC", 0, 16), ind(xwin, r("OFF", 4, 5)), COPY, scale=FM)
+        ts(r("R32", 0, 16), r("D16", 0, 16), cf(0), None, OP.mult)
+        mm(r("PS", s1, s1 + 16), r("GM", 0, 128), r("R32", 0, 16), True, True)
+        ts(r("OFF", 6, 7), a, r("I0", 0, 1), r("PADC", 0, 1), OP.mult, OP.add)
+        kk = r("CI", 4, 5)
+        red(kk, r("PS", s1, s1 + 16))
+        ts(r("CI", 5, 6), kk, 4, 255, OP.arith_shift_right, OP.bitwise_and)
+        ts(r("CI", 6, 7), kk, 15, None, OP.bitwise_and)
+        cp(r("OFF", 0, 1), r("CI", 5, 6))
+        tt(cf(33), r("II", 0, 1), r("CI", 6, 7), OP.is_equal)
+        ts(r("CI", 7, 8), kk, 4095, None, OP.bitwise_and)
+        ts(r("GQ", 48, 64), ind(r("IQ", 0, 256), r("OFF", 0, 1)), cf(33), None, OP.mult)
+        mm(r("PS", s2, s2 + 16), r("GM", 0, 128), r("GQ", 48, 64), True, True)
+        ts(cf(15), kk, 0.0, cf(8), OP.is_lt, OP.mult)
+        ts(r("Y0", 0, 256), r("NF", 0, 256), a, cf(13), OP.is_gt, OP.mult)
+        mm(YSUM, r("IDF", 0, 128), r("Y0", 0, 256), False, False)
+        cp(cf(14), r("CI", 7, 8))
+        ts(cf(16), cf(15), -8192.0, 8192.0, OP.mult, OP.add)
+        tt(r("NI", 0, 16), r("XA", 0, 16), r("XC", 0, 16), OP.add)
+        tt(cf(17), cf(16), b, OP.add)
+        ts(r("Y1", 0, 256), r("NF", 0, 256), b, cf(11), OP.is_gt, OP.mult)
+        mm(YSUM, r("IDF", 0, 128), r("Y1", 0, 256), False, True)
+        act(r("VA", 0, 256), YSUM, ACT.Abs)
+        q2 = r("PS", s2, s2 + 1)
+        d, L = cf(27), cf(28)
+        ts(cf(22), q2, cf(14), cf(17), OP.max, OP.is_gt)
+        ts(cf(23), q2, cf(14), cf(21), OP.min, OP.subtract)
+        ts(cf(24), q2, cf(14), 4095.0, OP.max, OP.subtract)
+        ts(cf(26), cf(23), cf(22), cf(21), OP.mult, OP.add)
+        ts(d, cf(24), cf(22), 4095.0, OP.mult, OP.add)
+        ts(r("NJ", 0, 16), r("NI", 0, 16), 1, None, OP.arith_shift_right)
+        tt(L, d, cf(26), OP.subtract)
+        tt(cf(29), d, cf(12), OP.subtract)
+        cp(ind(r(X, 0, P + 16), r("OFF", 6, 7)), r("NJ", 0, 16))
+        tt(cf(31), L, a, OP.add)
+        ts(cf(30), L, -1.0, None, OP.mult)
+
+        o1, o2 = [[ps(4 + k, HC * h, HC * h + HC) for h in (0, 1)] for k in (0, 1)]
+        o3 = [r("PS", K0[h], K0[h] + HC) for h in (0, 1)]
+        both = (0, 1)
+        for h in both:
+            ts(o1[h], W("NF", h), d, L, OP.is_gt, OP.mult)
+            ts(W("TB", h), W("NF", h), cf(31), cf(25), OP.is_gt, OP.mult)
+        for h in both:
+            ts(o2[h], W("NF", h), cf(29), cf(30), OP.is_gt, OP.mult)
+            tt(W("TA", h), o1[h], W("TB", h), OP.add)
+        for h in both:
+            tt(o3[h], o2[h], W("TA", h), OP.add)
+        for h in both:
+            tt(W("TC", h), o3[h], W("VA", h), OP.add)
+        for h in both:
+            cp(W("RO", h), W("TC", h))
+        for n, (c0, c1, q) in enumerate(MOVE):
+            src = ind(r(X, 0, XW), r("RO", c0 // 16, c1 // 16))
+            if q == "s":
+                act(r(X2, c0, c1), src, COPY)
+            else:
+                cp(r(X2, c0, c1), src)
+            if t == 3:
+                dma("y", "y%d" % n, T.y[:, c0:c1], T[X2][:, c0:c1], [], [r(X2, c0, c1)])
+        if t < 3:
+            for bl in range(4):
+                u_block(X2, bl)
+            ts(r("UP%d" % t, 0, 16), r("NJ", 0, 16), 2.0, None, OP.mult)
+            for (j, tu) in UPD:
+                if tu == t:
+                    send(asker[j], T["RU%d%d" % (j, t)][:], r("UP%d" % t, 0, 32), "ru%d%d" % (j, t), lanes(core, asker[j]))
+
+    total["ls"] = sent[0]
+    for sem, val in total.items():
+        if clock["g"].get(sem, 0) < val:
+            g.wait_ge(T.sem[sem], val)

@@ -6,37 +6,48 @@ XW = FO + P
 HALF = 2048
 HC = 128
 BANK = 512
-SDT = (1856, 672, 480, 352, 512, 512)
-SY = (608, 448)
-SET = (768, 448)
-YC = 1248
-CUT = (1024, 1536)
+SDT = (768, 896, 736, 288, 0, 320)
+UNITS = ((0, 1024, 1024, 1024), (1024, 2048, 448, 1024), (2048, 3072, 0, 256), (3072, 4096, 32, 288))
 MOVE = ((0, 1024, "s"), (1024, 2048, "v"), (2048, 3072, "s"), (3072, 4096, "v"))
+WENG = "sssssvss"
+ENG = {"n": "s", "kur0": "v", "kur": "v", "ka": "v", "cv": "v", "sp": "s"}
+MINP = 256
+ORDER = ("wi5 li00 wi0 wi4 li01 wi3 li10 wi6 wi7 wi2 sp0 li12 li11 wi1 dv00 ds00 li02 ds01 su00 dv01 dv02 ds02 su01 ds10 sp1 su02 dv10 ds12 ys1 ys0 yv1 yv0 "
+         "hh0 tw ds11 dv11 su10 dv12 su11 su12 yv2 hh1 ts0 ts1 yv3 ys2 ys3 eh0 tv1 hh3 hh2 zy1 eh1 ki0 zy0 tv0 es0 tv2 fl zy2 es1 ts2 ts3 tv3 zy3 ki1 es2 es3").split()
+ORDER0 = ORDER
 VOID = 1920.0
+BIG = 33554432.0
 
-BF, F4, I4, U2 = "bfloat16", "float32", "int32", "uint16"
+BF, F2, F4, I4, U2 = "bfloat16", "float16", "float32", "int32", "uint16"
 SCRATCH = {"PS": ("psum", [128, 4096], F4)}
-for _names, _w, _d in ((("XB0", "XB1"), XW, BF), (("T1", "T2", "T3"), P + 16, BF), (("TMB", "YB", "ZB", "NX"), P, BF),
-                       (("AD0", "AD1", "AD2"), HALF, BF), (("XQ", "NA"), 1024, BF), (("SG1", "SG2", "VD"), 256, BF), (("EQ",), 768, BF),
-                       (("KM",), 12, I4), (("WT", "PIX", "II", "GI"), 1, I4), (("KMF",), 12, F4),
-                       (("WTF", "IF", "GF", "PF", "G15", "FM", "FM2", "SM", "I0", "PADC"), 1, F4),
-                       (("ROW", "Z0"), 144, F4), (("ROWI", "ROWG"), 128, I4), (("NB", "NF", "PN"), 256, F4),
-                       (("GM", "IDF", "I2K"), 128, F4), (("D16",), 16, F4), (("ZW", "ZD", "ZE", "ZS"), 144, BF),
-                       (("IB", "IN", "IEQ", "IVD"), 128, BF), (("UR", "U", "US", "V1", "KI", "IQ", "IH", "KD", "UQ", "UA", "UH"), 256, I4),
-                       (("QR", "QI"), 768, I4), (("QO",), 768, U2), (("QB",), 768, F4), (("QSO", "HO", "RO"), 256, U2),
-                       (("KA", "KB", "KF", "DIRT", "CC", "NN", "K2", "Y0", "Y1", "VA", "TA", "TB", "TC"), 256, F4),
-                       (("CF",), 64, F4), (("CI",), 16, I4), (("OFF",), 16, U2), (("R32",), 32, F4), (("GQ",), 64, F4),
+for _names, _w, _d in ((("XB0", "XB1"), XW, BF), (("TW1", "TW2"), P + 16, F4), (("W",), P, F4),
+                       (("TMB", "L1", "L2", "L3", "YB"), P, BF), (("ZB",), P, F2), (("AD",), 3 * P, F2),
+                       (("SG1", "SG2", "NN", "CV", "M1", "M2", "INVB"), 256, BF), (("EQ",), 768, BF), (("QB",), 768, F2),
+                       (("UC", "KF", "VD", "CMC"), 256, F2), (("SPW",), 512, F2), (("C16",), 128, BF), (("NJH",), 16, F2),
+                       (("KM",), 12, I4), (("WT", "PIX", "II", "GI"), 1, I4), (("KMF", "KP"), 12, F4),
+                       (("COL",), 32, F4), (("ROW", "Z0"), 144, F4), (("ROWI", "ROWG"), 128, I4), (("NB", "NF", "PN"), 256, F4),
+                       (("GM", "GMN", "IDF", "C15"), 128, F4), (("D16",), 16, F4), (("ZD", "ZM", "ZY"), 144, BF), (("ZV",), 144, F2),
+                       (("IB", "IN", "IEQ", "IVD", "I2K", "I16K", "IM4", "IBG", "ONE", "BW", "BT", "CK0", "CK1", "CK2"), 128, BF), (("CA",), 384, F2), (("W3",), 24, BF),
+                       (("V1", "KI", "IQ", "IH", "KD", "VI", "UA", "UH", "INV"), 256, I4),
+                       (("QR", "QI"), 768, I4), (("QO",), 768, U2), (("QSO", "HO", "RO"), 256, U2),
+                       (("US", "KA", "KB", "KS", "CM", "Y0", "Y1", "VA", "TA", "TB", "TC"), 256, F4),
+                       (("CF",), 64, F4), (("CI",), 16, I4), (("OFF",), 16, U2), (("R32",), 32, F4), (("GQ",), 128, F4),
                        (("XA", "XC"), 16, F4), (("NI", "NJ"), 16, I4),
                        (("UP0", "UP1", "UP2", "RU10", "RU11", "RU12", "RU20", "RU30", "RU31"), 32, F4)):
     for _n in _names:
         SCRATCH[_n] = ("sbuf", [128, _w], _d)
 UPD = [(1, 0), (2, 0), (3, 0), (1, 1), (3, 1), (1, 2)]
-SEMAPHORES = (["cv", "cs", "cp", "cg", "km", "wt", "xf", "sa", "sb", "ls"] + ["x%d" % i for i in range(4)] + ["tm%d" % i for i in range(2)]
-              + ["nx0", "nx1"] + ["y%d" % i for i in range(4)] + ["rt1", "rt2", "rt3"] + ["ru%d%d" % u for u in UPD])
+NT1 = 2
+SEMAPHORES = (["cv", "cs", "cp", "cg", "km", "wt", "xf", "sa", "sb", "ls"] + ["x%d" % i for i in range(4)] + ["tm%d" % i for i in range(NT1)]
+              + ["y%d" % i for i in range(len(MOVE))] + ["rt1%d" % i for i in range(NT1)]
+              + ["rt2", "rt3", "hand"] + ["ru%d%d" % u for u in UPD])
 
+STAT, DRY, NR = [], False, 4
 OP = AluOpType
 ACT = ActivationFunctionType
 COPY = ACT.Identity
+CYC, GAT, PEC, LAT, SFIX, DLAT, DRATE = 0.83, 1.3, 0.55, 150.0, 100.0, 1800.0, 300.0
+ARR = {1: 22000.0, 2: 30000.0, 3: 45000.0}
 
 
 def r(name, c0, c1, step=1):
@@ -47,13 +58,692 @@ def ind(win, off):
     return ("i", win, off)
 
 
+def width(a):
+    return 16 * (a[2][3] - a[2][2]) if a[0] == "i" else -(-(a[3] - a[2]) // a[4])
+
+
 def rank_program(g, core, T, topo):
     rank = T.rank_of(core)
-    if rank is None:
-        return
     N = len(T.cores)
+
+    def lanes(src, dst):
+        e = topo.engines(src, dst)
+        if topo.chip(src) != topo.chip(dst):
+            return e
+        far = [topo.engines(src, c) for c in T.cores if topo.chip(c) != topo.chip(src)]
+        rest = [k for k in e if not any(k in f for f in far)]
+        return rest if rest else e
+
+    def relay(k):
+        src, dst = T.cores[k], T.cores[(k - 3) % N]
+        return [c for c in topo.cores_of(src) if topo.die(c) == topo.die(src) and c not in T.cores and topo.may_write(c, dst)][0]
+
+    if rank is None:
+        for k in range(N):
+            if relay(k) == core:
+                dst = T.cores[(k - 3) % N]
+                rid, pid, _ = topo.addr(dst)
+                use = lanes(core, dst)
+                g.wait_ge(T.sem.hand, len(lanes(T.cores[k], core)))
+                g.remote_dma(T.L3[:], T.L3[:], T.sem.rt3, T.sem.ls, pid, rid, sum(1 << e for e in use))
+                g.wait_ge(T.sem.ls, len(use))
+        return
     queue = {"v": g.vector, "s": g.scalar, "p": g.tensor, "g": g, "y": g.sync}
     own = {"v": "cv", "s": "cs", "p": "cp", "g": "cg"}
+
+    def ap(a):
+        if isinstance(a, tuple) and a and a[0] == "r":
+            return T[a[1]][:, a[2]:a[3]] if a[4] == 1 else T[a[1]][:, a[2]:a[3]:a[4]]
+        if isinstance(a, tuple) and a and a[0] == "i":
+            return ap(a[1]).indirect(ap(a[2]))
+        return a
+
+    def regs(a):
+        if isinstance(a, tuple) and a and a[0] == "r":
+            return [a]
+        if isinstance(a, tuple) and a and a[0] == "i":
+            return [a[1], a[2]]
+        return []
+
+    def banks_of(lst):
+        return sorted({b for x in lst if x[1] == "PS" for b in range(x[2] // BANK, (x[3] - 1) // BANK + 1)})
+
+    plan = []
+    busy = {q: [] for q in queue}
+    held = {b: [] for b in range(8)}
+    pe_last = {b: 0.0 for b in range(8)}
+    seen = {}
+    dfree = [0.0]
+
+    def ready_at(q, outs, ins):
+        t = 0.0
+        for x in ins:
+            for y in seen.get(x[1], []):
+                if y[2] and y[0] < x[3] and x[2] < y[1]:
+                    t = max(t, y[4] + LAT)
+        for x in outs:
+            for y in seen.get(x[1], []):
+                if y[0] < x[3] and x[2] < y[1]:
+                    t = max(t, y[4] + (0.0 if y[3] == q == "p" else LAT))
+        if q == "p":
+            for b in banks_of(outs):
+                t = max(t, pe_last[b])
+        return t
+
+    def gap(q, t, dur):
+        lst = busy[q]
+        lo, hi = 0, len(lst)
+        while lo < hi:
+            mid = (lo + hi) // 2
+            if lst[mid][1] <= t:
+                lo = mid + 1
+            else:
+                hi = mid
+        while lo < len(lst):
+            if lst[lo][0] - t >= dur:
+                return t, lst[lo][0], lo
+            t = max(t, lst[lo][1])
+            lo += 1
+        return t, 1e12, lo
+
+    def place(q, dur, outs, ins, done=None):
+        t = ready_at(q, outs, ins)
+        bs = banks_of(outs + ins)
+        while True:
+            t, _, k = gap(q, t, dur)
+            hit = [y[1] + LAT for b in bs for y in held[b][-160:] if y[2] != q and y[0] - LAT < t + dur and t < y[1] + LAT]
+            if not hit:
+                break
+            t = max(hit)
+        busy[q].insert(k, (t, t + dur))
+        for b in bs:
+            held[b].append((t, t + dur, q))
+            if q == "p":
+                pe_last[b] = t + dur
+        end = t + dur if done is None else done(t)
+        mark(q if done is None else q + "dma", outs, ins, end)
+        return t
+
+    def mark(q, outs, ins, end):
+        for lst, w in ((ins, False), (outs, True)):
+            for (_, name, c0, c1, st) in lst:
+                old = seen.get(name, [])
+                e = end
+                if w and st == 1:
+                    old = [y for y in old if not (c0 <= y[0] and y[1] <= c1)]
+                elif not w:
+                    e = max([end] + [y[4] for y in old if not y[2] and y[3] == q and c0 <= y[0] and y[1] <= c1])
+                    old = [y for y in old if y[2] or y[3] != q or not (c0 <= y[0] and y[1] <= c1)]
+                old.append((c0, c1, w, q, e))
+                seen[name] = old
+
+    def split(out, args, kw):
+        outs = regs(out)
+        ins = outs[1:]
+        for a in list(args) + list(kw.values()):
+            ins = ins + regs(a)
+        return outs[:1], ins
+
+    def cost(q, call, out, args):
+        wide = [a for a in [out] + list(args) if regs(a) and width(a) > 1]
+        n = max([width(a) for a in wide] + [1])
+        if q == "p":
+            return PEC * max(64, width(out)) * (4 if SCRATCH[args[0][1]][2] == F4 else 1)
+        if q == "g":
+            return 130 + 2 * CYC * n
+        if out[0] == "i":
+            return 50 + 3.5 * CYC * n
+        if args and regs(args[0]) and args[0][0] == "i":
+            return (65 if q == "s" else 50) + GAT * n
+        if q == "s":
+            return SFIX + CYC * max(64, n)
+        rate = 1.0
+        if call == "tensor_tensor":
+            rate = 1.0 if "PS" in (args[0][1], args[1][1]) else 2.0
+        elif call != "tensor_reduce" and all(SCRATCH[a[1]][2] in (BF, F2, U2) for a in wide):
+            rate = 0.5
+        return CYC * max(64, n * rate)
+
+    calls = {"memset": g.vector.memset, "tensor_scalar": g.vector.tensor_scalar, "tensor_tensor": g.vector.tensor_tensor,
+             "tensor_copy": g.vector.tensor_copy, "tensor_reduce": g.vector.tensor_reduce, "activation": g.scalar.activation,
+             "matmul": g.tensor.matmul, "iota": g.iota}
+
+    def E(q, call, out, *args, **kw):
+        EE(q, [(call, out, args, kw)])
+
+    def EE(q, group):
+        outs, ins, dur = [], [], []
+        for call, out, args, kw in group:
+            o, i = split(out, args, kw)
+            outs += o
+            ins += i
+            dur.append(cost(q, call, out, args))
+        t = place(q, sum(dur), outs, ins)
+        for (call, out, args, kw), d in zip(group, dur):
+            plan.append((t, len(plan), "c", q, call, out, args, kw))
+            t += d
+
+    def dma(q, sem, out_ap, in_ap, outs, ins, nbytes):
+        def done(t):
+            dfree[0] = max(dfree[0], t + DLAT) + nbytes / DRATE
+            return dfree[0]
+        t = place(q, 50.0, outs, ins, done)
+        plan.append((t, len(plan), "d", q, sem, out_ap, in_ap, outs, ins))
+
+    def send(dst, out_ap, in_reg, sem, use):
+        t = place("g", 500.0, [], [in_reg])
+        plan.append((t, len(plan), "r", dst, out_ap, in_reg, sem, use))
+        return t
+
+    def spread(q, make, c0, c1):
+        while c0 < c1:
+            call, out, args, kw = make(c0, c1)
+            o, i = split(out, args, kw)
+            t = ready_at(q, o, i)
+            t, e, _ = gap(q, t, 66 + GAT * min(MINP, c1 - c0))
+            n = min(c1 - c0, int((e - t - 66) / GAT) // 32 * 32)
+            if 0 < c1 - c0 - n < 96:
+                n = max(32, n - 96)
+            EE(q, [make(c0, c0 + n)])
+            c0 += n
+
+    def ts(out, a, s1, s2, o0, o1=None):
+        if o1 is None:
+            E("v", "tensor_scalar", out, a, s1, None, o0)
+        else:
+            E("v", "tensor_scalar", out, a, s1, s2, o0, o1)
+
+    def tt(out, a, b, o):
+        E("v", "tensor_tensor", out, a, b, o)
+
+    def cp(out, a):
+        E("v", "tensor_copy", out, a)
+
+    def red(out, a):
+        E("v", "tensor_reduce", out, a, AxisListType.X, OP.min)
+
+    def act(out, a, f, **kw):
+        E("s", "activation", out, a, f, **kw)
+
+    def lin(q, out, a, scale, bias):
+        if q == "s":
+            act(out, a, COPY, scale=scale, bias=bias)
+        else:
+            ts(out, a, scale, bias, OP.mult, OP.add)
+
+    def conv(out, a):
+        if ENG["cv"] == "s":
+            act(out, a, COPY)
+        else:
+            cp(out, a)
+
+    def mm(out, lhsT, rhs, start, stop):
+        E("p", "matmul", out, lhsT, rhs, start, stop)
+
+    def fill(out, v):
+        E("v", "memset", out, v)
+
+    def ps(b, c0, c1):
+        return r("PS", b * BANK + c0, b * BANK + c1)
+
+    def cf(k):
+        return r("CF", k, k + 1)
+
+    def col(k):
+        return r("COL", k, k + 1)
+
+    def eye(name):
+        return r(name, 0, 128)
+
+    def wsum(c, z, buf, c0, n, start, stop):
+        for j in (0, 8):
+            EE("p", [("matmul", r("PS", c, c + n // 16), (r(z, 15 - i, 143 - i), r(buf, c0 + i, c0 + n, 16), start and i == 0, stop and i == 15), {})
+                     for i in range(j, j + 8)])
+
+    RAW, SPK, VS, UP = [[BANK * h + HC * k for h in (0, 1)] for k in range(4)]
+    K0 = (2 * BANK, 3 * BANK + 128)
+    PIX0 = 2 * BANK + 384
+    KU = (4 * BANK, 5 * BANK + 128)
+    KEY = 4 * BANK + 384
+    K2, YSUM = ps(4, 0, 256), ps(5, 128, 384)
+    s1, s2, s3, s4, s5 = RAW[0], RAW[1], SPK[0], SPK[1], K0[0]
+
+    for i in range(4):
+        c = r("XB0", 1024 * i, 1024 * i + 1024)
+        dma("y", "x%d" % i, ap(c), T.x[:, 1024 * i:1024 * i + 1024], [c], [], 262144)
+    dma("s", "wt", T.WT[:], T.wt[:], [r("WT", 0, 1)], [], 0)
+    dma("s", "km", T.KM[:], T.km[:], [r("KM", 0, 12)], [], 0)
+    TP = P // NT1
+    for i in range(NT1):
+        c = r("TMB", TP * i, TP * i + TP)
+        dma("y", "tm%d" % i, ap(c), T.tm[:, TP * i:TP * i + TP], [c], [], 256 * TP)
+    dma("y", "sa", T.SG1[:], T.x[15:128:16, 0:P], [r("SG1", 0, 256)], [], 65536)
+    dma("y", "xf", T.XB0[:, FO:FO + P], T.x[:], [r("XB0", FO, FO + P)], [], 1048576)
+    E("g", "iota", r("PIX", 0, 1), [[0, 1]], 0, 1)
+    E("g", "iota", r("ROW", 0, 144), [[1, 144]], 0, 0, allow_small_or_imprecise_dtypes=True)
+    E("g", "iota", r("ROWI", 0, 128), [[1, 128]], 0, 0)
+    E("g", "iota", r("NB", 0, 256), [[16, 256]], 0, 0, allow_small_or_imprecise_dtypes=True)
+    IF, PF, FM, SM, GF, WTF, G15, HS, FM2, I0, PADC, B2 = [col(k) for k in range(12)]
+    Z0, ROWM = r("Z0", 0, 144), r("ROW", 0, 128)
+    fill(eye("ONE"), 1.0)
+    ts(eye("CA"), eye("ONE"), 4112.0, None, OP.mult)
+    for c in (128, 256):
+        ts(r("CA", c, c + 128), eye("ONE"), 0.0, None, OP.mult)
+    fill(eye("C16"), 16.0)
+    ts(r("II", 0, 1), r("PIX", 0, 1), 15, None, OP.bitwise_and)
+    ts(r("GI", 0, 1), r("PIX", 0, 1), 4, None, OP.arith_shift_right)
+    cp(PF, r("PIX", 0, 1))
+    cp(IF, r("II", 0, 1))
+    cp(GF, r("GI", 0, 1))
+    cp(WTF, r("WT", 0, 1))
+    ts(G15, GF, 16.0, 15.0, OP.mult, OP.add)
+    ts(FM, IF, 14.5, None, OP.is_lt)
+    ts(SM, IF, 14.5, None, OP.is_gt)
+    ts(Z0, r("ROW", 0, 144), G15, None, OP.is_equal)
+    for k, c in enumerate((WTF, FM, SM)):
+        ts(r("W3", 8 * k, 8 * k + 8), r("ROW", 0, 8), GF, c, OP.is_equal, OP.mult)
+    ts(r("ROWG", 0, 128), eye("ROWI"), 4, None, OP.arith_shift_right)
+    ts(eye("GM"), r("ROWG", 0, 128), GF, None, OP.is_equal)
+    ts(r("ROWG", 0, 128), eye("ROWI"), 15, None, OP.bitwise_and)
+    ts(eye("C15"), r("ROWG", 0, 128), 14.5, None, OP.is_gt)
+    tt(eye("C15"), eye("C15"), eye("GM"), OP.mult)
+    ts(eye("IDF"), ROWM, PF, None, OP.is_equal)
+    tt(eye("GMN"), eye("C15"), eye("IDF"), OP.add)
+    ts(eye("BW"), eye("GMN"), FM, None, OP.mult)
+    cp(r("KMF", 0, 12), r("KM", 0, 12))
+    ts(r("KP", 0, 12), r("KMF", 0, 12), 128.0, None, OP.add)
+    for name, v in (("IB", 1.0), ("IN", -1.0), ("IEQ", VOID * 16384.0), ("I16K", 16384.0)):
+        ts(eye(name), ROWM, PF, v, OP.is_equal, OP.mult)
+    ts(HS, FM, 0.5, None, OP.mult)
+    ts(r("NF", 0, 256), r("NB", 0, 256), IF, None, OP.add)
+    for h in (0, 1):
+        cp(r("PS", PIX0 + HC * h, PIX0 + HC * h + HC), r("NF", HC * h, HC * h + HC))
+    ts(col(12), FM, 49152.0, -16384.0, OP.mult, OP.add)
+    ts(r("ZD", 0, 144), Z0, col(12), None, OP.mult)
+    for m in range(3):
+        ts(col(13 + m), PF, 63.5, 262144.0 + 32.0 + 64.0 * m, OP.is_gt, OP.mult)
+        ts(eye("CK%d" % m), eye("ONE"), col(13 + m), -262144.0, OP.mult, OP.add)
+
+    asker = {j: T.cores[(rank - j) % N] for j in (1, 2, 3)}
+    lands = []
+    for j in (1, 2, 3):
+        n = len(lanes(T.cores[(rank + j) % N], core))
+        if j == 1:
+            for i in range(NT1):
+                lands.append((r("L1", TP * i, TP * i + TP), "rt1%d" % i, n))
+                mark("remote", [lands[-1][0]], [], ARR[1] - 6000.0 * (NT1 - 1 - i) / NT1)
+        else:
+            lands.append((r("L%d" % j, 0, P), "rt%d" % j, n))
+            mark("remote", [lands[-1][0]], [], ARR[j])
+        for (jj, t) in UPD:
+            if jj == j:
+                lands.append((r("RU%d%d" % (j, t), 0, 32), "ru%d%d" % (j, t), n))
+    for i in range(NT1):
+        send(asker[1], T.L1[:, TP * i:TP * i + TP], r("TMB", TP * i, TP * i + TP), "rt1%d" % i, lanes(core, asker[1]))
+    send(asker[2], T.L2[:], r("TMB", 0, P), "rt2", lanes(core, asker[2]))
+    send(relay(rank), T.L3[:], r("TMB", 0, P), "hand", lanes(core, relay(rank)))
+
+    def late_constants():
+        for name in ("TW1", "TW2", "XB0", "XB1"):
+            fill(r(name, P, P + 16), 0.0)
+        for j in (0, 1, 2):
+            fill(r("UP%d" % j, 0, 32), 0.0)
+        ts(col(16), WTF, 4.0, SM, OP.mult, OP.add)
+        ts(r("ZV", 0, 144), Z0, col(16), None, OP.mult)
+        ts(col(17), FM, 8192.0, -4096.0, OP.mult, OP.add)
+        ts(r("ZM", 0, 144), Z0, col(17), None, OP.mult)
+        ts(r("ZY", 0, 144), Z0, FM, -2048.0, OP.mult, OP.mult)
+        tt(eye("GMN"), eye("GMN"), eye("IDF"), OP.add)
+        ts(eye("BT"), eye("GMN"), FM, None, OP.mult)
+        ts(B2, SM, 2.0, None, OP.mult)
+        ts(eye("GMN"), eye("GM"), -1.0, None, OP.mult)
+        for name, v in (("IVD", VOID * 2048.0), ("I2K", 2048.0), ("IM4", -4.0), ("IBG", BIG)):
+            ts(eye(name), ROWM, PF, v, OP.is_equal, OP.mult)
+        ts(r("D16", 0, 16), r("ROW", 0, 16), IF, None, OP.is_equal)
+        ts(r("PN", 0, 256), r("NF", 0, 256), -2097152.0, None, OP.add)
+        fill(r("CV", 0, 256), 0.0078125)
+        fill(cf(24), 4095.0)
+        for (c0, c1, sy, st) in UNITS:
+            if c0 + sy < c1:
+                fill(r("CV", (c0 + sy) // 16, c1 // 16), -64.0)
+            if c0 + st < c1:
+                c = r("PN", (c0 + st) // 16, c1 // 16)
+                ts(c, c, 8192.0, None, OP.add)
+        ts(I0, IF, 0.5, None, OP.is_lt)
+        ts(PADC, IF, 0.5, 4096.0, OP.is_gt, OP.mult)
+        tt(PADC, PADC, IF, OP.add)
+        ts(FM2, FM, -1.0, 2.0, OP.mult, OP.add)
+
+    ring, built = [0], [0]
+    waiting = {}
+
+    def flush(k):
+        if k in waiting:
+            act(*waiting.pop(k), ACT.Abs, scale=HS)
+
+    def settle(x):
+        for j in [(ring[0] + 1) % 2, ring[0] % 2]:
+            if j in waiting and waiting[j][0][1] == x[1] and waiting[j][0][2] < x[3] and x[2] < waiting[j][0][3]:
+                flush(j)
+
+    def slot(n):
+        ring[0] += 1
+        flush(ring[0] % 2)
+        return ps(6 + ring[0] % 2, 0, n)
+
+    def pieces(c0, c1):
+        n = c1 - c0
+        k = -(-n // BANK)
+        cut = [c0 + min(n, -(-n * i // (32 * max(k, 1))) * 32) for i in range(k + 1)]
+        return list(zip(cut[:-1], cut[1:]))
+
+    def widen(dst, src, mat, bias, eng, c0, c1, until=None):
+        for c in range(c0, c1, BANK):
+            if until is not None:
+                t0 = max(ready_at("p", [ps(6 + (ring[0] + 1) % 2, 0, BANK)], [r(src, c, c + BANK)]) + 400.0, ready_at("s", [r(dst, c, c + BANK)], []))
+                if gap("s", t0, 530.0)[0] + 530.0 > until:
+                    return c
+            o = slot(BANK)
+            mm(o, eye(mat), r(src, c, c + BANK), True, True)
+            lin(eng[c // BANK], r(dst, c, c + BANK), o, 1.0, bias)
+        return c1
+
+    def sums_of(xb, h):
+        c = RAW[h]
+        mm(r("PS", c, c + 384), eye("ONE"), r("CA", 0, 384), True, False)
+        for j in (0, 8):
+            EE("p", [("matmul", r("PS", c + i, c + 384, 16), (r(xb, HALF * h + i, HALF * h + HALF, 16), r("W3", 0, 24), False, i == 15), {})
+                     for i in range(j, j + 8)])
+
+    def Wr(name, h, k=0):
+        return r(name, 256 * k, 256 * k + 256) if h == 2 else r(name, 256 * k + HC * h, 256 * k + HC * h + HC)
+
+    def pix(h):
+        return r("PS", PIX0 + HC * h, PIX0 + HC * h + HC)
+
+    for h in (0, 1):
+        sums_of("XB0", h)
+
+    for t in range(NR):
+        X, X2 = "XB%d" % (t % 2), "XB%d" % (1 - t % 2)
+        xwin = r(X, 0, P)
+        tj = 1 + t % 3
+        TB = "TW1" if tj == 1 else "TW2"
+
+        def lists(h, m):
+            raw, u = r("PS", RAW[h], RAW[h] + HC), r("PS", UP[h], UP[h] + HC)
+            if m == 0:
+                lin(ENG["n"], Wr("NN", h), raw, 1.0, 0.5)
+                tt(Wr("UC", h), raw, Wr("NN", h), OP.subtract)
+                mm(u, eye("ONE"), eye("C16"), True, False)
+                mm(u, Wr("UC", h), eye("IB"), False, True)
+                act(Wr("US", h), u, ACT.Square, bias=-2048.0)
+                ts(Wr("V1", h), Wr("US", h), 0.03125, -0.484375, OP.mult, OP.add)
+            k = r("PS", KU[h] + HC * m, KU[h] + HC * m + HC)
+            lin(ENG["kur" if m else "kur0"], k, u, r("KP", 3 * t + m, 3 * t + m + 1), 0.0)
+            tt(Wr("QR", h, m), k, Wr("V1", h), OP.add)
+            ts(Wr("QI", h, m), Wr("QR", h, m), 4095, None, OP.bitwise_and)
+            cp(Wr("QO", h, m), Wr("QI", h, m))
+
+        def own_sum(h):
+            lin(ENG["sp"], Wr("SPW", 2, h), r("PS", SPK[h], SPK[h] + 2 * HC), -1.0, 1.0)
+
+        def ad(h, m, c0, c1):
+            return r("AD", HALF * (3 * h + m) + c0, HALF * (3 * h + m) + c1)
+
+        def d_v(h, m):
+            oc = 256 * m + HC * h
+            s = SDT[3 * h + m]
+            for c0, c1 in ((1024, HALF), (s, 1024)) if m == 2 and s < 1024 else ((s, HALF),):
+                spread("v", lambda c0, c1: ("tensor_tensor", ad(h, m, c0, c1),
+                                            (ind(r("W", 0, P), r("QO", oc + c0 // 16, oc + c1 // 16)), r(X, HALF * h + c0, HALF * h + c1), OP.max), {}),
+                       c0, c1)
+
+        def d_s(h, m):
+            oc = 256 * m + HC * h
+            for c, e in pieces(0, SDT[3 * h + m]):
+                act(ad(h, m, c, e), ind(xwin, r("QO", oc + c // 16, oc + e // 16)), COPY)
+                o = slot(e - c)
+                mm(o, eye("IN"), r(X, HALF * h + c, HALF * h + e), True, False)
+                mm(o, eye("IB"), ad(h, m, c, e), False, True)
+                waiting[ring[0] % 2] = (ad(h, m, c, e), o)
+                flush(1 - ring[0] % 2)
+
+        def d_sum(h, m):
+            c, s = K0[h] + 128 * m, SDT[3 * h + m] // 16
+            o = r("PS", c, c + HC)
+            tt(Wr("EQ", h, m), pix(h), Wr("QI", h, m), OP.is_equal)
+            ts(Wr("QB", h, m), Wr("QO", h, m), -2048.0, None, OP.add)
+            settle(ad(h, m, 0, HALF))
+            mm(o, eye("ONE"), eye("CK%d" % m), True, False)
+            mm(o, eye("IEQ"), Wr("EQ", h, m), False, False)
+            if s < HC:
+                mm(r("PS", c + s, c + HC), Wr("SPW", 0, h), r("I16K", s, HC), False, False)
+            for k in (1, 0):
+                wsum(c + 64 * k, "ZD", "AD", HALF * (3 * h + m) + 1024 * k, 1024, False, False)
+            mm(o, eye("IB"), Wr("QB", h, m), False, True)
+            if m == 0:
+                lin(ENG["ka"], Wr("KA", h), o, 1.0, 0.0)
+            else:
+                tt(Wr("KB" if m == 1 else "KI", h), o, Wr("KA" if m == 1 else "KB", h), OP.min)
+            if m == 2:
+                ts(Wr("IQ", h), Wr("KI", h), 4095, None, OP.bitwise_and)
+                cp(Wr("QSO", h), Wr("IQ", h))
+
+        def e_head(h):
+            ts(Wr("KD", h), Wr("KI", h), 14, None, OP.arith_shift_right)
+            conv(Wr("KF", h), Wr("KD", h))
+            ts(Wr("VD", h), Wr("KF", h), VOID - 1024.0, None, OP.is_ge)
+            o = r("PS", KEY + HC * h, KEY + HC * h + HC)
+            mm(o, eye("IDF"), Wr("PN", h), True, False)
+            mm(o, eye("I2K"), Wr("KF", h), False, False)
+            mm(o, eye("IVD"), Wr("VD", h), False, False)
+
+        def y_s(k):
+            c0, c1, sy, st = UNITS[k]
+            if sy:
+                act(r("YB", c0, c0 + sy), ind(xwin, r("QSO", c0 // 16, (c0 + sy) // 16)), COPY)
+
+        def y_v(k):
+            c0, c1, sy, st = UNITS[k]
+            spread("v", lambda a, b: ("tensor_tensor", r("YB", a, b), (ind(xwin, r("QSO", a // 16, b // 16)), r(X, FO + a, FO + b), OP.add), {}), c0 + sy, c1)
+
+        def h_list(k):
+            c0, c1, sy, st = UNITS[k]
+            h, w0, w1, ws = c0 // HALF, c0 // 16, c1 // 16, (c0 + sy) // 16
+            c = VS[k % 2] + 64 * (k // 2) - w0
+            mm(r("PS", c + w0, c + w1), eye("ONE"), r("CV", w0, w1), True, False)
+            if ws < w1:
+                mm(r("PS", c + ws, c + w1), Wr("UC", h), r("IM4", ws - HC * h, w1 - HC * h), False, False)
+            if sy:
+                mm(r("PS", c + w0, c + ws), Wr("SPW", 1, h), r("IN", w0 - HC * h, ws - HC * h), False, False)
+            wsum(c + w0, "ZV", "YB", c0, c1 - c0, False, True)
+            cp(r("VI", w0, w1), r("PS", c + w0, c + w1))
+            ts(r("UA", w0, w1), r("VI", w0, w1), 2, 4095, OP.arith_shift_right, OP.bitwise_and)
+            c = UP[h] - HC * h
+            tt(r("UH", w0, w1), r("PS", c + w0, c + w1), r("UA", w0, w1), OP.mult)
+            ts(r("IH", w0, w1), r("UH", w0, w1), 4, 4095, OP.arith_shift_right, OP.bitwise_and)
+            cp(r("HO", w0, w1), r("IH", w0, w1))
+
+        def score_s(k):
+            c0, c1, sy, st = UNITS[k]
+            twin = r(TB, 0, P)
+            for c, e in pieces(c0, c0 + st):
+                act(r("ZB", c, e), ind(twin, r("HO", c // 16, e // 16)), COPY)
+                o = slot(e - c)
+                mm(o, eye("IB"), r("YB", c, e), True, False)
+                if c < c0 + sy:
+                    n = min(e, c0 + sy) - c
+                    mm(r("PS", o[2], o[2] + n), eye("IB"), r(X, c, c + n), False, False)
+                mm(o, eye("IN"), r("ZB", c, e), False, True)
+                waiting[ring[0] % 2] = (r("ZB", c, e), o)
+                flush(1 - ring[0] % 2)
+
+        def score_v(k):
+            c0, c1, sy, st = UNITS[k]
+            twin = r(TB, 0, P)
+            spread("v", lambda a, b: ("tensor_tensor", r("ZB", a, b), (ind(twin, r("HO", a // 16, b // 16)), r("YB", a, b), OP.max), {}), c0 + st, c1)
+
+        def y_sum(k):
+            c0, c1, sy, st = UNITS[k]
+            if c0 + st < c1:
+                wsum(KEY + (c0 + st) // 16, "ZY", "YB", c0 + st, c1 - c0 - st, False, False)
+
+        def e_sum(k):
+            c0, c1, sy, st = UNITS[k]
+            settle(r("ZB", c0, c1))
+            left[c0 // HALF] -= c1 - c0
+            wsum(KEY + c0 // 16, "ZM", "ZB", c0, c1 - c0, False, left[c0 // HALF] == 0)
+
+        def tables():
+            if t < 3:
+                widen(TB, "L%d" % (t + 1), "BT", B2, "s" * 8, built[0], P)
+            for (j, tu) in UPD:
+                if j == tj and tu < t:
+                    RU = "RU%d%d" % (j, tu)
+                    cp(r("OFF", 8 + 2 * tu, 9 + 2 * tu), r(RU, 16, 17))
+                    cp(ind(r(TB, 0, P + 16), r("OFF", 8 + 2 * tu, 9 + 2 * tu)), r(RU, 0, 16))
+
+        def kinds(h):
+            tt(Wr("CM", h), pix(h), Wr("IQ", h), OP.min)
+            act(Wr("CMC", h), Wr("CM", h), COPY, bias=-2048.0)
+            ts(Wr("INV", h), Wr("VI", h), 1, None, OP.bitwise_and)
+            conv(Wr("INVB", h), Wr("INV", h))
+
+        def flip():
+            ts(r("SG2", 0, 256), r("SG1", 0, 256), -1.0, 1.0, OP.mult, OP.add)
+            dma("y", "sb", T[X][15:128:16, FO:FO + P], T.SG2[:], [r(X, FO, FO + P)], [r("SG2", 0, 256)], 65536)
+
+        left = [HALF, HALF]
+        if t:
+            dma("y", "xf", T[X][:, FO:FO + P], ap(xwin), [r(X, FO, FO + P)], [xwin], 1048576)
+            dma("y", "sa", T.SG1[:], T[X][15:128:16, 0:P], [r("SG1", 0, 256)], [xwin], 65536)
+        steps = {"li": lists, "wi": lambda k: widen("W", X, "BW", SM, WENG, BANK * k, BANK * k + BANK), "sp": own_sum,
+                 "ds": d_s, "dv": d_v, "su": d_sum, "ys": y_s, "yv": y_v, "hh": h_list, "eh": e_head, "ts": score_s, "tv": score_v,
+                 "zy": y_sum, "es": e_sum, "tw": tables, "ki": kinds, "fl": flip}
+        for k in (ORDER0 if t == 0 else ORDER):
+            if t == 0 and k == "su00":
+                late_constants()
+            steps[k[:2]](*[int(c) for c in k[2:]])
+        key = [r("PS", KEY + HC * h, KEY + HC * h + HC) for h in (0, 1)]
+        for h in (0, 1):
+            red(cf(h), key[h])
+            ts(r("R32", 16 * h, 16 * h + 16), r("D16", 0, 16), cf(h), None, OP.mult)
+
+        mm(r("PS", s1, s1 + 32), eye("GM"), r("R32", 0, 32), True, True)
+        kk = r("CI", 0, 1)
+        red(kk, r("PS", s1, s1 + 32))
+        red(cf(2), r("PS", s1, s1 + 32))
+        ts(r("CI", 1, 2), kk, 4, 255, OP.arith_shift_right, OP.bitwise_and)
+        ts(r("CI", 3, 4), kk, 4095, None, OP.bitwise_and)
+        cp(r("OFF", 0, 1), r("CI", 1, 2))
+        cp(cf(3), r("CI", 3, 4))
+        ts(cf(4), cf(0), cf(1), cf(2), OP.min, OP.is_equal)
+        iq = ind(r("IQ", 0, 256), r("OFF", 0, 1))
+        ts(r("GQ", 0, 16), iq, cf(3), cf(4), OP.min, OP.mult)
+        ts(r("GQ", 16, 32), iq, cf(3), cf(4), OP.max, OP.mult)
+        mm(r("PS", s2, s2 + 2), eye("GM"), r("GQ", 0, 32, 16), True, True)
+        for h in (0, 1):
+            act(Wr("KS", h), key[h], COPY)
+        mm(K2, eye("IBG"), Wr("INVB", 2), True, False)
+        for h in (0, 1):
+            mm(r("PS", K2[2] + HC * h, K2[2] + HC * h + HC), eye("IDF"), Wr("KS", h), False, False)
+        ts(Wr("M1", 2), Wr("CMC", 2), 2048.0, r("PS", s2, s2 + 1), OP.add, OP.is_le)
+        ts(Wr("M2", 2), Wr("CMC", 2), 2048.0, r("PS", s2 + 1, s2 + 2), OP.add, OP.is_ge)
+        mm(K2, eye("IBG"), Wr("M1", 2), False, False)
+        mm(K2, eye("IBG"), Wr("M2", 2), False, True)
+        red(cf(5), K2)
+        ts(r("R32", 0, 16), r("D16", 0, 16), cf(5), None, OP.mult)
+        mm(r("PS", s1, s1 + 16), eye("GM"), r("R32", 0, 16), True, True)
+        kk = r("CI", 4, 5)
+        red(kk, r("PS", s1, s1 + 16))
+        red(cf(10), r("PS", s1, s1 + 16))
+        ts(r("CI", 5, 6), kk, 4, 255, OP.arith_shift_right, OP.bitwise_and)
+        ts(r("CI", 7, 8), kk, 4095, None, OP.bitwise_and)
+        cp(r("OFF", 14, 15), r("CI", 5, 6))
+        cp(cf(11), r("CI", 7, 8))
+        ts(r("GQ", 32, 48), ind(r("INV", 0, 256), r("OFF", 0, 1)), cf(4), None, OP.mult)
+        ts(r("GQ", 48, 64), ind(r("IH", 0, 256), r("OFF", 0, 1)), cf(4), None, OP.mult)
+        mm(r("PS", s5, s5 + 2), eye("GM"), r("GQ", 32, 64, 16), True, True)
+        a, b, inv, hc = [r("PS", c, c + 1) for c in (s2, s2 + 1, s5, s5 + 1)]
+        dr, ba, nb = cf(12), cf(17), cf(19)
+        ts(ba, b, a, None, OP.subtract)
+        ts(cf(18), a, b, FO + 1.0, OP.add, OP.add)
+        ts(cf(20), b, -2.0, -1.0 - FO, OP.mult, OP.add)
+        ts(cf(28), cf(20), inv, ba, OP.mult, OP.add)
+        ts(cf(22), cf(18), inv, None, OP.mult)
+        mm(YSUM, eye("IDF"), Wr("NF", 2), True, False)
+        ts(Wr("Y0", 2), Wr("NF", 2), a, cf(28), OP.is_gt, OP.mult)
+        mm(YSUM, eye("IDF"), Wr("Y0", 2), False, False)
+        ts(Wr("Y1", 2), Wr("NF", 2), b, cf(22), OP.is_gt, OP.mult)
+        mm(YSUM, eye("IDF"), Wr("Y1", 2), False, True)
+        act(Wr("VA", 2), YSUM, ACT.Abs)
+        ts(dr, inv, -1.0, 1.0, OP.mult, OP.add)
+        ts(nb, b, -1.0, 4095.0, OP.mult, OP.add)
+        ts(cf(14), b, 1000000.0, None, OP.add)
+        ts(cf(13), cf(5), 16000000.0, dr, OP.is_lt, OP.mult)
+        ts(cf(21), nb, inv, b, OP.mult, OP.add)
+        ts(cf(15), cf(5), cf(10), cf(13), OP.is_equal, OP.mult)
+        ts(cf(16), cf(15), -1000000.0, cf(14), OP.mult, OP.add)
+        iq = ind(r("IQ", 0, 256), r("OFF", 14, 15))
+        ts(r("GQ", 64, 80), iq, cf(11), cf(16), OP.max, OP.is_gt)
+        ts(r("GQ", 80, 96), iq, cf(11), -4095.0, OP.max, OP.add)
+        ts(r("GQ", 96, 112), iq, cf(11), cf(21), OP.min, OP.subtract)
+        tt(r("GQ", 112, 116), r("GQ", 80, 84), r("GQ", 64, 68), OP.mult)
+        tt(r("GQ", 116, 118), r("GQ", 96, 98), r("GQ", 64, 66), OP.mult)
+        ts(cf(25), a, b, 4095.0, OP.subtract, OP.add)
+        ts(cf(26), nb, dr, a, OP.mult, OP.add)
+        ts(cf(27), nb, dr, None, OP.mult)
+        ts(cf(30), ba, dr, None, OP.mult)
+        mm(r("PS", s3, s3 + 4), eye("IDF"), r("CF", 24, 28), True, False)
+        mm(r("PS", s3, s3 + 4), eye("GM"), r("GQ", 112, 116), False, False)
+        mm(r("PS", s3 + 2, s3 + 4), eye("GMN"), r("GQ", 116, 118), False, True)
+        cp(r("OFF", 2, 5, 2), r("PS", s2, s2 + 2))
+        if t < 3:
+            ts(r("UP%d" % t, 16, 17), hc, I0, PADC, OP.mult, OP.add)
+        act(r("XA", 0, 16), ind(xwin, r("OFF", 2, 3)), COPY, scale=FM2)
+        act(r("XC", 0, 16), ind(xwin, r("OFF", 4, 5)), COPY, scale=FM)
+        ts(r("OFF", 6, 7), a, I0, PADC, OP.mult, OP.add)
+        tt(r("NI", 0, 16), r("XA", 0, 16), r("XC", 0, 16), OP.add)
+        ts(r("NJ", 0, 16), r("NI", 0, 16), 1, None, OP.arith_shift_right)
+        cp(ind(r(X, 0, P + 16), r("OFF", 6, 7)), r("NJ", 0, 16))
+
+        t4, t2, t3, L = [r("PS", s3 + k, s3 + k + 1) for k in range(4)]
+        for h in (0, 1):
+            o = [r("PS", K0[h] + HC * k, K0[h] + HC * k + HC) for k in range(3)]
+            ts(o[0], Wr("NF", h), t4, L, OP.is_gt, OP.mult)
+            ts(Wr("TB", h), Wr("NF", h), t2, L, OP.is_gt, OP.mult)
+            ts(o[1], Wr("NF", h), t3, cf(30), OP.is_gt, OP.mult)
+            tt(Wr("TA", h), o[0], Wr("TB", h), OP.subtract)
+            tt(o[2], Wr("VA", h), o[1], OP.subtract)
+            tt(Wr("TC", h), o[2], Wr("TA", h), OP.add)
+            cp(Wr("RO", h), Wr("TC", h))
+        if t < 3:
+            UPt = "UP%d" % t
+            cp(r("NJH", 0, 16), r("NJ", 0, 16))
+            mm(r("PS", s4, s4 + 16), eye("BT"), r("NJH", 0, 16), True, True)
+            ts(r(UPt, 0, 16), r("PS", s4, s4 + 16), B2, None, OP.add)
+            for (j, tu) in UPD:
+                if tu == t:
+                    at = send(asker[j], T["RU%d%d" % (j, t)][:], r(UPt, 0, 32), "ru%d%d" % (j, t), lanes(core, asker[j]))
+                    mark("remote", [r("RU%d%d" % (j, t), 0, 32)], [], at + 4000.0)
+        if t < 2:
+            built[0] = widen("TW2", "L%d" % (t + 2), "BT", B2, "s" * 8, 0, P, ready_at("s", [], [r("RO", 0, 64)]))
+        for n, (c0, c1, q) in enumerate(MOVE):
+            src = ind(r(X, 0, XW), r("RO", c0 // 16, c1 // 16))
+            if q == "s":
+                act(r(X2, c0, c1), src, COPY)
+            else:
+                cp(r(X2, c0, c1), src)
+            if t == 3:
+                dma("y", "y%d" % n, T.y[:, c0:c1], T[X2][:, c0:c1], [], [r(X2, c0, c1)], 256 * (c1 - c0))
+        if t < 3:
+            for h in (0, 1):
+                sums_of(X2, h)
+
+    STAT.append(max(b[-1][1] for b in busy.values() if b))
+    if DRY:
+        return
     total = {}
     clock = {q: {} for q in queue}
     rec = {}
@@ -75,12 +765,10 @@ def rank_program(g, core, T, topo):
             for x in rec.get(name, []):
                 if x[0] < c1 and c0 < x[1] and not (x[3] == q and q == "p"):
                     deps.append(x)
-        for (_, name, c0, c1, st) in list(outs) + list(ins):
-            if name == "PS":
-                for b in range(c0 // BANK, (c1 - 1) // BANK + 1):
-                    for q2, x in bank.get(b, {}).items():
-                        if q2 != q:
-                            deps.append(x)
+        for b in banks_of(list(outs) + list(ins)):
+            for q2, x in bank.get(b, {}).items():
+                if q2 != q:
+                    deps.append(x)
         ck = clock[q]
         deps.sort(key=lambda x: -x[6])
         todo = {}
@@ -106,539 +794,36 @@ def rank_program(g, core, T, topo):
                     old = [x for x in old if x[2] or x[3] != q or not (c0 <= x[0] and x[1] <= c1)]
                 old.append(new)
                 rec[name] = old
-                if name == "PS":
-                    for b in range(c0 // BANK, (c1 - 1) // BANK + 1):
-                        bank.setdefault(b, {})[q] = new
-
-    def ap(a):
-        if isinstance(a, tuple) and a and a[0] == "r":
-            return T[a[1]][:, a[2]:a[3]] if a[4] == 1 else T[a[1]][:, a[2]:a[3]:a[4]]
-        if isinstance(a, tuple) and a and a[0] == "i":
-            return ap(a[1]).indirect(ap(a[2]))
-        return a
-
-    def regs(a):
-        if isinstance(a, tuple) and a and a[0] == "r":
-            return [a]
-        if isinstance(a, tuple) and a and a[0] == "i":
-            return [a[1], a[2]]
-        return []
+                for b in banks_of([(_, name, c0, c1, st)]):
+                    bank.setdefault(b, {})[q] = new
 
     def bump(sem, n):
         total[sem] = total.get(sem, 0) + n
         return (sem, total[sem])
 
-    def E(q, call, out, *args, **kw):
-        outs = regs(out)
-        ins = outs[1:]
-        outs = outs[:1]
-        for a in list(args) + list(kw.values()):
-            ins = ins + regs(a)
-        need(q, outs, ins)
-        tok = bump(own[q], 1)
-        call(ap(out), *[ap(a) for a in args], **{k: ap(v) for k, v in kw.items()}).then_inc(T.sem[tok[0]], 1)
-        note(q, clock[q], outs, ins, tok)
-
-    def dma(q, sem, out_ap, in_ap, outs, ins):
-        need(q, outs, ins)
-        tok = bump(sem, 16)
-        queue[q].dma_start(out_ap, in_ap).then_inc(T.sem[sem], 16)
-        note(q + "dma", clock[q], outs, ins, tok)
-
-    def arrival(outs, tok):
-        note("remote", {}, outs, [], tok)
-
-    def ts(out, a, s1, s2, o0, o1=None):
-        if o1 is None:
-            E("v", g.vector.tensor_scalar, out, a, s1, None, o0)
+    for reg, sem, n in lands:
+        note("remote", {}, [reg], [], bump(sem, n))
+    for x in sorted(plan, key=lambda x: x[:2]):
+        if x[2] == "c":
+            q, call, out, args, kw = x[3:]
+            outs, ins = split(out, args, kw)
+            need(q, outs, ins)
+            tok = bump(own[q], 1)
+            calls[call](ap(out), *[ap(a) for a in args], **{k: ap(v) for k, v in kw.items()}).then_inc(T.sem[tok[0]], 1)
+            note(q, clock[q], outs, ins, tok)
+        elif x[2] == "d":
+            q, sem, out_ap, in_ap, outs, ins = x[3:]
+            need(q, outs, ins)
+            tok = bump(sem, 16)
+            queue[q].dma_start(out_ap, in_ap).then_inc(T.sem[sem], 16)
+            note(q + "dma", clock[q], outs, ins, tok)
         else:
-            E("v", g.vector.tensor_scalar, out, a, s1, s2, o0, o1)
+            dst, out_ap, in_reg, sem, use = x[3:]
+            need("g", [], [in_reg])
+            rid, pid, _ = topo.addr(dst)
+            g.remote_dma(out_ap, ap(in_reg), T.sem[sem], T.sem["ls"], pid, rid, sum(1 << e for e in use))
+            bump("ls", len(use))
 
-    def tt(out, a, b, o):
-        E("v", g.vector.tensor_tensor, out, a, b, o)
-
-    def cp(out, a):
-        E("v", g.vector.tensor_copy, out, a)
-
-    def red(out, a):
-        E("v", g.vector.tensor_reduce, out, a, AxisListType.X, OP.min)
-
-    def act(out, a, f, **kw):
-        E("s", g.scalar.activation, out, a, f, **kw)
-
-    def mm(out, lhsT, rhs, start, stop):
-        E("p", g.tensor.matmul, out, lhsT, rhs, start, stop)
-
-    def ps(b, c0, c1):
-        return r("PS", b * BANK + c0, b * BANK + c1)
-
-    def cf(k):
-        return r("CF", k, k + 1)
-
-    def wsum(col, z, buf, c0, n, start, stop):
-        for i in range(16):
-            mm(r("PS", col, col + n // 16), r(z, 15 - i, 143 - i), r(buf, c0 + i, c0 + n, 16), start and i == 0, stop and i == 15)
-
-    U0, UQ0, SG0, PIX0 = (0, BANK + 128), (128, BANK + 256), 384, 2 * BANK + 384
-    K0 = (2 * BANK, 3 * BANK + 128)
-    KU0, KEY = 4 * BANK, 4 * BANK + 384
-    SMALL1, SMALL2 = 256, BANK + 384
-    CLAMP, YSUM = ps(7, 0, 256), ps(6, 256, 512)
-    PIXW = r("PS", PIX0, PIX0 + 256)
-
-    dma("s", "wt", T.WT[:], T.wt[:], [r("WT", 0, 1)], [])
-    dma("s", "km", T.KM[:], T.km[:], [r("KM", 0, 12)], [])
-    for i in range(4):
-        c = r("XB0", 1024 * i, 1024 * i + 1024)
-        dma("y", "x%d" % i, ap(c), T.x[:, 1024 * i:1024 * i + 1024], [c], [])
-    for i in range(2):
-        c = r("TMB", 2048 * i, 2048 * i + 2048)
-        dma("s", "tm%d" % i, ap(c), T.tm[:, 2048 * i:2048 * i + 2048], [c], [])
-    NXC = [HALF * h + min(SDT[3 * h:3 * h + 3] + SY[h:h + 1]) for h in (0, 1)]
-    for h in (0, 1):
-        c = r("NX", NXC[h], HALF * h + HALF)
-        dma("y", "nx%d" % h, ap(c), T.x[:, NXC[h]:HALF * h + HALF], [c], [])
-    E("g", g.iota, r("PIX", 0, 1), [[0, 1]], 0, 1)
-    E("g", g.iota, r("ROW", 0, 144), [[1, 144]], 0, 0, allow_small_or_imprecise_dtypes=True)
-    E("g", g.iota, r("NB", 0, 256), [[16, 256]], 0, 0, allow_small_or_imprecise_dtypes=True)
-    E("g", g.iota, r("ROWI", 0, 128), [[1, 128]], 0, 0)
-    for j in (1, 2, 3):
-        E("v", g.vector.memset, r("T%d" % j, P, P + 16), 0.0)
-    for j in (0, 1):
-        E("v", g.vector.memset, r("XB%d" % j, P, P + 16), 0.0)
-    for j in (0, 1, 2):
-        E("v", g.vector.memset, r("UP%d" % j, 0, 32), 0.0)
-    IF, PF, FM, INV15 = r("IF", 0, 1), r("PF", 0, 1), r("FM", 0, 1), r("SM", 0, 1)
-    Z0, ROWM = r("Z0", 0, 144), r("ROW", 0, 128)
-    ts(r("II", 0, 1), r("PIX", 0, 1), 15, None, OP.bitwise_and)
-    ts(r("GI", 0, 1), r("PIX", 0, 1), 4, None, OP.arith_shift_right)
-    cp(PF, r("PIX", 0, 1))
-    cp(IF, r("II", 0, 1))
-    cp(r("GF", 0, 1), r("GI", 0, 1))
-    cp(r("WTF", 0, 1), r("WT", 0, 1))
-    ts(r("G15", 0, 1), r("GF", 0, 1), 16.0, 15.0, OP.mult, OP.add)
-    ts(FM, IF, 14.5, None, OP.is_lt)
-    ts(INV15, IF, 14.5, None, OP.is_gt)
-    ts(Z0, r("ROW", 0, 144), r("G15", 0, 1), None, OP.is_equal)
-    ts(r("ZW", 0, 144), Z0, r("WTF", 0, 1), None, OP.mult)
-    cp(r("KMF", 0, 12), r("KM", 0, 12))
-    ts(r("NF", 0, 256), r("NB", 0, 256), IF, None, OP.add)
-    cp(PIXW, r("NF", 0, 256))
-    ts(r("IB", 0, 128), ROWM, PF, None, OP.is_equal)
-    ts(r("IN", 0, 128), ROWM, PF, -1.0, OP.is_equal, OP.mult)
-    ts(r("IEQ", 0, 128), ROWM, PF, VOID * 16384.0, OP.is_equal, OP.mult)
-    ts(r("IDF", 0, 128), ROWM, PF, None, OP.is_equal)
-    ts(r("ZD", 0, 144), Z0, FM, 16384.0, OP.mult, OP.mult)
-
-    sent = [0]
-
-    def send(dst, out_ap, in_reg, sem, use):
-        need("g", [], [in_reg])
-        rid, pid, _ = topo.addr(dst)
-        m = 0
-        for e in use:
-            m |= 1 << e
-        g.remote_dma(out_ap, ap(in_reg), T.sem[sem], T.sem["ls"], pid, rid, m)
-        sent[0] += len(use)
-
-    def lanes(src, dst):
-        e = topo.engines(src, dst)
-        if topo.chip(src) != topo.chip(dst):
-            return e
-        far = [topo.engines(src, c) for c in T.cores if topo.chip(c) != topo.chip(src)]
-        rest = [k for k in e if not any(k in f for f in far)]
-        return rest if rest else e
-
-    asker = {j: T.cores[(rank - j) % N] for j in (1, 2, 3)}
-    for j in (1, 2, 3):
-        n = len(lanes(T.cores[(rank + j) % N], core))
-        bump("rt%d" % j, n * (2 if j == 1 else 1))
-        arrival([r("T%d" % j, 0, P)], ("rt%d" % j, total["rt%d" % j]))
-        for (jj, t) in UPD:
-            if jj == j:
-                arrival([r("RU%d%d" % (j, t), 0, 32)], bump("ru%d%d" % (j, t), n))
-    for i in range(2):
-        c = r("TMB", 2048 * i, 2048 * i + 2048)
-        act(c, c, COPY, scale=2.0)
-        send(asker[1], T.T1[:, 2048 * i:2048 * i + 2048], c, "rt1", lanes(core, asker[1]))
-    send(asker[2], T.T2[:, 0:P], r("TMB", 0, P), "rt2", lanes(core, asker[2]))
-    send(asker[3], T.T3[:, 0:P], r("TMB", 0, P), "rt3", lanes(core, asker[3]))
-
-    def late_constants():
-        ts(r("D16", 0, 16), r("ROW", 0, 16), IF, None, OP.is_equal)
-        ts(r("ROWG", 0, 128), r("ROWI", 0, 128), 4, None, OP.arith_shift_right)
-        ts(r("ZE", 0, 144), Z0, FM, 2048.0, OP.mult, OP.mult)
-        ts(r("ZS", 0, 144), Z0, INV15, None, OP.mult)
-        ts(r("GM", 0, 128), r("ROWG", 0, 128), r("GF", 0, 1), None, OP.is_equal)
-        ts(r("IVD", 0, 128), ROWM, PF, VOID * 2048.0, OP.is_equal, OP.mult)
-        ts(r("I2K", 0, 128), ROWM, PF, 2048.0, OP.is_equal, OP.mult)
-        ts(r("PN", 0, 256), r("NF", 0, 256), -14680064.0, None, OP.add)
-        ts(r("I0", 0, 1), IF, 0.5, None, OP.is_lt)
-        ts(r("PADC", 0, 1), IF, 0.5, 4096.0, OP.is_gt, OP.mult)
-        tt(r("PADC", 0, 1), r("PADC", 0, 1), IF, OP.add)
-        ts(r("FM2", 0, 1), FM, -1.0, 2.0, OP.mult, OP.add)
-
-    def u_block(xb, b):
-        wsum(U0[b // 2] + (b % 2) * 64, "ZW", xb, 1024 * b, 1024, True, True)
-
-    def flip_copy(xb, first):
-        x0, full = r(xb, 0, P), r(xb, FO, FO + P)
-        dma("y", "sa", T.SG1[:], T[xb][15:128:16, 0:P], [r("SG1", 0, 256)], [x0])
-        dma("y", "xf", ap(full), T.x[:] if first else ap(x0), [full], [] if first else [x0])
-        ts(r("SG2", 0, 256), r("SG1", 0, 256), -1.0, 1.0, OP.mult, OP.add)
-        dma("y", "sb", T[xb][15:128:16, FO:FO + P], T.SG2[:], [full], [r("SG2", 0, 256)])
-
-    for b in range(4):
-        u_block("XB0", b)
-
-    ring = [0]
-
-    def pieces(n):
-        k = -(-n // BANK)
-        cut = [min(n, -(-n * i // (32 * k)) * 32) for i in range(k + 1)]
-        return list(zip(cut[:-1], cut[1:]))
-
-    def run(*chains):
-        chains = list(chains)
-        while chains:
-            chains = [c for c in chains if next(c, 0) is None]
-
-    for t in range(4):
-        X, X2 = "XB%d" % (t % 2), "XB%d" % (1 - t % 2)
-        xwin = r(X, 0, P)
-        tj = 1 + t % 3
-        TB = "T%d" % tj
-
-        def W(name, h, k=0):
-            return r(name, 256 * k, 256 * k + 256) if h == 2 else r(name, 256 * k + HC * h, 256 * k + HC * h + HC)
-
-        def kur(h, m):
-            return r("PS", KU0 + 256 * m + HC * h, KU0 + 256 * m + HC * h + HC)
-
-        def list_ops(h):
-            cp(W("UR", h), r("PS", U0[h], U0[h] + HC))
-            yield
-            ts(W("U", h), W("UR", h), 4095, None, OP.bitwise_and)
-            yield
-            tt(W("US", h), W("U", h), W("U", h), OP.mult)
-            ts(kur(h, 0), W("U", h), r("KMF", 3 * t, 3 * t + 1), None, OP.mult)
-            ts(W("V1", h), W("US", h), 5, None, OP.arith_shift_right)
-            yield
-            for _ in q_ops(h, 0):
-                yield
-
-        def q_ops(h, m):
-            if m:
-                ts(kur(h, m), W("U", h), r("KMF", 3 * t + m, 3 * t + m + 1), None, OP.mult)
-                yield
-            tt(W("QR", h, m), kur(h, m), W("V1", h), OP.add)
-            yield
-            ts(W("QI", h, m), W("QR", h, m), 4095, None, OP.bitwise_and)
-            yield
-            cp(W("QO", h, m), W("QI", h, m))
-
-        def q_more(m):
-            tt(W("EQ", 2, m), W("QI", 2, m), PIXW, OP.is_equal)
-            ts(W("QB", 2, m), W("QI", 2, m), 4096.0 * m - 16777216.0, None, OP.add)
-
-        def d_v(h, m):
-            oc, s = 256 * m + HC * h, SDT[3 * h + m]
-            tt(r("AD%d" % m, s, HALF), ind(xwin, r("QO", oc + s // 16, oc + HC)), r("NX", HALF * h + s, HALF * h + HALF), OP.subtract)
-
-        def d_s(h, m):
-            todo = []
-            for c, e in pieces(SDT[3 * h + m]):
-                k, n = ring[0] % 2, e - c
-                ring[0] += 1
-                oc = 256 * m + HC * h
-                act(r("XQ", 512 * k, 512 * k + n), ind(xwin, r("QO", oc + c // 16, oc + e // 16)), COPY)
-                mm(ps(6 + k, 0, n), r("IB", 0, 128), r("XQ", 512 * k, 512 * k + n), True, False)
-                mm(ps(6 + k, 0, n), r("IN", 0, 128), r(X, HALF * h + c, HALF * h + e), False, True)
-                todo.append((c, n, k))
-                if len(todo) > 1:
-                    d_abs(m, todo.pop(0))
-            return todo
-
-        def d_abs(m, job):
-            c, n, k = job
-            act(r("AD%d" % m, c, c + n), ps(6 + k, 0, n), ACT.Abs)
-
-        def d_vabs(h, m):
-            c = r("AD%d" % m, SDT[3 * h + m], HALF)
-            act(c, c, ACT.Abs)
-
-        def d_sum(h, m):
-            c = K0[h] + 128 * m
-            mm(r("PS", c, c + HC), r("IDF", 0, 128), W("QB", h, m), True, False)
-            mm(r("PS", c, c + HC), r("IEQ", 0, 128), W("EQ", h, m), False, False)
-            wsum(c, "ZD", "AD%d" % m, 0, HALF, False, True)
-
-        def choose(h):
-            c = K0[h]
-            cp(W("KA", h), r("PS", c, c + 128))
-            tt(W("KB", h), r("PS", c + 128, c + 256), W("KA", h), OP.min)
-            tt(W("KI", h), r("PS", c + 256, c + 384), W("KB", h), OP.min)
-            ts(W("IQ", h), W("KI", h), 4095, None, OP.bitwise_and)
-            cp(W("QSO", h), W("IQ", h))
-
-        def y_v(h, c0, c1):
-            c0, c1 = c0 + HALF * h, c1 + HALF * h
-            tt(r("YB", c0, c1), ind(xwin, r("QSO", c0 // 16, c1 // 16)), r("NX", c0, c1), OP.add)
-
-        def y_s(h):
-            c0 = HALF * h + SY[h]
-            act(r("YB", HALF * h, c0), ind(xwin, r("QSO", HC * h, c0 // 16)), COPY)
-
-        def u_sum(h):
-            wsum(UQ0[h], "ZW", "YB", HALF * h, HALF, True, True)
-
-        def s_sum(h):
-            wsum(SG0 + HC * h, "ZS", "YB", HALF * h, HALF, True, False)
-            wsum(SG0 + HC * h, "ZS", X, HALF * h, SY[h], False, True)
-
-        def h_ops(h):
-            s, c = SY[h] // 16, HC * h
-            cp(r("UQ", c, c + s), r("PS", UQ0[h], UQ0[h] + s))
-            tt(r("UQ", c + s, c + HC), r("PS", UQ0[h] + s, UQ0[h] + HC), r("U", c + s, c + HC), OP.subtract)
-            ts(W("UA", h), W("UQ", h), 4095, None, OP.bitwise_and)
-            tt(W("UH", h), W("UA", h), W("U", h), OP.mult)
-            ts(W("IH", h), W("UH", h), 4, 4095, OP.arith_shift_right, OP.bitwise_and)
-            cp(W("HO", h), W("IH", h))
-
-        def t_v(h, c0, c1):
-            c0, c1 = c0 + HALF * h, c1 + HALF * h
-            tt(r("ZB", c0, c1), ind(r(TB, 0, P), r("HO", c0 // 16, c1 // 16)), r("YB", c0, c1), OP.subtract)
-
-        def t_s(h):
-            todo = []
-            for c, e in pieces(SET[h]):
-                k, n = ring[0] % 2, e - c
-                ring[0] += 1
-                p0 = HALF * h + c
-                act(r("NA", 512 * k, 512 * k + n), ind(r(TB, 0, P), r("HO", p0 // 16, (p0 + n) // 16)), COPY, scale=-1.0)
-                mm(ps(6 + k, 0, n), r("IB", 0, 128), r("YB", p0, p0 + n), True, False)
-                if c < SY[h]:
-                    n1 = min(n, SY[h] - c)
-                    mm(ps(6 + k, 0, n1), r("IB", 0, 128), r(X, p0, p0 + n1), False, False)
-                mm(ps(6 + k, 0, n), r("IB", 0, 128), r("NA", 512 * k, 512 * k + n), False, True)
-                todo.append((p0, n, k))
-                if len(todo) > 1:
-                    t_abs(todo.pop(0))
-            return todo
-
-        def t_abs(job):
-            p0, n, k = job
-            act(r("ZB", p0, p0 + n), ps(6 + k, 0, n), ACT.Abs)
-
-        def t_vabs(h, c0, c1):
-            act(r("ZB", HALF * h + c0, HALF * h + c1), r("ZB", HALF * h + c0, HALF * h + c1), ACT.Abs)
-
-        def e_head(h):
-            w0, w1 = HC * h, HC * h + HC
-            o = r("PS", KEY + w0, KEY + w1)
-            mm(o, r("IDF", 0, 128), r("PN", w0, w1), True, False)
-            mm(o, r("I2K", 0, 128), r("KF", w0, w1), False, False)
-            mm(o, r("IVD", 0, 128), r("VD", w0, w1), False, False)
-
-        def e_sum(h, c0, c1):
-            wsum(KEY + HC * h + c0 // 16, "ZE", "ZB", HALF * h + c0, c1 - c0, False, c1 == HALF)
-
-        if t:
-            act(r("NX", NXC[0], HALF), r(X, NXC[0], HALF), COPY)
-            c = r("NX", NXC[1], P)
-            dma("y", "nx1", ap(c), T[X][:, NXC[1]:P], [c], [r(X, NXC[1], P)])
-        run(list_ops(0))
-        pend = None
-        for n, (h, m) in enumerate([(h, m) for h in (0, 1) for m in (0, 1, 2)]):
-            left = d_s(h, m)
-            if pend is not None:
-                d_vabs(*pend)
-            for job in left:
-                d_abs(m, job)
-            if n == 1:
-                q_more(0)
-                q_more(1)
-            elif n == 2:
-                q_more(2)
-            if pend is not None:
-                d_sum(*pend)
-            pend = (h, m)
-            if n == 0:
-                d_v(0, 0)
-                run(list_ops(1), q_ops(0, 1))
-                d_v(0, 1)
-                run(q_ops(0, 2), q_ops(1, 1), q_ops(1, 2))
-            elif n == 1:
-                d_v(0, 2)
-            elif n == 2:
-                if t == 0:
-                    late_constants()
-            else:
-                d_v(h, m)
-                if n == 3:
-                    flip_copy(X, t == 0)
-                if n == 4:
-                    choose(0)
-        d_vabs(1, 2)
-        d_sum(1, 2)
-        y_s(0)
-        y_v(0, SY[0], HALF)
-        u_sum(0)
-        s_sum(0)
-        choose(1)
-        y_s(1)
-        y_v(1, SY[1], YC)
-        for (j, tu) in UPD:
-            if j == tj and tu < t:
-                RU = "RU%d%d" % (j, tu)
-                cp(r("OFF", 8 + 2 * tu, 9 + 2 * tu), r(RU, 16, 17))
-                cp(ind(r(TB, 0, P + 16), r("OFF", 8 + 2 * tu, 9 + 2 * tu)), r(RU, 0, 16))
-        h_ops(0)
-        y_v(1, YC, HALF)
-        mid = (SET[0] + HALF) // 2 // 32 * 32
-        left = t_s(0)
-        u_sum(1)
-        ts(W("KD", 2), W("KI", 2), 14, None, OP.arith_shift_right)
-        t_v(0, SET[0], mid)
-        cp(W("KF", 2), W("KD", 2))
-        ts(W("VD", 2), W("KD", 2), VOID - 1024.0, None, OP.is_ge)
-        e_head(0)
-        e_head(1)
-        h_ops(1)
-        t_v(0, mid, HALF)
-        s_sum(1)
-        for job in left:
-            t_abs(job)
-        t_vabs(0, SET[0], mid)
-        left = t_s(1)
-        t_vabs(0, mid, HALF)
-        e_sum(0, 0, HALF)
-        for job in left:
-            t_abs(job)
-        cuts = [SET[1], CUT[0], CUT[1], HALF]
-        for c0, c1 in zip(cuts[:-1], cuts[1:]):
-            t_v(1, c0, c1)
-            t_vabs(1, c0, c1)
-        e_sum(1, 0, CUT[0])
-        e_sum(1, CUT[0], HALF)
-        red(cf(0), r("PS", KEY, KEY + HC))
-        ts(r("R32", 0, 16), r("D16", 0, 16), cf(0), None, OP.mult)
-        tt(ps(2, 0, 256), W("IQ", 2), PIXW, OP.min)
-        ts(W("DIRT", 2), r("PS", SG0, SG0 + 256), 1.0, None, OP.not_equal)
-        tt(W("CC", 2), ps(2, 0, 256), W("DIRT", 2), OP.mult)
-        red(cf(1), r("PS", KEY + HC, KEY + 2 * HC))
-        ts(r("R32", 16, 32), r("D16", 0, 16), cf(1), None, OP.mult)
-
-        s1, s2 = SMALL1, SMALL2
-        mm(r("PS", s1, s1 + 32), r("GM", 0, 128), r("R32", 0, 32), True, True)
-        kk = r("CI", 0, 1)
-        red(kk, r("PS", s1, s1 + 32))
-        ts(r("CI", 1, 2), kk, 4, 255, OP.arith_shift_right, OP.bitwise_and)
-        ts(r("CI", 2, 3), kk, 15, None, OP.bitwise_and)
-        cp(r("OFF", 0, 1), r("CI", 1, 2))
-        tt(cf(2), r("II", 0, 1), r("CI", 2, 3), OP.is_equal)
-        ts(r("CI", 3, 4), kk, 4095, None, OP.bitwise_and)
-        for n, w in enumerate(["IQ", "DIRT", "IH"]):
-            ts(r("GQ", 16 * n, 16 * n + 16), ind(r(w, 0, 256), r("OFF", 0, 1)), cf(2), None, OP.mult)
-        mm(r("PS", s2, s2 + 48), r("GM", 0, 128), r("GQ", 0, 48), True, True)
-        cp(cf(3), r("CI", 3, 4))
-        q1, dirc, hc = r("PS", s2, s2 + 1), r("PS", s2 + 16, s2 + 17), r("PS", s2 + 32, s2 + 33)
-        a, b = cf(6), cf(7)
-        ts(cf(4), q1, cf(3), 0.5, OP.min, OP.add)
-        ts(cf(5), q1, cf(3), -0.5, OP.max, OP.add)
-        ts(CLAMP, r("CC", 0, 256), cf(4), cf(5), OP.max, OP.min)
-        ts(a, q1, cf(3), None, OP.min)
-        ts(b, q1, cf(3), None, OP.max)
-        tt(r("NN", 0, 256), CLAMP, r("CC", 0, 256), OP.is_equal)
-        ts(r("OFF", 2, 3), q1, cf(3), None, OP.min)
-        ts(r("OFF", 4, 5), q1, cf(3), None, OP.max)
-        tt(r("K2", 0, 256), r("PS", KEY, KEY + 256), r("NN", 0, 256), OP.mult)
-        if t < 3:
-            ts(r("UP%d" % t, 16, 17), hc, r("I0", 0, 1), r("PADC", 0, 1), OP.mult, OP.add)
-        cp(cf(8), dirc)
-        mm(YSUM, r("IDF", 0, 128), r("NF", 0, 256), True, False)
-        red(cf(0), r("K2", 0, 256))
-        act(cf(9), cf(8), COPY, scale=-1.0, bias=1.0)
-        act(cf(10), a, COPY, bias=b)
-        act(cf(18), cf(9), COPY, scale=FO + 1.0)
-        act(cf(12), a, COPY, scale=-1.0, bias=b)
-        act(cf(11), cf(10), COPY, scale=cf(9), bias=cf(18))
-        act(cf(32), cf(12), COPY, scale=cf(8))
-        act(cf(19), cf(11), COPY, scale=-1.0)
-        act(cf(13), cf(12), COPY, scale=cf(8), bias=cf(19))
-        act(cf(20), cf(9), COPY, scale=4095.0)
-        act(cf(21), b, COPY, scale=cf(8), bias=cf(20))
-        act(cf(25), cf(32), COPY, scale=-1.0)
-        act(r("XA", 0, 16), ind(xwin, r("OFF", 2, 3)), COPY, scale=r("FM2", 0, 1))
-        act(r("XC", 0, 16), ind(xwin, r("OFF", 4, 5)), COPY, scale=FM)
-        ts(r("R32", 0, 16), r("D16", 0, 16), cf(0), None, OP.mult)
-        mm(r("PS", s1, s1 + 16), r("GM", 0, 128), r("R32", 0, 16), True, True)
-        ts(r("OFF", 6, 7), a, r("I0", 0, 1), r("PADC", 0, 1), OP.mult, OP.add)
-        kk = r("CI", 4, 5)
-        red(kk, r("PS", s1, s1 + 16))
-        ts(r("CI", 5, 6), kk, 4, 255, OP.arith_shift_right, OP.bitwise_and)
-        ts(r("CI", 6, 7), kk, 15, None, OP.bitwise_and)
-        cp(r("OFF", 0, 1), r("CI", 5, 6))
-        tt(cf(33), r("II", 0, 1), r("CI", 6, 7), OP.is_equal)
-        ts(r("CI", 7, 8), kk, 4095, None, OP.bitwise_and)
-        ts(r("GQ", 48, 64), ind(r("IQ", 0, 256), r("OFF", 0, 1)), cf(33), None, OP.mult)
-        mm(r("PS", s2, s2 + 16), r("GM", 0, 128), r("GQ", 48, 64), True, True)
-        ts(cf(15), kk, 0.0, cf(8), OP.is_lt, OP.mult)
-        ts(r("Y0", 0, 256), r("NF", 0, 256), a, cf(13), OP.is_gt, OP.mult)
-        mm(YSUM, r("IDF", 0, 128), r("Y0", 0, 256), False, False)
-        cp(cf(14), r("CI", 7, 8))
-        ts(cf(16), cf(15), -8192.0, 8192.0, OP.mult, OP.add)
-        tt(r("NI", 0, 16), r("XA", 0, 16), r("XC", 0, 16), OP.add)
-        tt(cf(17), cf(16), b, OP.add)
-        ts(r("Y1", 0, 256), r("NF", 0, 256), b, cf(11), OP.is_gt, OP.mult)
-        mm(YSUM, r("IDF", 0, 128), r("Y1", 0, 256), False, True)
-        act(r("VA", 0, 256), YSUM, ACT.Abs)
-        q2 = r("PS", s2, s2 + 1)
-        d, L = cf(27), cf(28)
-        ts(cf(22), q2, cf(14), cf(17), OP.max, OP.is_gt)
-        ts(cf(23), q2, cf(14), cf(21), OP.min, OP.subtract)
-        ts(cf(24), q2, cf(14), 4095.0, OP.max, OP.subtract)
-        ts(cf(26), cf(23), cf(22), cf(21), OP.mult, OP.add)
-        ts(d, cf(24), cf(22), 4095.0, OP.mult, OP.add)
-        ts(r("NJ", 0, 16), r("NI", 0, 16), 1, None, OP.arith_shift_right)
-        tt(L, d, cf(26), OP.subtract)
-        tt(cf(29), d, cf(12), OP.subtract)
-        cp(ind(r(X, 0, P + 16), r("OFF", 6, 7)), r("NJ", 0, 16))
-        tt(cf(31), L, a, OP.add)
-        ts(cf(30), L, -1.0, None, OP.mult)
-
-        o1, o2 = [[ps(4 + k, HC * h, HC * h + HC) for h in (0, 1)] for k in (0, 1)]
-        o3 = [r("PS", K0[h], K0[h] + HC) for h in (0, 1)]
-        both = (0, 1)
-        for h in both:
-            ts(o1[h], W("NF", h), d, L, OP.is_gt, OP.mult)
-            ts(W("TB", h), W("NF", h), cf(31), cf(25), OP.is_gt, OP.mult)
-        for h in both:
-            ts(o2[h], W("NF", h), cf(29), cf(30), OP.is_gt, OP.mult)
-            tt(W("TA", h), o1[h], W("TB", h), OP.add)
-        for h in both:
-            tt(o3[h], o2[h], W("TA", h), OP.add)
-        for h in both:
-            tt(W("TC", h), o3[h], W("VA", h), OP.add)
-        for h in both:
-            cp(W("RO", h), W("TC", h))
-        for n, (c0, c1, q) in enumerate(MOVE):
-            src = ind(r(X, 0, XW), r("RO", c0 // 16, c1 // 16))
-            if q == "s":
-                act(r(X2, c0, c1), src, COPY)
-            else:
-                cp(r(X2, c0, c1), src)
-            if t == 3:
-                dma("y", "y%d" % n, T.y[:, c0:c1], T[X2][:, c0:c1], [], [r(X2, c0, c1)])
-        if t < 3:
-            for bl in range(4):
-                u_block(X2, bl)
-            ts(r("UP%d" % t, 0, 16), r("NJ", 0, 16), 2.0, None, OP.mult)
-            for (j, tu) in UPD:
-                if tu == t:
-                    send(asker[j], T["RU%d%d" % (j, t)][:], r("UP%d" % t, 0, 32), "ru%d%d" % (j, t), lanes(core, asker[j]))
-
-    total["ls"] = sent[0]
     for sem, val in total.items():
         if clock["g"].get(sem, 0) < val:
             g.wait_ge(T.sem[sem], val)

@@ -6,16 +6,21 @@ XW = FO + P
 HALF = 2048
 HC = 128
 BANK = 512
-SDT = (768, 896, 736, 288, 0, 320)
-UNITS = ((0, 1024, 1024, 1024), (1024, 2048, 448, 1024), (2048, 3072, 0, 256), (3072, 4096, 32, 288))
-MOVE = ((0, 1024, "s"), (1024, 2048, "v"), (2048, 3072, "s"), (3072, 4096, "v"))
-WENG = "sssssvss"
-ENG = {"n": "s", "kur0": "v", "kur": "v", "ka": "v", "cv": "v", "sp": "s"}
-MINP = 256
-ORDER = ("wi5 li00 wi0 wi4 li01 wi3 li10 wi6 wi7 wi2 sp0 li12 li11 wi1 dv00 ds00 li02 ds01 su00 dv01 dv02 ds02 su01 ds10 sp1 su02 dv10 ds12 ys1 ys0 yv1 yv0 "
-         "hh0 tw ds11 dv11 su10 dv12 su11 su12 yv2 hh1 ts0 ts1 yv3 ys2 ys3 eh0 tv1 hh3 hh2 zy1 eh1 ki0 zy0 tv0 es0 tv2 fl zy2 es1 ts2 ts3 tv3 zy3 ki1 es2 es3").split()
-ORDER0 = ORDER
+SDT = (992, 640, 672, 800, 928, 480)
+UNITS = ((0, 1024, 384, 480), (1024, 2048, 928, 960), (2048, 3072, 288, 288), (3072, 4096, 480, 480))
+MOVE = ((0, 1152, "s"), (1152, 2048, "v"), (2048, 3200, "s"), (3200, 4096, "v"))
+WENG = "ssssssss"
+ENG = {"n": "v", "kur0": "v", "kur": "v", "ka": "s", "cv": "v", "sp": "s", "iq": "v"}
+MINP, FILLN = 256, 192
+LATE = ("yv0", "tv3", "mv", "yv1", "dv12", "tv0", "dv00")
+ORDER = ("wi3 uu0 li00 wi6 uu1 li10 li01 sp0 wi1 li11 li02 wi2 wi4 xf wi0 li12 wi7 eq0 eq2 sp1 wi5 ds00 eq1 ds02 dv00 ds01 dv01 su00 dv02 dv11 su01 dv10 su02 "
+         "ds10 ds11 ds12 dv12 su10 su11 yv0 su12 ys0 ys1 yv1 tw hh0 hh1 eh1 ts1 tv0 ys3 yv2 yv3 ys2 hh2 hh3 fl zy1 tv1 eh0 tv3 ts0 zy0 es1 ts2 tv2 ts3 es0 es2 es3 ki2").split()
+ORDER0 = ("uu0 wi1 uu1 li00 li10 wi0 wi2 wi5 wi7 li01 eq0 sp0 wi4 wi6 wi3 li11 ds00 li02 eq1 dv00 dv02 ds11 xf ds02 ds01 li12 su00 dv01 ds12 eq2 dv11 dv10 su01 "
+          "ds10 su02 dv12 sp1 su10 yv0 su11 ys1 ys0 su12 eh1 tw ys3 yv1 hh0 hh1 yv3 tv1 ys2 yv2 tv0 eh0 hh2 hh3 ts1 zy0 ts0 ts2 es1 tv3 ts3 tv2 zy1 es2 es0 es3 ki2 fl").split()
 VOID = 1920.0
+NUMBERS = (((0, 0, 0), (0, 0, 4095)), ((0, 0, 0), (1, -1, 4095)), ((0, 1, -4095), (1, -1, 4095)), ((0, 1, -4095), (0, -1, 4095)),
+           ((0, -2, -1 - FO), (-1, 1, 0)), ((1, 1, FO + 1), (0, 0, 0)), ((1, -1, 0), (-1, 1, 0)), ((0, -1, 4095), (0, 1, 0)),
+           ((0, 0, -1), (0, 0, 1)), ((0, 0, 0), (0, 1, 1000000)))
 BIG = 33554432.0
 
 BF, F2, F4, I4, U2 = "bfloat16", "float16", "float32", "int32", "uint16"
@@ -23,31 +28,33 @@ SCRATCH = {"PS": ("psum", [128, 4096], F4)}
 for _names, _w, _d in ((("XB0", "XB1"), XW, BF), (("TW1", "TW2"), P + 16, F4), (("W",), P, F4),
                        (("TMB", "L1", "L2", "L3", "YB"), P, BF), (("ZB",), P, F2), (("AD",), 3 * P, F2),
                        (("SG1", "SG2", "NN", "CV", "M1", "M2", "INVB"), 256, BF), (("EQ",), 768, BF), (("QB",), 768, F2),
-                       (("UC", "KF", "VD", "CMC"), 256, F2), (("SPW",), 512, F2), (("C16",), 128, BF), (("NJH",), 16, F2),
+                       (("UC", "KF", "VD", "CMC"), 256, F2), (("SPW",), 512, F2), (("C16",), 256, BF), (("NC",), 256, F2), (("NJH",), 16, F2),
                        (("KM",), 12, I4), (("WT", "PIX", "II", "GI"), 1, I4), (("KMF", "KP"), 12, F4),
                        (("COL",), 32, F4), (("ROW", "Z0"), 144, F4), (("ROWI", "ROWG"), 128, I4), (("NB", "NF", "PN"), 256, F4),
-                       (("GM", "GMN", "IDF", "C15"), 128, F4), (("D16",), 16, F4), (("ZD", "ZM", "ZY"), 144, BF), (("ZV",), 144, F2),
-                       (("IB", "IN", "IEQ", "IVD", "I2K", "I16K", "IM4", "IBG", "ONE", "BW", "BT", "CK0", "CK1", "CK2"), 128, BF), (("CA",), 384, F2), (("W3",), 24, BF),
-                       (("V1", "KI", "IQ", "IH", "KD", "VI", "UA", "UH", "INV"), 256, I4),
+                       (("GM", "GMN", "IDF", "C15"), 128, F4), (("D16",), 16, F4), (("ZM", "ZY"), 144, BF), (("ZV",), 144, F2),
+                       (("IB", "IN", "IEQ", "IVD", "I2K", "IM4", "IBG", "ONE", "BW", "BT", "CK0", "CK1", "CK2"), 128, BF), (("CA",), 384, F2), (("W3",), 24, BF), (("WD",), 8, BF), (("IS0", "IS1", "IS2", "IS3", "IS4", "IS5"), 128, BF),
+                       (("V1", "KI", "IH", "KD", "VI", "UA", "UH", "INV"), 256, I4),
                        (("QR", "QI"), 768, I4), (("QO",), 768, U2), (("QSO", "HO", "RO"), 256, U2),
-                       (("US", "KA", "KB", "KS", "CM", "Y0", "Y1", "VA", "TA", "TB", "TC"), 256, F4),
-                       (("CF",), 64, F4), (("CI",), 16, I4), (("OFF",), 16, U2), (("R32",), 32, F4), (("GQ",), 128, F4),
+                       (("IQ", "US", "KA", "KB", "KS", "CM", "Y0", "Y1", "VA", "TA", "TB", "TC"), 256, F4),
+                       (("CF",), 64, F4), (("CI",), 16, I4), (("OFF",), 16, U2), (("R32",), 32, F4), (("RA",), 64, F4), (("CO",), 96, F4), (("GQ",), 128, F4),
                        (("XA", "XC"), 16, F4), (("NI", "NJ"), 16, I4),
                        (("UP0", "UP1", "UP2", "RU10", "RU11", "RU12", "RU20", "RU30", "RU31"), 32, F4)):
     for _n in _names:
         SCRATCH[_n] = ("sbuf", [128, _w], _d)
 UPD = [(1, 0), (2, 0), (3, 0), (1, 1), (3, 1), (1, 2)]
-NT1 = 2
+LOADS = [("TMB", 0)] + [("XB0", i) for i in range(4)] + [("TMB", i) for i in (3, 1, 2)]
+HAND = 1
+NT1 = 4
 SEMAPHORES = (["cv", "cs", "cp", "cg", "km", "wt", "xf", "sa", "sb", "ls"] + ["x%d" % i for i in range(4)] + ["tm%d" % i for i in range(NT1)]
               + ["y%d" % i for i in range(len(MOVE))] + ["rt1%d" % i for i in range(NT1)]
-              + ["rt2", "rt3", "hand"] + ["ru%d%d" % u for u in UPD])
+              + ["rt2", "rt3", "hand"] + ["hd%d" % i for i in range(NT1)] + ["ru%d%d" % u for u in UPD])
 
-STAT, DRY, NR = [], False, 4
+STAT, DRY, NR, ENDS = [], False, 4, []
 OP = AluOpType
 ACT = ActivationFunctionType
 COPY = ACT.Identity
-CYC, GAT, PEC, LAT, SFIX, DLAT, DRATE = 0.83, 1.3, 0.55, 150.0, 100.0, 1800.0, 300.0
-ARR = {1: 22000.0, 2: 30000.0, 3: 45000.0}
+CYC, GAT, PEC, LAT, SFIX, VFIX, DLAT, DRATE = 0.83, 1.35, 0.47, 170.0, 110.0, 15.0, 1800.0, 240.0
+ARR = {1: (14000.0, 18000.0, 22000.0, 20000.0), 2: 32000.0, 3: 50000.0}
 
 
 def r(name, c0, c1, step=1):
@@ -56,6 +63,13 @@ def r(name, c0, c1, step=1):
 
 def ind(win, off):
     return ("i", win, off)
+
+
+def shares(k):
+    c0, c1, sy, st = UNITS[k]
+    if k % 2:
+        return (c1 - sy, c1), (c0, c1 - sy), (c1 - st, c1), (c0, c1 - st)
+    return (c0, c0 + sy), (c0 + sy, c1), (c0, c0 + st), (c0 + st, c1)
 
 
 def width(a):
@@ -74,19 +88,24 @@ def rank_program(g, core, T, topo):
         rest = [k for k in e if not any(k in f for f in far)]
         return rest if rest else e
 
-    def relay(k):
-        src, dst = T.cores[k], T.cores[(k - 3) % N]
+    def relay(k, j):
+        src, dst = T.cores[k], T.cores[(k - j) % N]
         return [c for c in topo.cores_of(src) if topo.die(c) == topo.die(src) and c not in T.cores and topo.may_write(c, dst)][0]
 
     if rank is None:
+        sent = 0
         for k in range(N):
-            if relay(k) == core:
-                dst = T.cores[(k - 3) % N]
-                rid, pid, _ = topo.addr(dst)
-                use = lanes(core, dst)
-                g.wait_ge(T.sem.hand, len(lanes(T.cores[k], core)))
-                g.remote_dma(T.L3[:], T.L3[:], T.sem.rt3, T.sem.ls, pid, rid, sum(1 << e for e in use))
-                g.wait_ge(T.sem.ls, len(use))
+            jobs = [(1, T.L1[:, P // NT1 * i:P // NT1 * (i + 1)], "hd%d" % i, "rt1%d" % i) for i in range(NT1 - HAND, NT1)] + [(3, T.L3[:], "hand", "rt3")]
+            for j, piece, came, went in jobs:
+                if relay(k, j) == core:
+                    dst = T.cores[(k - j) % N]
+                    rid, pid, _ = topo.addr(dst)
+                    use = lanes(core, dst)
+                    g.wait_ge(T.sem[came], len(lanes(T.cores[k], core)))
+                    g.remote_dma(piece, piece, T.sem[went], T.sem.ls, pid, rid, sum(1 << e for e in use))
+                    sent += len(use)
+        if sent:
+            g.wait_ge(T.sem.ls, sent)
         return
     queue = {"v": g.vector, "s": g.scalar, "p": g.tensor, "g": g, "y": g.sync}
     own = {"v": "cv", "s": "cs", "p": "cp", "g": "cg"}
@@ -114,6 +133,7 @@ def rank_program(g, core, T, topo):
     pe_last = {b: 0.0 for b in range(8)}
     seen = {}
     dfree = [0.0]
+    later, defer = [], [False]
 
     def ready_at(q, outs, ins):
         t = 0.0
@@ -202,7 +222,7 @@ def rank_program(g, core, T, topo):
             rate = 1.0 if "PS" in (args[0][1], args[1][1]) else 2.0
         elif call != "tensor_reduce" and all(SCRATCH[a[1]][2] in (BF, F2, U2) for a in wide):
             rate = 0.5
-        return CYC * max(64, n * rate)
+        return VFIX + CYC * max(64, n * rate)
 
     calls = {"memset": g.vector.memset, "tensor_scalar": g.vector.tensor_scalar, "tensor_tensor": g.vector.tensor_tensor,
              "tensor_copy": g.vector.tensor_copy, "tensor_reduce": g.vector.tensor_reduce, "activation": g.scalar.activation,
@@ -218,10 +238,27 @@ def rank_program(g, core, T, topo):
             outs += o
             ins += i
             dur.append(cost(q, call, out, args))
+        for job in list(later):
+            o = job[0](job[1], job[2])[1]
+            if job in later and any(x[1] == o[1] and x[2] < o[3] and o[2] < x[3] for x in outs + ins):
+                later.remove(job)
+                spread("v", *job, now=True)
         t = place(q, sum(dur), outs, ins)
         for (call, out, args, kw), d in zip(group, dur):
             plan.append((t, len(plan), "c", q, call, out, args, kw))
             t += d
+        if q == "v" and later and sum(dur) < 300 and gap("v", t, 1.0)[1] > 1e11:
+            job = later.pop(0)
+            call, out, args, kw = job[0](job[1], job[2])
+            if ready_at("v", *split(out, args, kw)) <= t + LAT:
+                n = job[2] - job[1] if job[2] - job[1] < FILLN + 96 else FILLN
+                keep = list(later)
+                del later[:]
+                EE("v", [job[0](job[1], job[1] + n)])
+                later.extend(keep)
+                job[1] += n
+            if job[1] < job[2]:
+                later.insert(0, job)
 
     def dma(q, sem, out_ap, in_ap, outs, ins, nbytes):
         def done(t):
@@ -235,7 +272,11 @@ def rank_program(g, core, T, topo):
         plan.append((t, len(plan), "r", dst, out_ap, in_reg, sem, use))
         return t
 
-    def spread(q, make, c0, c1):
+    def spread(q, make, c0, c1, now=False):
+        if defer[0] and not now:
+            if c0 < c1:
+                later.append([make, c0, c1])
+            return
         while c0 < c1:
             call, out, args, kw = make(c0, c1)
             o, i = split(out, args, kw)
@@ -246,6 +287,10 @@ def rank_program(g, core, T, topo):
                 n = max(32, n - 96)
             EE(q, [make(c0, c0 + n)])
             c0 += n
+
+    def settle_moves():
+        while later:
+            spread("v", *later.pop(0), now=True)
 
     def ts(out, a, s1, s2, o0, o1=None):
         if o1 is None:
@@ -300,25 +345,22 @@ def rank_program(g, core, T, topo):
             EE("p", [("matmul", r("PS", c, c + n // 16), (r(z, 15 - i, 143 - i), r(buf, c0 + i, c0 + n, 16), start and i == 0, stop and i == 15), {})
                      for i in range(j, j + 8)])
 
-    RAW, SPK, VS, UP = [[BANK * h + HC * k for h in (0, 1)] for k in range(4)]
+    RAW, SPK, VS = [[(BANK + HC) * h + HC * k for h in (0, 1)] for k in range(3)]
+    UP = (3 * HC, 4 * HC)
     K0 = (2 * BANK, 3 * BANK + 128)
     PIX0 = 2 * BANK + 384
-    KU = (4 * BANK, 5 * BANK + 128)
+    KU = 4 * BANK
     KEY = 4 * BANK + 384
     K2, YSUM = ps(4, 0, 256), ps(5, 128, 384)
     s1, s2, s3, s4, s5 = RAW[0], RAW[1], SPK[0], SPK[1], K0[0]
 
-    for i in range(4):
-        c = r("XB0", 1024 * i, 1024 * i + 1024)
-        dma("y", "x%d" % i, ap(c), T.x[:, 1024 * i:1024 * i + 1024], [c], [], 262144)
-    dma("s", "wt", T.WT[:], T.wt[:], [r("WT", 0, 1)], [], 0)
-    dma("s", "km", T.KM[:], T.km[:], [r("KM", 0, 12)], [], 0)
+    dma("s", "wt", T.WT[:], T.wt[:], [r("WT", 0, 1)], [], 60000)
+    dma("s", "km", T.KM[:], T.km[:], [r("KM", 0, 12)], [], 60000)
     TP = P // NT1
-    for i in range(NT1):
-        c = r("TMB", TP * i, TP * i + TP)
-        dma("y", "tm%d" % i, ap(c), T.tm[:, TP * i:TP * i + TP], [c], [], 256 * TP)
+    for name, i in LOADS:
+        c = r(name, TP * i, TP * i + TP)
+        dma("y", ("x%d" if name == "XB0" else "tm%d") % i, ap(c), (T.x if name == "XB0" else T.tm)[:, TP * i:TP * i + TP], [c], [], 256 * TP)
     dma("y", "sa", T.SG1[:], T.x[15:128:16, 0:P], [r("SG1", 0, 256)], [], 65536)
-    dma("y", "xf", T.XB0[:, FO:FO + P], T.x[:], [r("XB0", FO, FO + P)], [], 1048576)
     E("g", "iota", r("PIX", 0, 1), [[0, 1]], 0, 1)
     E("g", "iota", r("ROW", 0, 144), [[1, 144]], 0, 0, allow_small_or_imprecise_dtypes=True)
     E("g", "iota", r("ROWI", 0, 128), [[1, 128]], 0, 0)
@@ -329,7 +371,7 @@ def rank_program(g, core, T, topo):
     ts(eye("CA"), eye("ONE"), 4112.0, None, OP.mult)
     for c in (128, 256):
         ts(r("CA", c, c + 128), eye("ONE"), 0.0, None, OP.mult)
-    fill(eye("C16"), 16.0)
+    fill(r("C16", 0, 256), 16.0)
     ts(r("II", 0, 1), r("PIX", 0, 1), 15, None, OP.bitwise_and)
     ts(r("GI", 0, 1), r("PIX", 0, 1), 4, None, OP.arith_shift_right)
     cp(PF, r("PIX", 0, 1))
@@ -352,14 +394,17 @@ def rank_program(g, core, T, topo):
     ts(eye("BW"), eye("GMN"), FM, None, OP.mult)
     cp(r("KMF", 0, 12), r("KM", 0, 12))
     ts(r("KP", 0, 12), r("KMF", 0, 12), 128.0, None, OP.add)
-    for name, v in (("IB", 1.0), ("IN", -1.0), ("IEQ", VOID * 16384.0), ("I16K", 16384.0)):
+    for name, v in (("IB", 1.0), ("IN", -1.0), ("IEQ", VOID * 16384.0)):
         ts(eye(name), ROWM, PF, v, OP.is_equal, OP.mult)
     ts(HS, FM, 0.5, None, OP.mult)
     ts(r("NF", 0, 256), r("NB", 0, 256), IF, None, OP.add)
     for h in (0, 1):
         cp(r("PS", PIX0 + HC * h, PIX0 + HC * h + HC), r("NF", HC * h, HC * h + HC))
     ts(col(12), FM, 49152.0, -16384.0, OP.mult, OP.add)
-    ts(r("ZD", 0, 144), Z0, col(12), None, OP.mult)
+    ts(r("WD", 0, 8), r("ROW", 0, 8), GF, col(12), OP.is_equal, OP.mult)
+    for k in range(6):
+        ts(col(18 + k), PF, SDT[k] // 16 - 0.5, 16384.0, OP.is_gt, OP.mult)
+        ts(eye("IS%d" % k), eye("IB"), col(18 + k), None, OP.mult)
     for m in range(3):
         ts(col(13 + m), PF, 63.5, 262144.0 + 32.0 + 64.0 * m, OP.is_gt, OP.mult)
         ts(eye("CK%d" % m), eye("ONE"), col(13 + m), -262144.0, OP.mult, OP.add)
@@ -371,17 +416,19 @@ def rank_program(g, core, T, topo):
         if j == 1:
             for i in range(NT1):
                 lands.append((r("L1", TP * i, TP * i + TP), "rt1%d" % i, n))
-                mark("remote", [lands[-1][0]], [], ARR[1] - 6000.0 * (NT1 - 1 - i) / NT1)
+                mark("remote", [lands[-1][0]], [], ARR[1][i])
         else:
             lands.append((r("L%d" % j, 0, P), "rt%d" % j, n))
             mark("remote", [lands[-1][0]], [], ARR[j])
         for (jj, t) in UPD:
             if jj == j:
                 lands.append((r("RU%d%d" % (j, t), 0, 32), "ru%d%d" % (j, t), n))
-    for i in range(NT1):
-        send(asker[1], T.L1[:, TP * i:TP * i + TP], r("TMB", TP * i, TP * i + TP), "rt1%d" % i, lanes(core, asker[1]))
+    for i in [x[1] for x in LOADS if x[0] == "TMB"]:
+        via = i >= NT1 - HAND
+        dst = relay(rank, 1) if via else asker[1]
+        send(dst, T.L1[:, TP * i:TP * i + TP], r("TMB", TP * i, TP * i + TP), ("hd%d" if via else "rt1%d") % i, lanes(core, dst))
     send(asker[2], T.L2[:], r("TMB", 0, P), "rt2", lanes(core, asker[2]))
-    send(relay(rank), T.L3[:], r("TMB", 0, P), "hand", lanes(core, relay(rank)))
+    send(relay(rank, 3), T.L3[:], r("TMB", 0, P), "hand", lanes(core, relay(rank, 3)))
 
     def late_constants():
         for name in ("TW1", "TW2", "XB0", "XB1"):
@@ -402,13 +449,20 @@ def rank_program(g, core, T, topo):
         ts(r("D16", 0, 16), r("ROW", 0, 16), IF, None, OP.is_equal)
         ts(r("PN", 0, 256), r("NF", 0, 256), -2097152.0, None, OP.add)
         fill(r("CV", 0, 256), 0.0078125)
-        fill(cf(24), 4095.0)
-        for (c0, c1, sy, st) in UNITS:
-            if c0 + sy < c1:
-                fill(r("CV", (c0 + sy) // 16, c1 // 16), -64.0)
-            if c0 + st < c1:
-                c = r("PN", (c0 + st) // 16, c1 // 16)
-                ts(c, c, 8192.0, None, OP.add)
+        ts(Wr("NC", 2), Wr("NF", 2), -2048.0, None, OP.add)
+        fill(r("CO", 0, 96), 0.0)
+        for k, (x, y) in enumerate(NUMBERS):
+            for c, row in ((k, x), (16 + k, y)):
+                for j, v in enumerate(row):
+                    if v:
+                        E("g", "iota", r("CO", 32 * j + c, 32 * j + c + 1), [[0, 1]], v, 0, allow_small_or_imprecise_dtypes=True)
+        for k in (0, 2):
+            c0, c1 = shares(k)[1][0] // 16, shares(k + 1)[1][1] // 16
+            if c0 < c1:
+                fill(r("CV", c0, c1), -64.0)
+            c0, c1 = shares(k)[3][0] // 16, shares(k + 1)[3][1] // 16
+            if c0 < c1:
+                ts(r("PN", c0, c1), r("PN", c0, c1), 8192.0, None, OP.add)
         ts(I0, IF, 0.5, None, OP.is_lt)
         ts(PADC, IF, 0.5, 4096.0, OP.is_gt, OP.mult)
         tt(PADC, PADC, IF, OP.add)
@@ -459,10 +513,10 @@ def rank_program(g, core, T, topo):
         return r(name, 256 * k, 256 * k + 256) if h == 2 else r(name, 256 * k + HC * h, 256 * k + HC * h + HC)
 
     def pix(h):
-        return r("PS", PIX0 + HC * h, PIX0 + HC * h + HC)
+        return r("PS", PIX0 + HC * (h % 2), PIX0 + HC * min(h, 1) + HC)
 
-    for h in (0, 1):
-        sums_of("XB0", h)
+    for i in range(4):
+        cp(r("XB0", FO + 1024 * i, FO + 1024 * i + 1024), r("XB0", 1024 * i, 1024 * i + 1024))
 
     for t in range(NR):
         X, X2 = "XB%d" % (t % 2), "XB%d" % (1 - t % 2)
@@ -479,11 +533,15 @@ def rank_program(g, core, T, topo):
                 mm(u, Wr("UC", h), eye("IB"), False, True)
                 act(Wr("US", h), u, ACT.Square, bias=-2048.0)
                 ts(Wr("V1", h), Wr("US", h), 0.03125, -0.484375, OP.mult, OP.add)
-            k = r("PS", KU[h] + HC * m, KU[h] + HC * m + HC)
+            k = r("PS", KU + 256 * m + HC * h, KU + 256 * m + HC * h + HC)
             lin(ENG["kur" if m else "kur0"], k, u, r("KP", 3 * t + m, 3 * t + m + 1), 0.0)
             tt(Wr("QR", h, m), k, Wr("V1", h), OP.add)
             ts(Wr("QI", h, m), Wr("QR", h, m), 4095, None, OP.bitwise_and)
             cp(Wr("QO", h, m), Wr("QI", h, m))
+
+        def marks(m):
+            tt(Wr("EQ", 2, m), pix(2), Wr("QI", 2, m), OP.is_equal)
+            ts(Wr("QB", 2, m), Wr("QO", 2, m), -2048.0, None, OP.add)
 
         def own_sum(h):
             lin(ENG["sp"], Wr("SPW", 2, h), r("PS", SPK[h], SPK[h] + 2 * HC), -1.0, 1.0)
@@ -493,42 +551,43 @@ def rank_program(g, core, T, topo):
 
         def d_v(h, m):
             oc = 256 * m + HC * h
-            s = SDT[3 * h + m]
-            for c0, c1 in ((1024, HALF), (s, 1024)) if m == 2 and s < 1024 else ((s, HALF),):
-                spread("v", lambda c0, c1: ("tensor_tensor", ad(h, m, c0, c1),
-                                            (ind(r("W", 0, P), r("QO", oc + c0 // 16, oc + c1 // 16)), r(X, HALF * h + c0, HALF * h + c1), OP.max), {}),
-                       c0, c1)
+            spread("v", lambda c0, c1: ("tensor_tensor", ad(h, m, c0, c1),
+                                        (ind(r("W", 0, P), r("QO", oc + c0 // 16, oc + c1 // 16)), r(X, HALF * h + c0, HALF * h + c1), OP.max), {}),
+                   SDT[3 * h + m], HALF)
 
         def d_s(h, m):
             oc = 256 * m + HC * h
+            if SDT[3 * h + m]:
+                act(ad(h, m, 0, SDT[3 * h + m]), ind(xwin, r("QO", oc, oc + SDT[3 * h + m] // 16)), COPY)
             for c, e in pieces(0, SDT[3 * h + m]):
-                act(ad(h, m, c, e), ind(xwin, r("QO", oc + c // 16, oc + e // 16)), COPY)
                 o = slot(e - c)
                 mm(o, eye("IN"), r(X, HALF * h + c, HALF * h + e), True, False)
                 mm(o, eye("IB"), ad(h, m, c, e), False, True)
                 waiting[ring[0] % 2] = (ad(h, m, c, e), o)
-                flush(1 - ring[0] % 2)
 
         def d_sum(h, m):
             c, s = K0[h] + 128 * m, SDT[3 * h + m] // 16
             o = r("PS", c, c + HC)
-            tt(Wr("EQ", h, m), pix(h), Wr("QI", h, m), OP.is_equal)
-            ts(Wr("QB", h, m), Wr("QO", h, m), -2048.0, None, OP.add)
             settle(ad(h, m, 0, HALF))
             mm(o, eye("ONE"), eye("CK%d" % m), True, False)
-            mm(o, eye("IEQ"), Wr("EQ", h, m), False, False)
+            mm(o, Wr("EQ", h, m), eye("IEQ"), False, False)
             if s < HC:
-                mm(r("PS", c + s, c + HC), Wr("SPW", 0, h), r("I16K", s, HC), False, False)
-            for k in (1, 0):
-                wsum(c + 64 * k, "ZD", "AD", HALF * (3 * h + m) + 1024 * k, 1024, False, False)
-            mm(o, eye("IB"), Wr("QB", h, m), False, True)
+                mm(o, eye("IS%d" % (3 * h + m)), Wr("SPW", 0, h), False, False)
+            c0 = HALF * (3 * h + m)
+            for j in (0, 8):
+                EE("p", [("matmul", r("PS", c + i, c + HC, 16), (r("AD", c0 + i, c0 + HALF, 16), r("WD", 0, 8), False, False), {}) for i in range(j, j + 8)])
+            mm(o, Wr("QB", h, m), eye("IB"), False, True)
             if m == 0:
                 lin(ENG["ka"], Wr("KA", h), o, 1.0, 0.0)
             else:
                 tt(Wr("KB" if m == 1 else "KI", h), o, Wr("KA" if m == 1 else "KB", h), OP.min)
             if m == 2:
-                ts(Wr("IQ", h), Wr("KI", h), 4095, None, OP.bitwise_and)
-                cp(Wr("QSO", h), Wr("IQ", h))
+                o = r("PS", K0[h], K0[h] + HC)
+                ts(Wr("KD", h), Wr("KI", h), 4095, None, OP.bitwise_and)
+                ts(Wr("KF", h), Wr("KD", h), -2048.0, None, OP.add)
+                mm(o, Wr("KF", h), eye("IB"), True, True)
+                ts(Wr("QSO", h), o, 2048.0, None, OP.add)
+                lin(ENG["iq"], Wr("IQ", h), o, 1.0, 2048.0)
 
         def e_head(h):
             ts(Wr("KD", h), Wr("KI", h), 14, None, OP.arith_shift_right)
@@ -536,27 +595,25 @@ def rank_program(g, core, T, topo):
             ts(Wr("VD", h), Wr("KF", h), VOID - 1024.0, None, OP.is_ge)
             o = r("PS", KEY + HC * h, KEY + HC * h + HC)
             mm(o, eye("IDF"), Wr("PN", h), True, False)
-            mm(o, eye("I2K"), Wr("KF", h), False, False)
-            mm(o, eye("IVD"), Wr("VD", h), False, False)
+            mm(o, Wr("KF", h), eye("I2K"), False, False)
+            mm(o, Wr("VD", h), eye("IVD"), False, False)
 
         def y_s(k):
-            c0, c1, sy, st = UNITS[k]
-            if sy:
-                act(r("YB", c0, c0 + sy), ind(xwin, r("QSO", c0 // 16, (c0 + sy) // 16)), COPY)
+            a, b = shares(k)[0]
+            if a < b:
+                act(r("YB", a, b), ind(xwin, r("QSO", a // 16, b // 16)), COPY)
 
         def y_v(k):
-            c0, c1, sy, st = UNITS[k]
-            spread("v", lambda a, b: ("tensor_tensor", r("YB", a, b), (ind(xwin, r("QSO", a // 16, b // 16)), r(X, FO + a, FO + b), OP.add), {}), c0 + sy, c1)
+            spread("v", lambda a, b: ("tensor_tensor", r("YB", a, b), (ind(xwin, r("QSO", a // 16, b // 16)), r(X, FO + a, FO + b), OP.add), {}), *shares(k)[1])
 
         def h_list(k):
             c0, c1, sy, st = UNITS[k]
-            h, w0, w1, ws = c0 // HALF, c0 // 16, c1 // 16, (c0 + sy) // 16
+            h, w0, w1 = c0 // HALF, c0 // 16, c1 // 16
             c = VS[k % 2] + 64 * (k // 2) - w0
             mm(r("PS", c + w0, c + w1), eye("ONE"), r("CV", w0, w1), True, False)
-            if ws < w1:
-                mm(r("PS", c + ws, c + w1), Wr("UC", h), r("IM4", ws - HC * h, w1 - HC * h), False, False)
-            if sy:
-                mm(r("PS", c + w0, c + ws), Wr("SPW", 1, h), r("IN", w0 - HC * h, ws - HC * h), False, False)
+            for (a, b), src, mat in zip(shares(k)[:2], (Wr("SPW", 1, h), Wr("UC", h)), ("IN", "IM4")):
+                if a < b:
+                    mm(r("PS", c + a // 16, c + b // 16), src, r(mat, a // 16 - HC * h, b // 16 - HC * h), False, False)
             wsum(c + w0, "ZV", "YB", c0, c1 - c0, False, True)
             cp(r("VI", w0, w1), r("PS", c + w0, c + w1))
             ts(r("UA", w0, w1), r("VI", w0, w1), 2, 4095, OP.arith_shift_right, OP.bitwise_and)
@@ -566,28 +623,26 @@ def rank_program(g, core, T, topo):
             cp(r("HO", w0, w1), r("IH", w0, w1))
 
         def score_s(k):
-            c0, c1, sy, st = UNITS[k]
             twin = r(TB, 0, P)
-            for c, e in pieces(c0, c0 + st):
+            for c, e in pieces(*shares(k)[2]):
                 act(r("ZB", c, e), ind(twin, r("HO", c // 16, e // 16)), COPY)
                 o = slot(e - c)
                 mm(o, eye("IB"), r("YB", c, e), True, False)
-                if c < c0 + sy:
-                    n = min(e, c0 + sy) - c
-                    mm(r("PS", o[2], o[2] + n), eye("IB"), r(X, c, c + n), False, False)
+                a, b = max(c, shares(k)[0][0]), min(e, shares(k)[0][1])
+                if a < b:
+                    mm(r("PS", o[2] + a - c, o[2] + b - c), eye("IB"), r(X, a, b), False, False)
                 mm(o, eye("IN"), r("ZB", c, e), False, True)
                 waiting[ring[0] % 2] = (r("ZB", c, e), o)
                 flush(1 - ring[0] % 2)
 
         def score_v(k):
-            c0, c1, sy, st = UNITS[k]
             twin = r(TB, 0, P)
-            spread("v", lambda a, b: ("tensor_tensor", r("ZB", a, b), (ind(twin, r("HO", a // 16, b // 16)), r("YB", a, b), OP.max), {}), c0 + st, c1)
+            spread("v", lambda a, b: ("tensor_tensor", r("ZB", a, b), (ind(twin, r("HO", a // 16, b // 16)), r("YB", a, b), OP.max), {}), *shares(k)[3])
 
-        def y_sum(k):
-            c0, c1, sy, st = UNITS[k]
-            if c0 + st < c1:
-                wsum(KEY + (c0 + st) // 16, "ZY", "YB", c0 + st, c1 - c0 - st, False, False)
+        def y_sum(h):
+            c0, c1 = shares(2 * h)[3][0], shares(2 * h + 1)[3][1]
+            if c0 < c1:
+                wsum(KEY + c0 // 16, "ZY", "YB", c0, c1 - c0, False, False)
 
         def e_sum(k):
             c0, c1, sy, st = UNITS[k]
@@ -615,16 +670,22 @@ def rank_program(g, core, T, topo):
             dma("y", "sb", T[X][15:128:16, FO:FO + P], T.SG2[:], [r(X, FO, FO + P)], [r("SG2", 0, 256)], 65536)
 
         left = [HALF, HALF]
-        if t:
-            dma("y", "xf", T[X][:, FO:FO + P], ap(xwin), [r(X, FO, FO + P)], [xwin], 1048576)
-            dma("y", "sa", T.SG1[:], T[X][15:128:16, 0:P], [r("SG1", 0, 256)], [xwin], 65536)
-        steps = {"li": lists, "wi": lambda k: widen("W", X, "BW", SM, WENG, BANK * k, BANK * k + BANK), "sp": own_sum,
+
+        def second():
+            if t:
+                settle_moves()
+                dma("y", "xf", T[X][:, FO:FO + P], ap(xwin), [r(X, FO, FO + P)], [xwin], 1048576)
+                dma("y", "sa", T.SG1[:], T[X][15:128:16, 0:P], [r("SG1", 0, 256)], [xwin], 65536)
+
+        steps = {"uu": lambda h: sums_of(X, h), "xf": second, "li": lists, "eq": marks, "wi": lambda k: widen("W", X, "BW", SM, WENG, BANK * k, BANK * k + BANK), "sp": own_sum,
                  "ds": d_s, "dv": d_v, "su": d_sum, "ys": y_s, "yv": y_v, "hh": h_list, "eh": e_head, "ts": score_s, "tv": score_v,
                  "zy": y_sum, "es": e_sum, "tw": tables, "ki": kinds, "fl": flip}
         for k in (ORDER0 if t == 0 else ORDER):
             if t == 0 and k == "su00":
                 late_constants()
+            defer[0] = k in LATE
             steps[k[:2]](*[int(c) for c in k[2:]])
+            defer[0] = False
         key = [r("PS", KEY + HC * h, KEY + HC * h + HC) for h in (0, 1)]
         for h in (0, 1):
             red(cf(h), key[h])
@@ -666,38 +727,35 @@ def rank_program(g, core, T, topo):
         ts(r("GQ", 48, 64), ind(r("IH", 0, 256), r("OFF", 0, 1)), cf(4), None, OP.mult)
         mm(r("PS", s5, s5 + 2), eye("GM"), r("GQ", 32, 64, 16), True, True)
         a, b, inv, hc = [r("PS", c, c + 1) for c in (s2, s2 + 1, s5, s5 + 1)]
-        dr, ba, nb = cf(12), cf(17), cf(19)
-        ts(ba, b, a, None, OP.subtract)
-        ts(cf(18), a, b, FO + 1.0, OP.add, OP.add)
-        ts(cf(20), b, -2.0, -1.0 - FO, OP.mult, OP.add)
-        ts(cf(28), cf(20), inv, ba, OP.mult, OP.add)
-        ts(cf(22), cf(18), inv, None, OP.mult)
-        mm(YSUM, eye("IDF"), Wr("NF", 2), True, False)
-        ts(Wr("Y0", 2), Wr("NF", 2), a, cf(28), OP.is_gt, OP.mult)
-        mm(YSUM, eye("IDF"), Wr("Y0", 2), False, False)
-        ts(Wr("Y1", 2), Wr("NF", 2), b, cf(22), OP.is_gt, OP.mult)
-        mm(YSUM, eye("IDF"), Wr("Y1", 2), False, True)
-        act(Wr("VA", 2), YSUM, ACT.Abs)
-        ts(dr, inv, -1.0, 1.0, OP.mult, OP.add)
-        ts(nb, b, -1.0, 4095.0, OP.mult, OP.add)
-        ts(cf(14), b, 1000000.0, None, OP.add)
-        ts(cf(13), cf(5), 16000000.0, dr, OP.is_lt, OP.mult)
-        ts(cf(21), nb, inv, b, OP.mult, OP.add)
+        ts(r("RA", 0, 32), r("CO", 0, 32), r("GQ", 0, 1), None, OP.mult)
+        ts(r("RA", 32, 64), r("CO", 32, 64), r("GQ", 16, 17), None, OP.mult)
+        o = r("PS", s5 + 16, s5 + 48)
+        mm(o, eye("IDF"), r("CO", 64, 96), True, False)
+        mm(o, eye("GM"), r("RA", 0, 32), False, False)
+        mm(o, eye("GM"), r("RA", 32, 64), False, True)
+        ts(r("CF", 40, 50), r("PS", s5 + 16, s5 + 26), inv, None, OP.mult)
+        tt(r("CF", 24, 34), r("PS", s5 + 32, s5 + 42), r("CF", 40, 50), OP.add)
+        ts(cf(13), cf(5), 16000000.0, cf(32), OP.is_lt, OP.mult)
         ts(cf(15), cf(5), cf(10), cf(13), OP.is_equal, OP.mult)
-        ts(cf(16), cf(15), -1000000.0, cf(14), OP.mult, OP.add)
+        ts(cf(16), cf(15), -1000000.0, cf(33), OP.mult, OP.add)
         iq = ind(r("IQ", 0, 256), r("OFF", 14, 15))
         ts(r("GQ", 64, 80), iq, cf(11), cf(16), OP.max, OP.is_gt)
         ts(r("GQ", 80, 96), iq, cf(11), -4095.0, OP.max, OP.add)
-        ts(r("GQ", 96, 112), iq, cf(11), cf(21), OP.min, OP.subtract)
+        ts(r("GQ", 96, 112), iq, cf(11), cf(31), OP.min, OP.subtract)
         tt(r("GQ", 112, 116), r("GQ", 80, 84), r("GQ", 64, 68), OP.mult)
         tt(r("GQ", 116, 118), r("GQ", 96, 98), r("GQ", 64, 66), OP.mult)
-        ts(cf(25), a, b, 4095.0, OP.subtract, OP.add)
-        ts(cf(26), nb, dr, a, OP.mult, OP.add)
-        ts(cf(27), nb, dr, None, OP.mult)
-        ts(cf(30), ba, dr, None, OP.mult)
         mm(r("PS", s3, s3 + 4), eye("IDF"), r("CF", 24, 28), True, False)
         mm(r("PS", s3, s3 + 4), eye("GM"), r("GQ", 112, 116), False, False)
         mm(r("PS", s3 + 2, s3 + 4), eye("GMN"), r("GQ", 116, 118), False, True)
+        mm(YSUM, eye("ONE"), r("C16", 0, 256), True, False)
+        mm(YSUM, eye("IB"), Wr("NC", 2), False, False)
+        for h in (0, 1):
+            o = r("PS", YSUM[2] + HC * h, YSUM[2] + HC * h + HC)
+            ts(Wr("Y0", h), Wr("NF", h), a, cf(28), OP.is_gt, OP.mult)
+            mm(o, eye("IDF"), Wr("Y0", h), False, False)
+            ts(Wr("Y1", h), Wr("NF", h), b, cf(29), OP.is_gt, OP.mult)
+            mm(o, eye("IDF"), Wr("Y1", h), False, h == 1)
+        act(Wr("VA", 2), YSUM, ACT.Abs)
         cp(r("OFF", 2, 5, 2), r("PS", s2, s2 + 2))
         if t < 3:
             ts(r("UP%d" % t, 16, 17), hc, I0, PADC, OP.mult, OP.add)
@@ -730,16 +788,15 @@ def rank_program(g, core, T, topo):
         if t < 2:
             built[0] = widen("TW2", "L%d" % (t + 2), "BT", B2, "s" * 8, 0, P, ready_at("s", [], [r("RO", 0, 64)]))
         for n, (c0, c1, q) in enumerate(MOVE):
-            src = ind(r(X, 0, XW), r("RO", c0 // 16, c1 // 16))
             if q == "s":
-                act(r(X2, c0, c1), src, COPY)
+                act(r(X2, c0, c1), ind(r(X, 0, XW), r("RO", c0 // 16, c1 // 16)), COPY)
             else:
-                cp(r(X2, c0, c1), src)
+                defer[0] = n == len(MOVE) - 1 and t < NR - 1 and "mv" in LATE
+                spread("v", lambda a, b, X=X, X2=X2: ("tensor_copy", r(X2, a, b), (ind(r(X, 0, XW), r("RO", a // 16, b // 16)),), {}), c0, c1)
+                defer[0] = False
             if t == 3:
                 dma("y", "y%d" % n, T.y[:, c0:c1], T[X2][:, c0:c1], [], [r(X2, c0, c1)], 256 * (c1 - c0))
-        if t < 3:
-            for h in (0, 1):
-                sums_of(X2, h)
+        ENDS.append(ready_at("v", [], [r("RO", 0, 256)]))
 
     STAT.append(max(b[-1][1] for b in busy.values() if b))
     if DRY:

from concourse.mybir import AluOpType, AxisListType, ActivationFunctionType

P = 4096
FO = P + 16
XW = FO + P
HALF = 2048
HC = 128
BANK = 512
SDT = (992, 640, 672, 800, 928, 480)
UNITS = ((0, 1024, 384, 480), (1024, 2048, 928, 960), (2048, 3072, 288, 288), (3072, 4096, 480, 480))
MOVE = ((0, 1152, "s"), (1152, 2048, "v"), (2048, 3200, "s"), (3200, 4096, "v"))
WENG = "ssssssss"
ENG = {"n": "v", "kur0": "v", "kur": "v", "ka": "s", "cv": "v", "sp": "s", "iq": "v"}
MINP, FILLN = 256, 192
LATE = ("yv0", "tv3", "mv", "yv1", "dv12", "tv0", "dv00")
ORDER = ("wi3 uu0 li00 wi6 uu1 li10 li01 sp0 wi1 li11 li02 wi2 wi4 xf wi0 li12 wi7 eq0 eq2 sp1 wi5 ds00 eq1 ds02 dv00 ds01 dv01 su00 dv02 dv11 su01 dv10 su02 "
         "ds10 ds11 ds12 dv12 su10 su11 yv0 su12 ys0 ys1 yv1 tw hh0 hh1 eh1 ts1 tv0 ys3 yv2 yv3 ys2 hh2 hh3 fl zy1 tv1 eh0 tv3 ts0 zy0 es1 ts2 tv2 ts3 es0 es2 es3 ki2").split()
ORDER0 = ("uu0 wi1 uu1 li00 li10 wi0 wi2 wi5 wi7 li01 eq0 sp0 wi4 wi6 wi3 li11 ds00 li02 eq1 dv00 dv02 ds11 xf ds02 ds01 li12 su00 dv01 ds12 eq2 dv11 dv10 su01 "
          "ds10 su02 dv12 sp1 su10 yv0 su11 ys1 ys0 su12 eh1 tw ys3 yv1 hh0 hh1 yv3 tv1 ys2 yv2 tv0 eh0 hh2 hh3 ts1 zy0 ts0 ts2 es1 tv3 ts3 tv2 zy1 es2 es0 es3 ki2 fl").split()
VOID = 1920.0
NUMBERS = (((0, 0, 0), (0, 0, 4095)), ((0, 0, 0), (1, -1, 4095)), ((0, 1, -4095), (1, -1, 4095)), ((0, 1, -4095), (0, -1, 4095)),
           ((0, -2, -1 - FO), (-1, 1, 0)), ((1, 1, FO + 1), (0, 0, 0)), ((1, -1, 0), (-1, 1, 0)), ((0, -1, 4095), (0, 1, 0)),
           ((0, 0, -1), (0, 0, 1)), ((0, 0, 0), (0, 1, 1000000)))
BIG = 33554432.0

BF, F2, F4, I4, U2 = "bfloat16", "float16", "float32", "int32", "uint16"
SCRATCH = {"PS": ("psum", [128, 4096], F4)}
for _names, _w, _d in ((("XB0", "XB1"), XW, BF), (("TW1", "TW2"), P + 16, F4), (("W",), P, F4),
                       (("TMB", "L1", "L2", "L3", "YB"), P, BF), (("ZB",), P, F2), (("AD",), 3 * P, F2),
                       (("SG1", "SG2", "NN", "CV", "M1", "M2", "INVB"), 256, BF), (("EQ",), 768, BF), (("QB",), 768, F2),
                       (("UC", "KF", "VD", "CMC"), 256, F2), (("SPW",), 512, F2), (("C16",), 256, BF), (("NC",), 256, F2), (("NJH",), 16, F2),
                       (("KM",), 12, I4), (("WT", "PIX", "II", "GI"), 1, I4), (("KMF", "KP"), 12, F4),
                       (("COL",), 32, F4), (("ROW", "Z0"), 144, F4), (("ROWI", "ROWG"), 128, I4), (("NB", "NF", "PN"), 256, F4),
                       (("GM", "GMN", "IDF", "C15"), 128, F4), (("D16",), 16, F4), (("ZM", "ZY"), 144, BF), (("ZV",), 144, F2),
                       (("IB", "IN", "IEQ", "IVD", "I2K", "IM4", "IBG", "ONE", "BW", "BT", "CK0", "CK1", "CK2"), 128, BF), (("CA",), 384, F2), (("W3",), 24, BF), (("WD",), 8, BF), (("IS0", "IS1", "IS2", "IS3", "IS4", "IS5"), 128, BF),
                       (("V1", "KI", "IH", "KD", "VI", "UA", "UH", "INV"), 256, I4),
                       (("QR", "QI"), 768, I4), (("QO",), 768, U2), (("QSO", "HO", "RO"), 256, U2),
                       (("IQ", "US", "KA", "KB", "KS", "CM", "Y0", "Y1", "VA", "TA", "TB", "TC"), 256, F4),
                       (("CF",), 64, F4), (("CI",), 16, I4), (("OFF",), 16, U2), (("R32",), 32, F4), (("RA",), 64, F4), (("CO",), 96, F4), (("GQ",), 128, F4),
                       (("XA", "XC"), 16, F4), (("NI", "NJ"), 16, I4),
                       (("UP0", "UP1", "UP2", "RU10", "RU11", "RU12", "RU20", "RU30", "RU31"), 32, F4)):
    for _n in _names:
        SCRATCH[_n] = ("sbuf", [128, _w], _d)
UPD = [(1, 0), (2, 0), (3, 0), (1, 1), (3, 1), (1, 2)]
LOADS = [("TMB", 0)] + [("XB0", i) for i in range(4)] + [("TMB", i) for i in (3, 1, 2)]
HAND = 1
NT1 = 4
SEMAPHORES = (["cv", "cs", "cp", "cg", "km", "wt", "xf", "sa", "sb", "ls"] + ["x%d" % i for i in range(4)] + ["tm%d" % i for i in range(NT1)]
              + ["y%d" % i for i in range(len(MOVE))] + ["rt1%d" % i for i in range(NT1)]
              + ["rt2", "rt3", "hand"] + ["hd%d" % i for i in range(NT1)] + ["ru%d%d" % u for u in UPD])

STAT, DRY, NR, ENDS = [], False, 4, []
OP = AluOpType
ACT = ActivationFunctionType
COPY = ACT.Identity
CYC, GAT, PEC, LAT, SFIX, VFIX, DLAT, DRATE = 0.83, 1.35, 0.47, 170.0, 110.0, 15.0, 1800.0, 240.0
ARR = {1: (14000.0, 18000.0, 22000.0, 20000.0), 2: 32000.0, 3: 50000.0}


def r(name, c0, c1, step=1):
    return ("r", name, c0, c1, step)


def ind(win, off):
    return ("i", win, off)


def shares(k):
    c0, c1, sy, st = UNITS[k]
    if k % 2:
        return (c1 - sy, c1), (c0, c1 - sy), (c1 - st, c1), (c0, c1 - st)
    return (c0, c0 + sy), (c0 + sy, c1), (c0, c0 + st), (c0 + st, c1)


def width(a):
    return 16 * (a[2][3] - a[2][2]) if a[0] == "i" else -(-(a[3] - a[2]) // a[4])


def rank_program(g, core, T, topo):
    rank = T.rank_of(core)
    N = len(T.cores)

    def lanes(src, dst):
        e = topo.engines(src, dst)
        if topo.chip(src) != topo.chip(dst):
            return e
        far = [topo.engines(src, c) for c in T.cores if topo.chip(c) != topo.chip(src)]
        rest = [k for k in e if not any(k in f for f in far)]
        return rest if rest else e

    def relay(k, j):
        src, dst = T.cores[k], T.cores[(k - j) % N]
        return [c for c in topo.cores_of(src) if topo.die(c) == topo.die(src) and c not in T.cores and topo.may_write(c, dst)][0]

    if rank is None:
        sent = 0
        for k in range(N):
            jobs = [(1, T.L1[:, P // NT1 * i:P // NT1 * (i + 1)], "hd%d" % i, "rt1%d" % i) for i in range(NT1 - HAND, NT1)] + [(3, T.L3[:], "hand", "rt3")]
            for j, piece, came, went in jobs:
                if relay(k, j) == core:
                    dst = T.cores[(k - j) % N]
                    rid, pid, _ = topo.addr(dst)
                    use = lanes(core, dst)
                    g.wait_ge(T.sem[came], len(lanes(T.cores[k], core)))
                    g.remote_dma(piece, piece, T.sem[went], T.sem.ls, pid, rid, sum(1 << e for e in use))
                    sent += len(use)
        if sent:
            g.wait_ge(T.sem.ls, sent)
        return
    queue = {"v": g.vector, "s": g.scalar, "p": g.tensor, "g": g, "y": g.sync}
    own = {"v": "cv", "s": "cs", "p": "cp", "g": "cg"}

    def ap(a):
        if isinstance(a, tuple) and a and a[0] == "r":
            return T[a[1]][:, a[2]:a[3]] if a[4] == 1 else T[a[1]][:, a[2]:a[3]:a[4]]
        if isinstance(a, tuple) and a and a[0] == "i":
            return ap(a[1]).indirect(ap(a[2]))
        return a

    def regs(a):
        if isinstance(a, tuple) and a and a[0] == "r":
            return [a]
        if isinstance(a, tuple) and a and a[0] == "i":
            return [a[1], a[2]]
        return []

    def banks_of(lst):
        return sorted({b for x in lst if x[1] == "PS" for b in range(x[2] // BANK, (x[3] - 1) // BANK + 1)})

    plan = []
    busy = {q: [] for q in queue}
    held = {b: [] for b in range(8)}
    pe_last = {b: 0.0 for b in range(8)}
    seen = {}
    dfree = [0.0]
    later, defer = [], [False]

    def ready_at(q, outs, ins):
        t = 0.0
        for x in ins:
            for y in seen.get(x[1], []):
                if y[2] and y[0] < x[3] and x[2] < y[1]:
                    t = max(t, y[4] + LAT)
        for x in outs:
            for y in seen.get(x[1], []):
                if y[0] < x[3] and x[2] < y[1]:
                    t = max(t, y[4] + (0.0 if y[3] == q == "p" else LAT))
        if q == "p":
            for b in banks_of(outs):
                t = max(t, pe_last[b])
        return t

    def gap(q, t, dur):
        lst = busy[q]
        lo, hi = 0, len(lst)
        while lo < hi:
            mid = (lo + hi) // 2
            if lst[mid][1] <= t:
                lo = mid + 1
            else:
                hi = mid
        while lo < len(lst):
            if lst[lo][0] - t >= dur:
                return t, lst[lo][0], lo
            t = max(t, lst[lo][1])
            lo += 1
        return t, 1e12, lo

    def place(q, dur, outs, ins, done=None):
        t = ready_at(q, outs, ins)
        bs = banks_of(outs + ins)
        while True:
            t, _, k = gap(q, t, dur)
            hit = [y[1] + LAT for b in bs for y in held[b][-160:] if y[2] != q and y[0] - LAT < t + dur and t < y[1] + LAT]
            if not hit:
                break
            t = max(hit)
        busy[q].insert(k, (t, t + dur))
        for b in bs:
            held[b].append((t, t + dur, q))
            if q == "p":
                pe_last[b] = t + dur
        end = t + dur if done is None else done(t)
        mark(q if done is None else q + "dma", outs, ins, end)
        return t

    def mark(q, outs, ins, end):
        for lst, w in ((ins, False), (outs, True)):
            for (_, name, c0, c1, st) in lst:
                old = seen.get(name, [])
                e = end
                if w and st == 1:
                    old = [y for y in old if not (c0 <= y[0] and y[1] <= c1)]
                elif not w:
                    e = max([end] + [y[4] for y in old if not y[2] and y[3] == q and c0 <= y[0] and y[1] <= c1])
                    old = [y for y in old if y[2] or y[3] != q or not (c0 <= y[0] and y[1] <= c1)]
                old.append((c0, c1, w, q, e))
                seen[name] = old

    def split(out, args, kw):
        outs = regs(out)
        ins = outs[1:]
        for a in list(args) + list(kw.values()):
            ins = ins + regs(a)
        return outs[:1], ins

    def cost(q, call, out, args):
        wide = [a for a in [out] + list(args) if regs(a) and width(a) > 1]
        n = max([width(a) for a in wide] + [1])
        if q == "p":
            return PEC * max(64, width(out)) * (4 if SCRATCH[args[0][1]][2] == F4 else 1)
        if q == "g":
            return 130 + 2 * CYC * n
        if out[0] == "i":
            return 50 + 3.5 * CYC * n
        if args and regs(args[0]) and args[0][0] == "i":
            return (65 if q == "s" else 50) + GAT * n
        if q == "s":
            return SFIX + CYC * max(64, n)
        rate = 1.0
        if call == "tensor_tensor":
            rate = 1.0 if "PS" in (args[0][1], args[1][1]) else 2.0
        elif call != "tensor_reduce" and all(SCRATCH[a[1]][2] in (BF, F2, U2) for a in wide):
            rate = 0.5
        return VFIX + CYC * max(64, n * rate)

    calls = {"memset": g.vector.memset, "tensor_scalar": g.vector.tensor_scalar, "tensor_tensor": g.vector.tensor_tensor,
             "tensor_copy": g.vector.tensor_copy, "tensor_reduce": g.vector.tensor_reduce, "activation": g.scalar.activation,
             "matmul": g.tensor.matmul, "iota": g.iota}

    def E(q, call, out, *args, **kw):
        EE(q, [(call, out, args, kw)])

    def EE(q, group):
        outs, ins, dur = [], [], []
        for call, out, args, kw in group:
            o, i = split(out, args, kw)
            outs += o
            ins += i
            dur.append(cost(q, call, out, args))
        for job in list(later):
            o = job[0](job[1], job[2])[1]
            if job in later and any(x[1] == o[1] and x[2] < o[3] and o[2] < x[3] for x in outs + ins):
                later.remove(job)
                spread("v", *job, now=True)
        t = place(q, sum(dur), outs, ins)
        for (call, out, args, kw), d in zip(group, dur):
            plan.append((t, len(plan), "c", q, call, out, args, kw))
            t += d
        if q == "v" and later and sum(dur) < 300 and gap("v", t, 1.0)[1] > 1e11:
            job = later.pop(0)
            call, out, args, kw = job[0](job[1], job[2])
            if ready_at("v", *split(out, args, kw)) <= t + LAT:
                n = job[2] - job[1] if job[2] - job[1] < FILLN + 96 else FILLN
                keep = list(later)
                del later[:]
                EE("v", [job[0](job[1], job[1] + n)])
                later.extend(keep)
                job[1] += n
            if job[1] < job[2]:
                later.insert(0, job)

    def dma(q, sem, out_ap, in_ap, outs, ins, nbytes):
        def done(t):
            dfree[0] = max(dfree[0], t + DLAT) + nbytes / DRATE
            return dfree[0]
        t = place(q, 50.0, outs, ins, done)
        plan.append((t, len(plan), "d", q, sem, out_ap, in_ap, outs, ins))

    def send(dst, out_ap, in_reg, sem, use):
        t = place("g", 500.0, [], [in_reg])
        plan.append((t, len(plan), "r", dst, out_ap, in_reg, sem, use))
        return t

    def spread(q, make, c0, c1, now=False):
        if defer[0] and not now:
            if c0 < c1:
                later.append([make, c0, c1])
            return
        while c0 < c1:
            call, out, args, kw = make(c0, c1)
            o, i = split(out, args, kw)
            t = ready_at(q, o, i)
            t, e, _ = gap(q, t, 66 + GAT * min(MINP, c1 - c0))
            n = min(c1 - c0, int((e - t - 66) / GAT) // 32 * 32)
            if 0 < c1 - c0 - n < 96:
                n = max(32, n - 96)
            EE(q, [make(c0, c0 + n)])
            c0 += n

    def settle_moves():
        while later:
            spread("v", *later.pop(0), now=True)

    def ts(out, a, s1, s2, o0, o1=None):
        if o1 is None:
            E("v", "tensor_scalar", out, a, s1, None, o0)
        else:
            E("v", "tensor_scalar", out, a, s1, s2, o0, o1)

    def tt(out, a, b, o):
        E("v", "tensor_tensor", out, a, b, o)

    def cp(out, a):
        E("v", "tensor_copy", out, a)

    def red(out, a):
        E("v", "tensor_reduce", out, a, AxisListType.X, OP.min)

    def act(out, a, f, **kw):
        E("s", "activation", out, a, f, **kw)

    def lin(q, out, a, scale, bias):
        if q == "s":
            act(out, a, COPY, scale=scale, bias=bias)
        else:
            ts(out, a, scale, bias, OP.mult, OP.add)

    def conv(out, a):
        if ENG["cv"] == "s":
            act(out, a, COPY)
        else:
            cp(out, a)

    def mm(out, lhsT, rhs, start, stop):
        E("p", "matmul", out, lhsT, rhs, start, stop)

    def fill(out, v):
        E("v", "memset", out, v)

    def ps(b, c0, c1):
        return r("PS", b * BANK + c0, b * BANK + c1)

    def cf(k):
        return r("CF", k, k + 1)

    def col(k):
        return r("COL", k, k + 1)

    def eye(name):
        return r(name, 0, 128)

    def wsum(c, z, buf, c0, n, start, stop):
        for j in (0, 8):
            EE("p", [("matmul", r("PS", c, c + n // 16), (r(z, 15 - i, 143 - i), r(buf, c0 + i, c0 + n, 16), start and i == 0, stop and i == 15), {})
                     for i in range(j, j + 8)])

    RAW, SPK, VS = [[(BANK + HC) * h + HC * k for h in (0, 1)] for k in range(3)]
    UP = (3 * HC, 4 * HC)
    K0 = (2 * BANK, 3 * BANK + 128)
    PIX0 = 2 * BANK + 384
    KU = 4 * BANK
    KEY = 4 * BANK + 384
    K2, YSUM = ps(4, 0, 256), ps(5, 128, 384)
    s1, s2, s3, s4, s5 = RAW[0], RAW[1], SPK[0], SPK[1], K0[0]

    dma("s", "wt", T.WT[:], T.wt[:], [r("WT", 0, 1)], [], 60000)
    dma("s", "km", T.KM[:], T.km[:], [r("KM", 0, 12)], [], 60000)
    TP = P // NT1
    for name, i in LOADS:
        c = r(name, TP * i, TP * i + TP)
        dma("y", ("x%d" if name == "XB0" else "tm%d") % i, ap(c), (T.x if name == "XB0" else T.tm)[:, TP * i:TP * i + TP], [c], [], 256 * TP)
    dma("y", "sa", T.SG1[:], T.x[15:128:16, 0:P], [r("SG1", 0, 256)], [], 65536)
    E("g", "iota", r("PIX", 0, 1), [[0, 1]], 0, 1)
    E("g", "iota", r("ROW", 0, 144), [[1, 144]], 0, 0, allow_small_or_imprecise_dtypes=True)
    E("g", "iota", r("ROWI", 0, 128), [[1, 128]], 0, 0)
    E("g", "iota", r("NB", 0, 256), [[16, 256]], 0, 0, allow_small_or_imprecise_dtypes=True)
    IF, PF, FM, SM, GF, WTF, G15, HS, FM2, I0, PADC, B2 = [col(k) for k in range(12)]
    Z0, ROWM = r("Z0", 0, 144), r("ROW", 0, 128)
    fill(eye("ONE"), 1.0)
    ts(eye("CA"), eye("ONE"), 4112.0, None, OP.mult)
    for c in (128, 256):
        ts(r("CA", c, c + 128), eye("ONE"), 0.0, None, OP.mult)
    fill(r("C16", 0, 256), 16.0)
    ts(r("II", 0, 1), r("PIX", 0, 1), 15, None, OP.bitwise_and)
    ts(r("GI", 0, 1), r("PIX", 0, 1), 4, None, OP.arith_shift_right)
    cp(PF, r("PIX", 0, 1))
    cp(IF, r("II", 0, 1))
    cp(GF, r("GI", 0, 1))
    cp(WTF, r("WT", 0, 1))
    ts(G15, GF, 16.0, 15.0, OP.mult, OP.add)
    ts(FM, IF, 14.5, None, OP.is_lt)
    ts(SM, IF, 14.5, None, OP.is_gt)
    ts(Z0, r("ROW", 0, 144), G15, None, OP.is_equal)
    for k, c in enumerate((WTF, FM, SM)):
        ts(r("W3", 8 * k, 8 * k + 8), r("ROW", 0, 8), GF, c, OP.is_equal, OP.mult)
    ts(r("ROWG", 0, 128), eye("ROWI"), 4, None, OP.arith_shift_right)
    ts(eye("GM"), r("ROWG", 0, 128), GF, None, OP.is_equal)
    ts(r("ROWG", 0, 128), eye("ROWI"), 15, None, OP.bitwise_and)
    ts(eye("C15"), r("ROWG", 0, 128), 14.5, None, OP.is_gt)
    tt(eye("C15"), eye("C15"), eye("GM"), OP.mult)
    ts(eye("IDF"), ROWM, PF, None, OP.is_equal)
    tt(eye("GMN"), eye("C15"), eye("IDF"), OP.add)
    ts(eye("BW"), eye("GMN"), FM, None, OP.mult)
    cp(r("KMF", 0, 12), r("KM", 0, 12))
    ts(r("KP", 0, 12), r("KMF", 0, 12), 128.0, None, OP.add)
    for name, v in (("IB", 1.0), ("IN", -1.0), ("IEQ", VOID * 16384.0)):
        ts(eye(name), ROWM, PF, v, OP.is_equal, OP.mult)
    ts(HS, FM, 0.5, None, OP.mult)
    ts(r("NF", 0, 256), r("NB", 0, 256), IF, None, OP.add)
    for h in (0, 1):
        cp(r("PS", PIX0 + HC * h, PIX0 + HC * h + HC), r("NF", HC * h, HC * h + HC))
    ts(col(12), FM, 49152.0, -16384.0, OP.mult, OP.add)
    ts(r("WD", 0, 8), r("ROW", 0, 8), GF, col(12), OP.is_equal, OP.mult)
    for k in range(6):
        ts(col(18 + k), PF, SDT[k] // 16 - 0.5, 16384.0, OP.is_gt, OP.mult)
        ts(eye("IS%d" % k), eye("IB"), col(18 + k), None, OP.mult)
    for m in range(3):
        ts(col(13 + m), PF, 63.5, 262144.0 + 32.0 + 64.0 * m, OP.is_gt, OP.mult)
        ts(eye("CK%d" % m), eye("ONE"), col(13 + m), -262144.0, OP.mult, OP.add)

    asker = {j: T.cores[(rank - j) % N] for j in (1, 2, 3)}
    lands = []
    for j in (1, 2, 3):
        n = len(lanes(T.cores[(rank + j) % N], core))
        if j == 1:
            for i in range(NT1):
                lands.append((r("L1", TP * i, TP * i + TP), "rt1%d" % i, n))
                mark("remote", [lands[-1][0]], [], ARR[1][i])
        else:
            lands.append((r("L%d" % j, 0, P), "rt%d" % j, n))
            mark("remote", [lands[-1][0]], [], ARR[j])
        for (jj, t) in UPD:
            if jj == j:
                lands.append((r("RU%d%d" % (j, t), 0, 32), "ru%d%d" % (j, t), n))
    for i in [x[1] for x in LOADS if x[0] == "TMB"]:
        via = i >= NT1 - HAND
        dst = relay(rank, 1) if via else asker[1]
        send(dst, T.L1[:, TP * i:TP * i + TP], r("TMB", TP * i, TP * i + TP), ("hd%d" if via else "rt1%d") % i, lanes(core, dst))
    send(asker[2], T.L2[:], r("TMB", 0, P), "rt2", lanes(core, asker[2]))
    send(relay(rank, 3), T.L3[:], r("TMB", 0, P), "hand", lanes(core, relay(rank, 3)))

    def late_constants():
        for name in ("TW1", "TW2", "XB0", "XB1"):
            fill(r(name, P, P + 16), 0.0)
        for j in (0, 1, 2):
            fill(r("UP%d" % j, 0, 32), 0.0)
        ts(col(16), WTF, 4.0, SM, OP.mult, OP.add)
        ts(r("ZV", 0, 144), Z0, col(16), None, OP.mult)
        ts(col(17), FM, 8192.0, -4096.0, OP.mult, OP.add)
        ts(r("ZM", 0, 144), Z0, col(17), None, OP.mult)
        ts(r("ZY", 0, 144), Z0, FM, -2048.0, OP.mult, OP.mult)
        tt(eye("GMN"), eye("GMN"), eye("IDF"), OP.add)
        ts(eye("BT"), eye("GMN"), FM, None, OP.mult)
        ts(B2, SM, 2.0, None, OP.mult)
        ts(eye("GMN"), eye("GM"), -1.0, None, OP.mult)
        for name, v in (("IVD", VOID * 2048.0), ("I2K", 2048.0), ("IM4", -4.0), ("IBG", BIG)):
            ts(eye(name), ROWM, PF, v, OP.is_equal, OP.mult)
        ts(r("D16", 0, 16), r("ROW", 0, 16), IF, None, OP.is_equal)
        ts(r("PN", 0, 256), r("NF", 0, 256), -2097152.0, None, OP.add)
        fill(r("CV", 0, 256), 0.0078125)
        ts(Wr("NC", 2), Wr("NF", 2), -2048.0, None, OP.add)
        fill(r("CO", 0, 96), 0.0)
        for k, (x, y) in enumerate(NUMBERS):
            for c, row in ((k, x), (16 + k, y)):
                for j, v in enumerate(row):
                    if v:
                        E("g", "iota", r("CO", 32 * j + c, 32 * j + c + 1), [[0, 1]], v, 0, allow_small_or_imprecise_dtypes=True)
        for k in (0, 2):
            c0, c1 = shares(k)[1][0] // 16, shares(k + 1)[1][1] // 16
            if c0 < c1:
                fill(r("CV", c0, c1), -64.0)
            c0, c1 = shares(k)[3][0] // 16, shares(k + 1)[3][1] // 16
            if c0 < c1:
                ts(r("PN", c0, c1), r("PN", c0, c1), 8192.0, None, OP.add)
        ts(I0, IF, 0.5, None, OP.is_lt)
        ts(PADC, IF, 0.5, 4096.0, OP.is_gt, OP.mult)
        tt(PADC, PADC, IF, OP.add)
        ts(FM2, FM, -1.0, 2.0, OP.mult, OP.add)

    ring, built = [0], [0]
    waiting = {}

    def flush(k):
        if k in waiting:
            act(*waiting.pop(k), ACT.Abs, scale=HS)

    def settle(x):
        for j in [(ring[0] + 1) % 2, ring[0] % 2]:
            if j in waiting and waiting[j][0][1] == x[1] and waiting[j][0][2] < x[3] and x[2] < waiting[j][0][3]:
                flush(j)

    def slot(n):
        ring[0] += 1
        flush(ring[0] % 2)
        return ps(6 + ring[0] % 2, 0, n)

    def pieces(c0, c1):
        n = c1 - c0
        k = -(-n // BANK)
        cut = [c0 + min(n, -(-n * i // (32 * max(k, 1))) * 32) for i in range(k + 1)]
        return list(zip(cut[:-1], cut[1:]))

    def widen(dst, src, mat, bias, eng, c0, c1, until=None):
        for c in range(c0, c1, BANK):
            if until is not None:
                t0 = max(ready_at("p", [ps(6 + (ring[0] + 1) % 2, 0, BANK)], [r(src, c, c + BANK)]) + 400.0, ready_at("s", [r(dst, c, c + BANK)], []))
                if gap("s", t0, 530.0)[0] + 530.0 > until:
                    return c
            o = slot(BANK)
            mm(o, eye(mat), r(src, c, c + BANK), True, True)
            lin(eng[c // BANK], r(dst, c, c + BANK), o, 1.0, bias)
        return c1

    def sums_of(xb, h):
        c = RAW[h]
        mm(r("PS", c, c + 384), eye("ONE"), r("CA", 0, 384), True, False)
        for j in (0, 8):
            EE("p", [("matmul", r("PS", c + i, c + 384, 16), (r(xb, HALF * h + i, HALF * h + HALF, 16), r("W3", 0, 24), False, i == 15), {})
                     for i in range(j, j + 8)])

    def Wr(name, h, k=0):
        return r(name, 256 * k, 256 * k + 256) if h == 2 else r(name, 256 * k + HC * h, 256 * k + HC * h + HC)

    def pix(h):
        return r("PS", PIX0 + HC * (h % 2), PIX0 + HC * min(h, 1) + HC)

    for i in range(4):
        cp(r("XB0", FO + 1024 * i, FO + 1024 * i + 1024), r("XB0", 1024 * i, 1024 * i + 1024))

    for t in range(NR):
        X, X2 = "XB%d" % (t % 2), "XB%d" % (1 - t % 2)
        xwin = r(X, 0, P)
        tj = 1 + t % 3
        TB = "TW1" if tj == 1 else "TW2"

        def lists(h, m):
            raw, u = r("PS", RAW[h], RAW[h] + HC), r("PS", UP[h], UP[h] + HC)
            if m == 0:
                lin(ENG["n"], Wr("NN", h), raw, 1.0, 0.5)
                tt(Wr("UC", h), raw, Wr("NN", h), OP.subtract)
                mm(u, eye("ONE"), eye("C16"), True, False)
                mm(u, Wr("UC", h), eye("IB"), False, True)
                act(Wr("US", h), u, ACT.Square, bias=-2048.0)
                ts(Wr("V1", h), Wr("US", h), 0.03125, -0.484375, OP.mult, OP.add)
            k = r("PS", KU + 256 * m + HC * h, KU + 256 * m + HC * h + HC)
            lin(ENG["kur" if m else "kur0"], k, u, r("KP", 3 * t + m, 3 * t + m + 1), 0.0)
            tt(Wr("QR", h, m), k, Wr("V1", h), OP.add)
            ts(Wr("QI", h, m), Wr("QR", h, m), 4095, None, OP.bitwise_and)
            cp(Wr("QO", h, m), Wr("QI", h, m))

        def marks(m):
            tt(Wr("EQ", 2, m), pix(2), Wr("QI", 2, m), OP.is_equal)
            ts(Wr("QB", 2, m), Wr("QO", 2, m), -2048.0, None, OP.add)

        def own_sum(h):
            lin(ENG["sp"], Wr("SPW", 2, h), r("PS", SPK[h], SPK[h] + 2 * HC), -1.0, 1.0)

        def ad(h, m, c0, c1):
            return r("AD", HALF * (3 * h + m) + c0, HALF * (3 * h + m) + c1)

        def d_v(h, m):
            oc = 256 * m + HC * h
            spread("v", lambda c0, c1: ("tensor_tensor", ad(h, m, c0, c1),
                                        (ind(r("W", 0, P), r("QO", oc + c0 // 16, oc + c1 // 16)), r(X, HALF * h + c0, HALF * h + c1), OP.max), {}),
                   SDT[3 * h + m], HALF)

        def d_s(h, m):
            oc = 256 * m + HC * h
            if SDT[3 * h + m]:
                act(ad(h, m, 0, SDT[3 * h + m]), ind(xwin, r("QO", oc, oc + SDT[3 * h + m] // 16)), COPY)
            for c, e in pieces(0, SDT[3 * h + m]):
                o = slot(e - c)
                mm(o, eye("IN"), r(X, HALF * h + c, HALF * h + e), True, False)
                mm(o, eye("IB"), ad(h, m, c, e), False, True)
                waiting[ring[0] % 2] = (ad(h, m, c, e), o)

        def d_sum(h, m):
            c, s = K0[h] + 128 * m, SDT[3 * h + m] // 16
            o = r("PS", c, c + HC)
            settle(ad(h, m, 0, HALF))
            mm(o, eye("ONE"), eye("CK%d" % m), True, False)
            mm(o, Wr("EQ", h, m), eye("IEQ"), False, False)
            if s < HC:
                mm(o, eye("IS%d" % (3 * h + m)), Wr("SPW", 0, h), False, False)
            c0 = HALF * (3 * h + m)
            for j in (0, 8):
                EE("p", [("matmul", r("PS", c + i, c + HC, 16), (r("AD", c0 + i, c0 + HALF, 16), r("WD", 0, 8), False, False), {}) for i in range(j, j + 8)])
            mm(o, Wr("QB", h, m), eye("IB"), False, True)
            if m == 0:
                lin(ENG["ka"], Wr("KA", h), o, 1.0, 0.0)
            else:
                tt(Wr("KB" if m == 1 else "KI", h), o, Wr("KA" if m == 1 else "KB", h), OP.min)
            if m == 2:
                o = r("PS", K0[h], K0[h] + HC)
                ts(Wr("KD", h), Wr("KI", h), 4095, None, OP.bitwise_and)
                ts(Wr("KF", h), Wr("KD", h), -2048.0, None, OP.add)
                mm(o, Wr("KF", h), eye("IB"), True, True)
                ts(Wr("QSO", h), o, 2048.0, None, OP.add)
                lin(ENG["iq"], Wr("IQ", h), o, 1.0, 2048.0)

        def e_head(h):
            ts(Wr("KD", h), Wr("KI", h), 14, None, OP.arith_shift_right)
            conv(Wr("KF", h), Wr("KD", h))
            ts(Wr("VD", h), Wr("KF", h), VOID - 1024.0, None, OP.is_ge)
            o = r("PS", KEY + HC * h, KEY + HC * h + HC)
            mm(o, eye("IDF"), Wr("PN", h), True, False)
            mm(o, Wr("KF", h), eye("I2K"), False, False)
            mm(o, Wr("VD", h), eye("IVD"), False, False)

        def y_s(k):
            a, b = shares(k)[0]
            if a < b:
                act(r("YB", a, b), ind(xwin, r("QSO", a // 16, b // 16)), COPY)

        def y_v(k):
            spread("v", lambda a, b: ("tensor_tensor", r("YB", a, b), (ind(xwin, r("QSO", a // 16, b // 16)), r(X, FO + a, FO + b), OP.add), {}), *shares(k)[1])

        def h_list(k):
            c0, c1, sy, st = UNITS[k]
            h, w0, w1 = c0 // HALF, c0 // 16, c1 // 16
            c = VS[k % 2] + 64 * (k // 2) - w0
            mm(r("PS", c + w0, c + w1), eye("ONE"), r("CV", w0, w1), True, False)
            for (a, b), src, mat in zip(shares(k)[:2], (Wr("SPW", 1, h), Wr("UC", h)), ("IN", "IM4")):
                if a < b:
                    mm(r("PS", c + a // 16, c + b // 16), src, r(mat, a // 16 - HC * h, b // 16 - HC * h), False, False)
            wsum(c + w0, "ZV", "YB", c0, c1 - c0, False, True)
            cp(r("VI", w0, w1), r("PS", c + w0, c + w1))
            ts(r("UA", w0, w1), r("VI", w0, w1), 2, 4095, OP.arith_shift_right, OP.bitwise_and)
            c = UP[h] - HC * h
            tt(r("UH", w0, w1), r("PS", c + w0, c + w1), r("UA", w0, w1), OP.mult)
            ts(r("IH", w0, w1), r("UH", w0, w1), 4, 4095, OP.arith_shift_right, OP.bitwise_and)
            cp(r("HO", w0, w1), r("IH", w0, w1))

        def score_s(k):
            twin = r(TB, 0, P)
            for c, e in pieces(*shares(k)[2]):
                act(r("ZB", c, e), ind(twin, r("HO", c // 16, e // 16)), COPY)
                o = slot(e - c)
                mm(o, eye("IB"), r("YB", c, e), True, False)
                a, b = max(c, shares(k)[0][0]), min(e, shares(k)[0][1])
                if a < b:
                    mm(r("PS", o[2] + a - c, o[2] + b - c), eye("IB"), r(X, a, b), False, False)
                mm(o, eye("IN"), r("ZB", c, e), False, True)
                waiting[ring[0] % 2] = (r("ZB", c, e), o)
                flush(1 - ring[0] % 2)

        def score_v(k):
            twin = r(TB, 0, P)
            spread("v", lambda a, b: ("tensor_tensor", r("ZB", a, b), (ind(twin, r("HO", a // 16, b // 16)), r("YB", a, b), OP.max), {}), *shares(k)[3])

        def y_sum(h):
            c0, c1 = shares(2 * h)[3][0], shares(2 * h + 1)[3][1]
            if c0 < c1:
                wsum(KEY + c0 // 16, "ZY", "YB", c0, c1 - c0, False, False)

        def e_sum(k):
            c0, c1, sy, st = UNITS[k]
            settle(r("ZB", c0, c1))
            left[c0 // HALF] -= c1 - c0
            wsum(KEY + c0 // 16, "ZM", "ZB", c0, c1 - c0, False, left[c0 // HALF] == 0)

        def tables():
            if t < 3:
                widen(TB, "L%d" % (t + 1), "BT", B2, "s" * 8, built[0], P)
            for (j, tu) in UPD:
                if j == tj and tu < t:
                    RU = "RU%d%d" % (j, tu)
                    cp(r("OFF", 8 + 2 * tu, 9 + 2 * tu), r(RU, 16, 17))
                    cp(ind(r(TB, 0, P + 16), r("OFF", 8 + 2 * tu, 9 + 2 * tu)), r(RU, 0, 16))

        def kinds(h):
            tt(Wr("CM", h), pix(h), Wr("IQ", h), OP.min)
            act(Wr("CMC", h), Wr("CM", h), COPY, bias=-2048.0)
            ts(Wr("INV", h), Wr("VI", h), 1, None, OP.bitwise_and)
            conv(Wr("INVB", h), Wr("INV", h))

        def flip():
            ts(r("SG2", 0, 256), r("SG1", 0, 256), -1.0, 1.0, OP.mult, OP.add)
            dma("y", "sb", T[X][15:128:16, FO:FO + P], T.SG2[:], [r(X, FO, FO + P)], [r("SG2", 0, 256)], 65536)

        left = [HALF, HALF]

        def second():
            if t:
                settle_moves()
                dma("y", "xf", T[X][:, FO:FO + P], ap(xwin), [r(X, FO, FO + P)], [xwin], 1048576)
                dma("y", "sa", T.SG1[:], T[X][15:128:16, 0:P], [r("SG1", 0, 256)], [xwin], 65536)

        steps = {"uu": lambda h: sums_of(X, h), "xf": second, "li": lists, "eq": marks, "wi": lambda k: widen("W", X, "BW", SM, WENG, BANK * k, BANK * k + BANK), "sp": own_sum,
                 "ds": d_s, "dv": d_v, "su": d_sum, "ys": y_s, "yv": y_v, "hh": h_list, "eh": e_head, "ts": score_s, "tv": score_v,
                 "zy": y_sum, "es": e_sum, "tw": tables, "ki": kinds, "fl": flip}
        for k in (ORDER0 if t == 0 else ORDER):
            if t == 0 and k == "su00":
                late_constants()
            defer[0] = k in LATE
            steps[k[:2]](*[int(c) for c in k[2:]])
            defer[0] = False
        key = [r("PS", KEY + HC * h, KEY + HC * h + HC) for h in (0, 1)]
        for h in (0, 1):
            red(cf(h), key[h])
            ts(r("R32", 16 * h, 16 * h + 16), r("D16", 0, 16), cf(h), None, OP.mult)

        mm(r("PS", s1, s1 + 32), eye("GM"), r("R32", 0, 32), True, True)
        kk = r("CI", 0, 1)
        red(kk, r("PS", s1, s1 + 32))
        red(cf(2), r("PS", s1, s1 + 32))
        ts(r("CI", 1, 2), kk, 4, 255, OP.arith_shift_right, OP.bitwise_and)
        ts(r("CI", 3, 4), kk, 4095, None, OP.bitwise_and)
        cp(r("OFF", 0, 1), r("CI", 1, 2))
        cp(cf(3), r("CI", 3, 4))
        ts(cf(4), cf(0), cf(1), cf(2), OP.min, OP.is_equal)
        iq = ind(r("IQ", 0, 256), r("OFF", 0, 1))
        ts(r("GQ", 0, 16), iq, cf(3), cf(4), OP.min, OP.mult)
        ts(r("GQ", 16, 32), iq, cf(3), cf(4), OP.max, OP.mult)
        mm(r("PS", s2, s2 + 2), eye("GM"), r("GQ", 0, 32, 16), True, True)
        for h in (0, 1):
            act(Wr("KS", h), key[h], COPY)
        mm(K2, eye("IBG"), Wr("INVB", 2), True, False)
        for h in (0, 1):
            mm(r("PS", K2[2] + HC * h, K2[2] + HC * h + HC), eye("IDF"), Wr("KS", h), False, False)
        ts(Wr("M1", 2), Wr("CMC", 2), 2048.0, r("PS", s2, s2 + 1), OP.add, OP.is_le)
        ts(Wr("M2", 2), Wr("CMC", 2), 2048.0, r("PS", s2 + 1, s2 + 2), OP.add, OP.is_ge)
        mm(K2, eye("IBG"), Wr("M1", 2), False, False)
        mm(K2, eye("IBG"), Wr("M2", 2), False, True)
        red(cf(5), K2)
        ts(r("R32", 0, 16), r("D16", 0, 16), cf(5), None, OP.mult)
        mm(r("PS", s1, s1 + 16), eye("GM"), r("R32", 0, 16), True, True)
        kk = r("CI", 4, 5)
        red(kk, r("PS", s1, s1 + 16))
        red(cf(10), r("PS", s1, s1 + 16))
        ts(r("CI", 5, 6), kk, 4, 255, OP.arith_shift_right, OP.bitwise_and)
        ts(r("CI", 7, 8), kk, 4095, None, OP.bitwise_and)
        cp(r("OFF", 14, 15), r("CI", 5, 6))
        cp(cf(11), r("CI", 7, 8))
        ts(r("GQ", 32, 48), ind(r("INV", 0, 256), r("OFF", 0, 1)), cf(4), None, OP.mult)
        ts(r("GQ", 48, 64), ind(r("IH", 0, 256), r("OFF", 0, 1)), cf(4), None, OP.mult)
        mm(r("PS", s5, s5 + 2), eye("GM"), r("GQ", 32, 64, 16), True, True)
        a, b, inv, hc = [r("PS", c, c + 1) for c in (s2, s2 + 1, s5, s5 + 1)]
        ts(r("RA", 0, 32), r("CO", 0, 32), r("GQ", 0, 1), None, OP.mult)
        ts(r("RA", 32, 64), r("CO", 32, 64), r("GQ", 16, 17), None, OP.mult)
        o = r("PS", s5 + 16, s5 + 48)
        mm(o, eye("IDF"), r("CO", 64, 96), True, False)
        mm(o, eye("GM"), r("RA", 0, 32), False, False)
        mm(o, eye("GM"), r("RA", 32, 64), False, True)
        ts(r("CF", 40, 50), r("PS", s5 + 16, s5 + 26), inv, None, OP.mult)
        tt(r("CF", 24, 34), r("PS", s5 + 32, s5 + 42), r("CF", 40, 50), OP.add)
        ts(cf(13), cf(5), 16000000.0, cf(32), OP.is_lt, OP.mult)
        ts(cf(15), cf(5), cf(10), cf(13), OP.is_equal, OP.mult)
        ts(cf(16), cf(15), -1000000.0, cf(33), OP.mult, OP.add)
        iq = ind(r("IQ", 0, 256), r("OFF", 14, 15))
        ts(r("GQ", 64, 80), iq, cf(11), cf(16), OP.max, OP.is_gt)
        ts(r("GQ", 80, 96), iq, cf(11), -4095.0, OP.max, OP.add)
        ts(r("GQ", 96, 112), iq, cf(11), cf(31), OP.min, OP.subtract)
        tt(r("GQ", 112, 116), r("GQ", 80, 84), r("GQ", 64, 68), OP.mult)
        tt(r("GQ", 116, 118), r("GQ", 96, 98), r("GQ", 64, 66), OP.mult)
        mm(r("PS", s3, s3 + 4), eye("IDF"), r("CF", 24, 28), True, False)
        mm(r("PS", s3, s3 + 4), eye("GM"), r("GQ", 112, 116), False, False)
        mm(r("PS", s3 + 2, s3 + 4), eye("GMN"), r("GQ", 116, 118), False, True)
        mm(YSUM, eye("ONE"), r("C16", 0, 256), True, False)
        mm(YSUM, eye("IB"), Wr("NC", 2), False, False)
        for h in (0, 1):
            o = r("PS", YSUM[2] + HC * h, YSUM[2] + HC * h + HC)
            ts(Wr("Y0", h), Wr("NF", h), a, cf(28), OP.is_gt, OP.mult)
            mm(o, eye("IDF"), Wr("Y0", h), False, False)
            ts(Wr("Y1", h), Wr("NF", h), b, cf(29), OP.is_gt, OP.mult)
            mm(o, eye("IDF"), Wr("Y1", h), False, h == 1)
        act(Wr("VA", 2), YSUM, ACT.Abs)
        cp(r("OFF", 2, 5, 2), r("PS", s2, s2 + 2))
        if t < 3:
            ts(r("UP%d" % t, 16, 17), hc, I0, PADC, OP.mult, OP.add)
        act(r("XA", 0, 16), ind(xwin, r("OFF", 2, 3)), COPY, scale=FM2)
        act(r("XC", 0, 16), ind(xwin, r("OFF", 4, 5)), COPY, scale=FM)
        ts(r("OFF", 6, 7), a, I0, PADC, OP.mult, OP.add)
        tt(r("NI", 0, 16), r("XA", 0, 16), r("XC", 0, 16), OP.add)
        ts(r("NJ", 0, 16), r("NI", 0, 16), 1, None, OP.arith_shift_right)
        cp(ind(r(X, 0, P + 16), r("OFF", 6, 7)), r("NJ", 0, 16))

        t4, t2, t3, L = [r("PS", s3 + k, s3 + k + 1) for k in range(4)]
        for h in (0, 1):
            o = [r("PS", K0[h] + HC * k, K0[h] + HC * k + HC) for k in range(3)]
            ts(o[0], Wr("NF", h), t4, L, OP.is_gt, OP.mult)
            ts(Wr("TB", h), Wr("NF", h), t2, L, OP.is_gt, OP.mult)
            ts(o[1], Wr("NF", h), t3, cf(30), OP.is_gt, OP.mult)
            tt(Wr("TA", h), o[0], Wr("TB", h), OP.subtract)
            tt(o[2], Wr("VA", h), o[1], OP.subtract)
            tt(Wr("TC", h), o[2], Wr("TA", h), OP.add)
            cp(Wr("RO", h), Wr("TC", h))
        if t < 3:
            UPt = "UP%d" % t
            cp(r("NJH", 0, 16), r("NJ", 0, 16))
            mm(r("PS", s4, s4 + 16), eye("BT"), r("NJH", 0, 16), True, True)
            ts(r(UPt, 0, 16), r("PS", s4, s4 + 16), B2, None, OP.add)
            for (j, tu) in UPD:
                if tu == t:
                    at = send(asker[j], T["RU%d%d" % (j, t)][:], r(UPt, 0, 32), "ru%d%d" % (j, t), lanes(core, asker[j]))
                    mark("remote", [r("RU%d%d" % (j, t), 0, 32)], [], at + 4000.0)
        if t < 2:
            built[0] = widen("TW2", "L%d" % (t + 2), "BT", B2, "s" * 8, 0, P, ready_at("s", [], [r("RO", 0, 64)]))
        for n, (c0, c1, q) in enumerate(MOVE):
            if q == "s":
                act(r(X2, c0, c1), ind(r(X, 0, XW), r("RO", c0 // 16, c1 // 16)), COPY)
            else:
                defer[0] = n == len(MOVE) - 1 and t < NR - 1 and "mv" in LATE
                spread("v", lambda a, b, X=X, X2=X2: ("tensor_copy", r(X2, a, b), (ind(r(X, 0, XW), r("RO", a // 16, b // 16)),), {}), c0, c1)
                defer[0] = False
            if t == 3:
                dma("y", "y%d" % n, T.y[:, c0:c1], T[X2][:, c0:c1], [], [r(X2, c0, c1)], 256 * (c1 - c0))
        ENDS.append(ready_at("v", [], [r("RO", 0, 256)]))

    STAT.append(max(b[-1][1] for b in busy.values() if b))
    if DRY:
        return
    total = {}
    clock = {q: {} for q in queue}
    rec = {}
    bank = {}
    serial = [0]

    def merge(a, b):
        for k, v in b.items():
            if a.get(k, 0) < v:
                a[k] = v

    def need(q, outs, ins):
        deps = []
        for (_, name, c0, c1, st) in ins:
            for x in rec.get(name, []):
                if x[2] and x[0] < c1 and c0 < x[1]:
                    deps.append(x)
        for (_, name, c0, c1, st) in outs:
            for x in rec.get(name, []):
                if x[0] < c1 and c0 < x[1] and not (x[3] == q and q == "p"):
                    deps.append(x)
        for b in banks_of(list(outs) + list(ins)):
            for q2, x in bank.get(b, {}).items():
                if q2 != q:
                    deps.append(x)
        ck = clock[q]
        deps.sort(key=lambda x: -x[6])
        todo = {}
        for x in deps:
            sem, val = x[4]
            if ck.get(sem, 0) < val:
                todo[sem] = max(todo.get(sem, 0), val)
                merge(ck, x[5])
        for sem, val in todo.items():
            queue[q].wait_ge(T.sem[sem], val)

    def note(q, ck, outs, ins, tok):
        serial[0] += 1
        snap = dict(ck)
        merge(snap, {tok[0]: tok[1]})
        for lst, w in ((ins, False), (outs, True)):
            for (_, name, c0, c1, st) in lst:
                new = (c0, c1, w, q, tok, snap, serial[0])
                old = rec.get(name, [])
                if w and st == 1:
                    old = [x for x in old if not (c0 <= x[0] and x[1] <= c1)]
                elif not w:
                    old = [x for x in old if x[2] or x[3] != q or not (c0 <= x[0] and x[1] <= c1)]
                old.append(new)
                rec[name] = old
                for b in banks_of([(_, name, c0, c1, st)]):
                    bank.setdefault(b, {})[q] = new

    def bump(sem, n):
        total[sem] = total.get(sem, 0) + n
        return (sem, total[sem])

    for reg, sem, n in lands:
        note("remote", {}, [reg], [], bump(sem, n))
    for x in sorted(plan, key=lambda x: x[:2]):
        if x[2] == "c":
            q, call, out, args, kw = x[3:]
            outs, ins = split(out, args, kw)
            need(q, outs, ins)
            tok = bump(own[q], 1)
            calls[call](ap(out), *[ap(a) for a in args], **{k: ap(v) for k, v in kw.items()}).then_inc(T.sem[tok[0]], 1)
            note(q, clock[q], outs, ins, tok)
        elif x[2] == "d":
            q, sem, out_ap, in_ap, outs, ins = x[3:]
            need(q, outs, ins)
            tok = bump(sem, 16)
            queue[q].dma_start(out_ap, in_ap).then_inc(T.sem[sem], 16)
            note(q + "dma", clock[q], outs, ins, tok)
        else:
            dst, out_ap, in_reg, sem, use = x[3:]
            need("g", [], [in_reg])
            rid, pid, _ = topo.addr(dst)
            g.remote_dma(out_ap, ap(in_reg), T.sem[sem], T.sem["ls"], pid, rid, sum(1 << e for e in use))
            bump("ls", len(use))

    for sem, val in total.items():
        if clock["g"].get(sem, 0) < val:
            g.wait_ge(T.sem[sem], val)
